import numpy as np, ml_dtypes
CORES = [16,17,18,19,32,33,34,35]
N = 8
BF = ml_dtypes.bfloat16
def gentries(a):
    return np.ascontiguousarray(a.reshape(8, 16, -1).transpose(0, 2, 1)).reshape(8, -1)
def gtable(e):
    e = np.asarray(e); return np.ascontiguousarray(e.reshape(8, -1, 16).transpose(0, 2, 1)).reshape(128, -1).astype(np.int32)
S, C, B, U, RO, Q = 4096, 2048, 128, 64, 3, 8
L = B + U
def parts(rng):
    sk = (256 * (0.25 + 0.75 * rng.random((N, 8, 1, C))) * rng.random((N, 8, 16, C))).astype(np.int64); sk = np.minimum(sk, 255); sk[..., C - 1] = 0
    oc = np.where(rng.random((N, 8, S)) < 0.05, C - 1, rng.integers(0, C - 1, (N, 8, S)))
    cv = rng.integers(0, S, (N, 8, 16, S)); cd = np.ascontiguousarray(np.argsort(rng.random((N, 8, RO, S)), axis=-1)[..., :L * 16])
    return sk, oc, cv, cd
def fill(rng, share):
    u = rng.random((N, 8, 1, RO, B)); v = rng.random((N, 8, 1, RO, B))
    h = np.where(u < share, 9 + 31 * v, np.where(u < share + 0.1, 4 + 5 * v, np.where(u < share + 0.3, 0.0, 0.2 + 3.8 * v)))
    w = rng.random((N, 8, 16, RO, B)) * (rng.random((N, 8, 16, RO, B)) < 0.7)
    return np.minimum((80 * h * w).astype(np.int64), 4096)
def sums(sk, oc, cd):
    who = np.take_along_axis(oc, cd[:, :, 0, :B * 16], 2)
    return np.add.accumulate(np.take_along_axis(sk, who[:, :, None, :], 3).reshape(N, 8, 16, B, 16), axis=4)
def heavy(rng, sk, oc, cv, cd, nd):
    own = np.arange(S); j = np.arange(B)
    for g in rng.permutation(8)[:2]:
        left = []
        for q in range(N):
            v = rng.integers(200, 256, (16, C)); v[:, C - 1] = 0; e = rng.integers(L, C - 1, S)
            st = cd[q, g, 0].reshape(L, 16); late = st[B:].reshape(-1)
            cd[q, g, 1] = np.concatenate([rng.permutation(st[:B].reshape(-1)), rng.permutation(late)])
            cv[q, g] = rng.choice(np.setdiff1d(own, late), (16, S))
            p = rng.integers(10, 16, B); before = np.add.accumulate(v[:, e[st[:B]]], axis=2)[:, j, p - 1]
            x = 208 + (-before) % 16; want = before + x
            x[rng.integers(0, 16, B), j] -= rng.integers(0, 2, B)
            v[:, :B] = x; e[st[j, p]] = j
            big = rng.permutation(B)[:U // 2]; e[st[big[U // 8:], 8:]] = C - 1
            want[:, big] = 0; want[rng.integers(0, 16, U // 2), big] = 4096
            sk[q, g] = v; oc[q, g] = e; nd[q, g] = 0; nd[q, g, :, 0] = want
            end = np.add.reduce(v[:, e[st[:B]]], axis=2); u = np.nonzero(np.any(end < want, axis=0))[0][:U]
            left.append(np.maximum(want[:, u] - end[:, u], 0))
        for q in range(N):
            w = left[q - 1]; n = w.shape[1]; k = np.arange(n); z = np.argmax(w, axis=0); top = w[z, k]
            st = cd[q, g, 1].reshape(L, 16)[B:B + n]
            line = np.add.accumulate(sk[q, g][z[:, None], oc[q, g][st]], axis=1)
            p = np.add.reduce((line < top[:, None]).astype(np.int64), axis=1)
            before = np.where(p > 0, line[k, np.maximum(p - 1, 0)], 0)
            sk[q, g, z, B + k] = top - before - k % 2; oc[q, g, st[k, p]] = B + k
def pack(sk, oc, cv, cd, nd):
    return {"skill": np.ascontiguousarray(sk.reshape(N, 128, C)).astype(np.float32).astype(BF), "occ": oc.astype(np.int32), "cover": np.ascontiguousarray(cv.reshape(N, 128, S)).astype(np.int32),
            "cards": np.stack([gtable(a.reshape(8, -1)) for a in cd]), "need": np.ascontiguousarray(nd.reshape(N, 128, RO * B)).astype(np.float32).astype(BF)}
def setup_inputs(rng):
    sk, oc, cv, cd = parts(rng)
    return pack(sk, oc, cv, cd, fill(rng, rng.choice(np.array([0.03, 0.1, 0.2, 0.3]), (N, 8, 1, 1, 1))))
def setup_inputs_room(rng):
    sk, oc, cv, cd = parts(rng); nd = np.zeros((N, 8, 16, RO, B), np.int64); pre = sums(sk, oc, cd)
    nd[:, :, :, 0] = pre[..., 0] * (rng.random((N, 8, 1, B)) < 0.5)
    for q in range(N):
        for t in range(RO):
            size = rng.permutation(np.array([0, 1, U - 1, U, U + 1, B, U, 0]))
            for g in range(8):
                n = int(size[g]); lanes = rng.permutation(B)[:n]
                nd[q, g, :, t, lanes] = rng.integers(0, 256, (n, 16)); nd[q, g, rng.integers(0, 16, n), t, lanes] = 4096
    return pack(sk, oc, cv, cd, nd)
def setup_inputs_ties(rng):
    sk, oc, cv, cd = parts(rng)
    few = rng.integers(0, 3, sk.shape) * 16; m = np.arange(8)[None, :, None, None] % 2 == 0
    sk = np.where(m, few, sk // 16 * 16) * (rng.random((N, 8, 1, C)) > 0.1); sk[..., C - 1] = 0
    nd = fill(rng, 0.05); pre = sums(sk, oc, cd)
    p = rng.choice(np.array([0, 0, 1, 3, 7, 14, 15, 15]), (N, 8, B))
    w = np.take_along_axis(pre, p[:, :, None, :, None], 4)[..., 0]
    w = w + 16 * ((np.arange(16)[None, None, :, None] == rng.integers(0, 16, (N, 8, 1, B))) & (rng.random((N, 8, 1, B)) < 0.5))
    nd[:, :, :, 0] = w * (rng.random((N, 8, 1, B)) > 0.3)
    heavy(rng, sk, oc, cv, cd, nd)
    return pack(sk, oc, cv, cd, nd)
def setup_inputs_crowd(rng):
    sk, oc, cv, cd = parts(rng); h = B // 2; sk[..., 0] = 255; own = np.arange(S); o = rng.permutation(8)
    full = np.argsort(rng.random((N, 8, B)), axis=-1)[..., :U]
    for q in range(N):
        for g in range(8):
            card = cd[q, g, 0].reshape(L, 16)
            if g == o[0] or g == o[1]:
                k = rng.permutation(np.setdiff1d(own, card[full[q, g]].reshape(-1))); a, b = k[:L], k[L:2 * L]
                mid = rng.permutation(np.setdiff1d(own, k[:2 * L]))[:14 * L].reshape(L, 14)
                cd[q, g, 1] = np.concatenate([a[:, None], mid, b[:, None]], axis=1).reshape(-1)
                v = np.clip(sk[q, g], 16, 239); v[:, :16] = rng.integers(240, 256, (16, 16)); v[:, C - 1] = 0; sk[q, g] = v
                oc[q, g, a] = rng.integers(16, C - 1, L); oc[q, g, b] = rng.integers(0, 16, L)
                c = np.repeat(own[None, :], 16, axis=0)
                if g == o[0]: c[:, a] = b[rng.integers(0, 2, (16, L))]
                else: c[:, a] = np.where(np.arange(16)[:, None] >= rng.integers(0, 16, L)[None, :], b[None, :], a[None, :])
                cv[q, g] = c
            else:
                pool = card[h:h + 16, 15]; oc[q, g, pool[:8]] = 0
                c = pool[rng.integers(0, 16, (16, S))]; kind = rng.integers(0, 5, S)
                c[:15] = np.where(kind >= 3, own, c[:15]); c[15] = np.where(kind == 4, own, c[15]); cv[q, g] = c
    nd = fill(rng, 0.05); pre = sums(sk, oc, cd)
    nd[:, :, :, 0] = pre[..., 0] * (np.arange(B) < h); nd[:, o[:2]] = 0
    for q in range(N):
        for g in o[:2]:
            z = rng.integers(0, 16, U); l = full[q, g]; nd[q, g, z, 0, l] = pre[q, g, z, l, 15] // 16 * 16 + 16
            nd[q, g, rng.integers(0, 16, B), 1, np.arange(B)] = rng.integers(1, 17, B)
    return pack(sk, oc, cv, cd, nd)
def setup_inputs_bare(rng):
    sk, oc, cv, cd = parts(rng); h = rng.permutation(8)
    oc = np.where(rng.random((N, 8, S)) < rng.choice(np.array([0.4, 0.6, 0.8]), (N, 8, 1)), C - 1, oc); oc[:, h[0]] = C - 1
    ends = np.array([0, 1, S - 2, S - 1]); cv[:, h[2]] = rng.choice(ends, (N, 16, S)); oc[:, h[2], :2] = rng.integers(0, C - 1, (N, 2)); oc[:, h[2], S - 2:] = rng.integers(0, C - 1, (N, 2))
    nd = fill(rng, 0.05) * (rng.random((N, 8, 1, RO, B)) < 0.5); nd[::2, h[1]] = 0
    return pack(sk, oc, cv, cd, nd)
def setup_inputs_spread(rng):
    sk, oc, cv, cd = parts(rng)
    sk = np.minimum((np.exp2(8.2 * rng.random((N, 8, 1, C))) * rng.random((N, 8, 16, C))).astype(np.int64), 255); sk[..., C - 1] = 0
    oc = np.where(rng.random((N, 8, S)) < 0.1, C - 1, np.minimum(((C - 1) * rng.random((N, 8, S)) ** 3).astype(np.int64), C - 2))
    cv = np.minimum((S * rng.random((N, 8, 16, S)) ** 2).astype(np.int64), S - 1)
    nd = (np.minimum(np.exp2(12.2 * rng.random((N, 8, 1, RO, B))), 4096) * rng.choice(np.array([0.0, 0.25, 0.5, 1.0]), (N, 8, 16, RO, B))).astype(np.int64)
    return pack(sk, oc, cv, cd, nd * (rng.random((N, 8, 1, RO, B)) > 0.3))
def check_inputs(d):
    bad = []
    for k, hi in (("skill", 255), ("need", 4096), ("occ", C - 1), ("cover", S - 1), ("cards", S - 1)):
        x = np.asarray(d[k]).astype(np.float64)
        if not np.all((x >= 0) & (x <= hi) & (x == np.floor(x))): bad.append("range of " + k)
    if not np.all(np.asarray(d["skill"])[:, :, C - 1].astype(np.float32) == 0): bad.append("last column of skill")
    e = np.sort(np.asarray(d["cards"]).reshape(N, 8, 16, RO, L).transpose(0, 1, 3, 2, 4).reshape(N, 8, RO, 16 * L), axis=-1)
    if np.any(e[..., 1:] == e[..., :-1]): bad.append("equal stations on the cards of a round")
    return bad
def reference(skill, occ, cover, cards, need):
    sk = skill.astype(np.float32).astype(np.int64).reshape(N, 8, 16, C); cv = cover.astype(np.int64).reshape(N, 8, 16, S)
    cd = np.stack([gentries(a) for a in cards]).astype(np.int64).reshape(N, 8, RO, L, 16); nd = need.astype(np.float32).astype(np.int64).reshape(N, 8, 16, RO, B)
    oc = np.array(occ, dtype=np.int64); arrived = np.zeros((N, 8, 16, U), np.int64)
    for t in range(RO):
        sent = np.zeros((N, 8, 16, U), np.int64)
        for r in range(N):
            w = np.concatenate([nd[r, :, :, t], arrived[r]], axis=2)
            st = cd[r, :, t]; flat = st.reshape(8, -1)
            who = np.take_along_axis(oc[r], flat, 1)
            col = np.take_along_axis(sk[r], who[:, None, :], 2).reshape(8, 16, L, 16)
            pre = np.add.accumulate(col, axis=3)
            met = np.all(pre >= w[..., None], axis=1)
            zero = np.all(w == 0, axis=1)
            leave = ~np.concatenate([zero[..., None], met[..., :15]], axis=2)
            unmet = ~met[..., 15]; before = np.add.accumulate(unmet.astype(np.int64), axis=1) - unmet
            rest = np.maximum(w - pre[..., 15], 0); g, l = np.nonzero(unmet & (before < U))
            sent[(r + 1) % N][g, :, before[g, l]] = rest[g, :, l]
            np.put_along_axis(oc[r], flat, np.where(leave.reshape(8, -1), C - 1, who), 1)
            s = st[..., 0]; lost = leave[..., 0] & (who.reshape(8, L, 16)[..., 0] != C - 1)
            m = np.take_along_axis(cv[r], s[:, None, :], 2)
            a = np.take_along_axis(oc[r], m.reshape(8, -1), 1)
            ka = np.take_along_axis(sk[r], a[:, None, :], 2).reshape(8, 16, 16, L)
            a = a.reshape(8, 16, L); good = np.add.reduce((ka >= col[:, :, None, :, 0]).astype(np.int64), axis=1)
            fit = (a != C - 1) & (good >= Q); ok = lost & np.any(fit, axis=1)
            i = np.argmax(fit, axis=1)[:, None, :]
            src = np.take_along_axis(m, i, 1)[:, 0]; new = np.take_along_axis(a, i, 1)[:, 0]
            for g in range(8):
                lanes = np.nonzero(ok[g])[0]
                out, at = np.unique(src[g, lanes], return_index=True); lanes = lanes[at]
                oc[r, g, s[g, lanes]] = new[g, lanes]; oc[r, g, out] = C - 1
        arrived = sent
    return {"y": oc.astype(np.float32)}

@@ -1,0 +1,376 @@
+from concourse.mybir import dt, AluOpType as A_, ActivationFunctionType as F_
+
+EPS = 2.0 ** -40
+BIGS = 8192.0
+NST, NDUMP, NWIN = 4096, 4480, 4496
+KV = 12
+
+TYPES = {"b": "bfloat16", "f": "float32", "i": "int32", "u": "uint16", "h": "float16"}
+BUFS = """b skw 2048  i occ32 256  f occf 256  u bof 256  b skp 4096  b SK 8960  f NUM 8960  i cov 4096  i cd32 576
+i cs32 576  u cu 576  u cm 576  h ch 576  b nd 384  b XA 2064  b XB 1040  b a15 64  b N1 2048  f N2 1024  b R1 2048  b R2 1024
+b keep 3072  b AG 3072  b ge 3072  f mf 192  f ms 192  u mu 192  h code16 192  b eb 192  b bsb 192  b Fb 192  b sel 192
+h selm 192  h Rh 192  f vx 192  f tg 12  f offf 12  f tu 12  f slf 12  u LL0 16  u LL1 24  u LL2 24  b sv0 256  b sv1 384
+f nv 384  b um 192  f us 192  f uf 192  b ux 192  b cum 192  f uy 192  u ul 12  f df 192  f SW0 384  f SW1 384  f RC0 64
+f RC1 64  u L0u 72  f L0f 36  i pmi 1  i pmj 1  f pmf 1  f pk 1  f pz 1  f th0 1  f thr 1  i ia 192  i ic 192  i ib 192
+f dtf 192  f duf 192  f DT 192  f DU 192  b OD 192  b TC 192  b ones 160  b OB 160  b OBa 160  b OB8 128  b OBn 128
+h OBh 128  b Wb 160  h Wh 160  b Zb 160  h Zh 160  b Yb 160  h Yh 160  b Ib 128  b I5 128  b In 128  b Tri 128  b T8 128
+b EL 256  f NL 256  f ef 256  f YL 256""".split()
+SCRATCH = {BUFS[k + 1]: ("sbuf", [128, int(BUFS[k + 2])], TYPES[BUFS[k]]) for k in range(0, len(BUFS), 3)}
+SCRATCH["E2"] = ("sbuf", [128, 12, 192], "bfloat16")
+SCRATCH["PL"] = ("psum", [128, 3072], "float32")
+SCRATCH["PM"] = ("psum", [128, 512], "float32")
+SCRATCH["PN"] = ("psum", [128, 512], "float32")
+SEMAPHORES = ["qV", "qS", "qP", "qG", "arr0", "arr1", "snt"] + ["d%d" % i for i in range(14)]
+
+
+def tracker(g, T):
+    eng = {"V": g.vector, "S": g.scalar, "P": g.tensor, "G": g, "Y": g.sync}
+    num = {"V": 0, "S": 0, "P": 0, "G": 0, "D": 0}
+    know = {q: {} for q in eng}
+    snaps, lastw, readers = {}, {}, {}
+
+    def semof(p):
+        return T.sem["q" + p] if p in "VSPG" else T.sem[p]
+
+    def waits(q, deps):
+        best = {}
+        for p, n in deps:
+            if know[q].get(p, 0) < n:
+                best[p] = max(n, best.get(p, 0))
+        items = list(best.items())
+        for p, n in items:
+            if any(p2 != p and snaps[(p2, n2)].get(p, 0) >= n for p2, n2 in items):
+                continue
+            eng[q].wait_ge(semof(p), n)
+        k = know[q]
+        for p, n in items:
+            for a, b in snaps[(p, n)].items():
+                k[a] = max(k.get(a, 0), b)
+            k[p] = max(k.get(p, 0), n)
+
+    def before(q, R, W):
+        d = [lastw[r] for r in R if r in lastw]
+        for r in R:
+            if r[:2] in ("PL", "PM", "PN"):
+                d += [x for x in readers.get(r, []) if x[0] != q]
+        for w in W:
+            if w in lastw and not (q == "P" and lastw[w][0] == "P"):
+                d.append(lastw[w])
+            d += readers.get(w, [])
+        waits(q, d)
+
+    def note(tok, R, W):
+        for r in R:
+            readers.setdefault(r, []).append(tok)
+        for w in W:
+            lastw[w] = tok
+            readers[w] = []
+
+    def op(q, fns, R, W):
+        before(q, R, W)
+        fns = fns if isinstance(fns, list) else [fns]
+        for f in fns[:-1]:
+            f()
+        num[q] += 1
+        fns[-1]().then_inc(semof(q), 1)
+        tok = (q, num[q])
+        snaps[tok] = dict(know[q])
+        note(tok, R, W)
+
+    def dma(q, out, in_, R, W):
+        before(q, R, W)
+        p = "d%d" % num["D"]
+        num["D"] += 1
+        eng[q].dma_start(out, in_).then_inc(T.sem[p], 16)
+        tok = (p, 16)
+        snaps[tok] = dict(know[q])
+        note(tok, R, W)
+
+    def arrive(p, n, W):
+        snaps[(p, n)] = {}
+        note((p, n), [], W)
+
+    def finish():
+        for p, n in [(q, num[q]) for q in "VSPG" if num[q]] + [("d%d" % i, 16) for i in range(num["D"])]:
+            if know["G"].get(p, 0) < n:
+                g.wait_ge(semof(p), n)
+
+    return op, dma, arrive, before, finish
+
+
+def rank_program(g, core, T, topo):
+    rank = T.rank_of(core)
+    if rank is None:
+        return
+    cores = list(T.cores)
+    nxt = cores[(rank + 1) % len(cores)]
+    NE = 4
+    V, S, P = g.vector, g.scalar, g.tensor
+    op, dma, arrive, before, finish = tracker(g, T)
+    arrive("arr0", NE, ["RC0"])
+    arrive("arr1", NE, ["RC1"])
+    SKW = ["SK", "SKd"] + ["SK_%d" % i for i in range(16)]
+    RD = SKW + ["SKb"]
+
+    def v(fn, R, W):
+        op("V", fn, R, W)
+
+    def s(fn, R, W):
+        op("S", fn, R, W)
+
+    def p(fns, R, W):
+        op("P", fns, R, W)
+
+    def gp(fn, R, W):
+        op("G", fn, R, W)
+
+    def mm(out, l, r, a, b):
+        return lambda: P.matmul(out, l, r, a, b)
+
+    dma("Y", T.occ32[:, :], T.occ[:, :], [], ["occ32"])
+    dma("S", T.cs32[1:128, :], T.cards[0:127, :], [], ["cs32a"])
+    dma("Y", T.skw[:, :], T.skill[:, :], [], ["skw"])
+    dma("S", T.cs32[0:1, :], T.cards[127:128, :], [], ["cs32b"])
+    dma("S", T.cd32[:, :], T.cards[:, :], [], ["cd32"])
+    dma("S", T.nd[:, :], T.need[:, :], [], ["nd"])
+    dma("Y", T.cov[:, :], T.cover[:, :], [], ["cov"])
+
+    v(lambda: V.memset(T.ones[:, :], 1.0), [], ["ones"])
+    gp(lambda: g.iota(T.pmi[:, :], [[0, 1]], 0, 1), [], ["pmi"])
+    gp(lambda: g.iota(T.ib[:, :], [[16, 12], [0, 16]], 4097, 0), [], ["ib"])
+    gp(lambda: g.iota(T.ia[:, :], [[1, 192]], 256, -1), [], ["ia"])
+    gp(lambda: g.affine_select(T.OBa[:, :], T.ones[:, :], [[-16, 10], [0, 16]], A_.is_ge, 0.0, 16, 1), ["ones"], ["OBa"])
+    gp(lambda: g.affine_select(T.OB[:, :], T.OBa[:, :], [[16, 10], [0, 16]], A_.is_ge, 0.0, -1, -1), ["OBa"], ["OB"])
+    gp(lambda: g.affine_select(T.Wb[:, :], T.OB[:, :], [[0, 10], [1, 16]], A_.is_equal, 0.0, 0, 0), ["OB"], ["Wb"])
+    gp(lambda: g.affine_select(T.Zb[:, :], T.Wb[:, :], [[1, 160]], A_.is_equal, 0.0, -16, -1), ["Wb"], ["Zb"])
+    gp(lambda: g.affine_select(T.Yb[:, :], T.Wb[:, :], [[1, 160]], A_.is_equal, 0.0, -1, -1), ["Wb"], ["Yb"])
+    gp(lambda: g.affine_select(T.Ib[:, :], T.ones[:, 0:128], [[1, 128]], A_.is_equal, 0.0, 0, -1), ["ones"], ["Ib"])
+    gp(lambda: g.affine_select(T.Tri[:, :], T.OB[:, 16:144], [[1, 128]], A_.is_gt, 0.0, 0, -1), ["OB"], ["Tri"])
+    v(lambda: V.memset(T.SK[:, NST:NDUMP], 0.0), [], ["SKd"])
+    v(lambda: V.memset(T.SK[:, NDUMP:NWIN], BIGS), [], ["SKb"])
+    v(lambda: V.memset(T.N1[:, :], 0.0), [], ["N1"])
+    v(lambda: V.tensor_scalar(T.pmj[:, :], T.pmi[:, :], 15, None, A_.bitwise_and), ["pmi"], ["pmj"])
+    v(lambda: V.memset(T.N2[:, :], 0.0), [], ["N2"])
+    v(lambda: V.tensor_copy(T.pmf[:, :], T.pmj[:, :]), ["pmj"], ["pmf"])
+    v(lambda: V.tensor_scalar(T.ic[:, :], T.ia[:, :], 15, None, A_.bitwise_and), ["ia"], ["ic"])
+    v(lambda: V.tensor_scalar(T.pk[:, :], T.pmf[:, :], 0.0, None, A_.is_gt), ["pmf"], ["pk"])
+    v(lambda: V.tensor_scalar(T.pz[:, :], T.pmf[:, :], 0.0, float(NDUMP), A_.is_equal, A_.mult), ["pmf"], ["pz"])
+    v(lambda: V.tensor_scalar(T.th0[:, :], T.pmf[:, :], float(KV), 8.0, A_.is_lt, A_.mult), ["pmf"], ["th0"])
+    v(lambda: V.tensor_copy(T.bof[:, :], T.occ32[:, :]), ["occ32"], ["bof"])
+    v(lambda: V.tensor_scalar(T.cm[:, 0:192], T.cs32[:, 0:192], T.pk[:, 0:1], T.pz[:, 0:1], A_.mult, A_.add), ["cs32a", "cs32b", "pk", "pz"], ["cm0"])
+    v(lambda: V.tensor_scalar(T.dtf[:, :], T.ib[:, :], T.pmf[:, 0:1], None, A_.add), ["ib", "pmf"], ["dtf"])
+    v(lambda: V.tensor_scalar(T.OD[:, :], T.ic[:, :], 0.0, BIGS, A_.not_equal, A_.mult), ["ic"], ["OD"])
+    v(lambda: V.tensor_scalar(T.thr[:, :], T.th0[:, :], -0.5, None, A_.add), ["th0"], ["thr"])
+    v(lambda: V.tensor_scalar(T.duf[:, :], T.dtf[:, :], -3905.0, None, A_.add), ["dtf"], ["duf"])
+    v(lambda: V.tensor_copy(T.Wh[:, :], T.Wb[:, :]), ["Wb"], ["Wh"])
+    v(lambda: V.tensor_scalar(T.TC[:, :], T.OD[:, :], 10240.0, None, A_.add), ["OD"], ["TC"])
+    v(lambda: V.memset(T.SW0[:, 0:64], 0.0), [], ["SW0"])
+    v(lambda: V.memset(T.SW1[:, 0:64], 0.0), [], ["SW1"])
+    gp(lambda: g.affine_select(T.DT[:, :], T.dtf[:, :], [[0, 12], [1, 16]], A_.is_equal, 0.0, 0, 0), ["dtf"], ["DT"])
+    gp(lambda: g.affine_select(T.DU[:, :], T.duf[:, :], [[0, 12], [1, 16]], A_.is_equal, 0.0, 0, 0), ["duf"], ["DU"])
+    gp(lambda: g.iota(T.NUM[:, 0:NDUMP], [[0, NDUMP]], 0, 0, allow_small_or_imprecise_dtypes=True), [], ["NUM"])
+    v(lambda: V.memset(T.skw[:, 2047:2048], -1.0), [], ["skw"])
+    v(lambda: V.tensor_scalar(T.skp[:, 0:2048], T.skw[:, :].indirect(T.bof[:, 0:128]), EPS, 0.0, A_.add, A_.max), ["skw", "bof"], ["skpa"])
+    s(lambda: S.activation(T.skp[:, 2048:4096], T.skw[:, :].indirect(T.bof[:, 128:256]), F_.Relu, bias=EPS), ["skw", "bof"], ["skpb"])
+    v(lambda: V.tensor_scalar(T.N1[:, 0:2048:16], T.nd[:, 0:128], -1.0, None, A_.mult), ["nd"], ["N1"])
+    v(lambda: V.tensor_scalar(T.ch[:, :], T.cd32[:, :], -2048.0, None, A_.add), ["cd32"], ["ch"])
+    v(lambda: V.tensor_copy(T.Zh[:, :], T.Zb[:, :]), ["Zb"], ["Zh"])
+    v(lambda: V.tensor_copy(T.Yh[:, :], T.Yb[:, :]), ["Yb"], ["Yh"])
+    p([mm(T.PN[:, 0:36], T.Zh[:, 16 - i:144 - i], T.ch[:, i:576:16], i == 0, i == 15) for i in range(16)], ["Zh", "ch"], ["PN"])
+    p([mm(T.PN[:, 36:72], T.Yh[:, 16 - i:144 - i], T.ch[:, i:576:16], i == 0, i == 15) for i in range(16)], ["Yh", "ch"], ["PN"])
+    for i in range(16):
+        if i < 10:
+            v(lambda: V.tensor_copy(T.SK[:, 256 * i:256 * i + 256], T.skp[:, i:4096:16]), ["skpa", "skpb"], ["SK_%d" % i])
+        else:
+            s(lambda: S.activation(T.SK[:, 256 * i:256 * i + 256], T.skp[:, i:4096:16], F_.Copy), ["skpa", "skpb"], ["SK_%d" % i])
+    v(lambda: V.tensor_scalar(T.L0u[:, :], T.PN[:, 0:72], 2048.0, None, A_.add), ["PN"], ["L0u"])
+
+    def prep_m(t):
+        L = 128 if t == 0 else 192
+        v(lambda: V.tensor_copy(T.mf[:, 0:L], T.cov[:, :].indirect(T.L0u[:, 12 * t:12 * t + L // 16])), ["cov", "L0u"], ["mf"])
+        v(lambda: V.tensor_copy(T.mu[:, 0:L], T.mf[:, 0:L]), ["mf"], ["mu"])
+
+    def prep_s(t):
+        L = 128 if t == 0 else 192
+        s(lambda: S.activation(T.ms[:, 0:L], T.mf[:, 0:L], F_.Sign, bias=-2047.5), ["mf"], ["ms"])
+        s(lambda: S.activation(T.PN[:, 256:256 + L], T.ms[:, 0:L], F_.Copy, bias=-2047.5, scale=0.5), ["ms"], ["PN"])
+
+    def prep_c(t):
+        L = 128 if t == 0 else 192
+        v(lambda: V.tensor_tensor(T.code16[:, 0:L], T.mf[:, 0:L], T.PN[:, 256:256 + L], A_.add), ["mf", "PN"], ["code16"])
+
+    win = T.SK[:, 0:NWIN]
+
+    for t in range(3):
+        last = t == 2
+        L = 128 if t == 0 else 192
+        C = L // 16
+        H = L // 2
+        c0 = 192 * t
+        LL = T["LL%d" % t]
+        sv = T.sv0 if t == 0 else T.sv1
+        kv = "0" if t == 0 else "1"
+        cuk, cmk = (["cu0"], ["cm0"]) if t == 0 else (["cu1"], ["cm1"])
+
+        def leave(b, src, key):
+            p(mm(T.PL[:, 512 * b:512 * b + 512], T.OB[:, 16:144], src, True, True), ["OB", key], ["PL%d" % b])
+
+        def scat(k):
+            src = T.XA[:, 1 + 1024 * k:1025 + 1024 * k] if k < 2 else T.XB[:, 1:1025]
+            v(lambda: V.tensor_tensor(win.indirect(T.cu[:, c0 + 64 * k:c0 + 64 * k + 64]), src, T.keep[:, 1024 * k:1024 * k + 1024], A_.mult),
+              cuk + ["keep%d" % k] + (["XA0", "XA1", "XAf"] if k < 2 else ["XBa", "XBb", "XBf"]), SKW)
+
+        v(lambda: V.tensor_copy(T.XA[:, 0:1024], win.indirect(T.cm[:, c0:c0 + 64])), RD + cmk, ["XA0"])
+        s(lambda: S.activation(T.XA[:, 1024:2048], win.indirect(T.cm[:, c0 + 64:c0 + 128]), F_.Copy), RD + cmk, ["XA1"])
+        if t:
+            s(lambda: S.activation(T.XB[:, 512:1024], win.indirect(T.cm[:, c0 + 160:c0 + 192]), F_.Copy), RD + cmk, ["XBb"])
+        v(lambda: V.tensor_tensor_scan(T.R1[:, 0:1024], T.XA[:, 0:1024], T.N1[:, 0:1024], 0.0, A_.add, A_.min), ["XA0", "XAf", "N1"], ["R1a"])
+        for b in range(2):
+            leave(b, T.R1[:, 512 * b:512 * b + 512], "R1a")
+        if t:
+            v(lambda: V.tensor_copy(T.XB[:, 0:512], win.indirect(T.cm[:, c0 + 128:c0 + 160])), RD + cmk, ["XBa"])
+        s(lambda: S.activation(T.keep[:, 0:1024], T.PL[:, 0:1024], F_.Relu, bias=1.0), ["PL0", "PL1"], ["keep0"])
+        if t:
+            v(lambda: V.tensor_copy(T.a15[:, 0:64], win.indirect(T.L0u[:, 44 + 12 * t:48 + 12 * t])), RD + ["L0u"], ["a15"])
+        v(lambda: V.tensor_tensor_scan(T.R1[:, 1024:2048], T.XA[:, 1024:2048], T.N1[:, 1024:2048], 0.0, A_.add, A_.min), ["XA1", "XAf", "N1"], ["R1b"])
+        for b in range(2, 4):
+            leave(b, T.R1[:, 512 * b:512 * b + 512], "R1b")
+        s(lambda: S.activation(T.keep[:, 1024:2048], T.PL[:, 1024:2048], F_.Relu, bias=1.0), ["PL2", "PL3"], ["keep1"])
+        v(lambda: V.tensor_copy(T.XA[:, 16:2064:16], win.indirect(T.L0u[:, 36 + 12 * t:44 + 12 * t])), RD + ["L0u", "XA0", "XA1"], ["XAf"])
+        if t == 0:
+            v(lambda: V.tensor_copy(T.cu[:, 0:192], T.cd32[:, 0:192]), ["cd32"], ["cu0"])
+            v(lambda: V.tensor_scalar(T.L0f[:, :], T.PN[:, 0:36], 2048.0, None, A_.add), ["PN"], ["L0f"])
+            v(lambda: V.tensor_copy(T.occf[:, :], T.occ32[:, :]), ["occ32"], ["occf"])
+            dma("Y", T.NUM[0:128:16, 0:NST], T.occf[:, :], ["occf"], ["NUM"])
+        else:
+            prep_c(t)
+        scat(0)
+        if t == 0:
+            prep_m(0)
+            s(lambda: S.activation(T.I5[:, :], T.Ib[:, :], F_.Copy, scale=512.0), ["Ib"], ["I5"])
+            s(lambda: S.activation(T.In[:, :], T.Ib[:, :], F_.Copy, scale=-1.0), ["Ib"], ["In"])
+        else:
+            rc = T["RC%d" % (t - 1)]
+            v(lambda: V.tensor_scalar(T.N2[:, 0:1024:16], rc[:, :], 0.0, None, A_.min), ["RC%d" % (t - 1)], ["N2"])
+            v(lambda: V.tensor_tensor_scan(T.R2[:, :], T.XB[:, 0:1024], T.N2[:, :], 0.0, A_.add, A_.min), ["XBa", "XBb", "XBf", "N2"], ["R2"])
+            for b in range(4, 6):
+                leave(b, T.R2[:, 512 * (b - 4):512 * (b - 4) + 512], "R2")
+            s(lambda: S.activation(T.keep[:, 2048:3072], T.PL[:, 2048:3072], F_.Relu, bias=1.0), ["PL4", "PL5"], ["keep2"])
+            v(lambda: V.tensor_copy(T.XB[:, 16:1040:16], T.a15[:, :]), ["a15", "XBa", "XBb"], ["XBf"])
+        if not last:
+            p([mm(T.PN[:, 0:128], T.Ib[:, :], T.XA[:, 1 + i:2048:16], i == 0, False) for i in range(15)]
+              + [mm(T.PN[:, 0:128], T.Ib[:, :], T.XA[:, 16:2064:16], False, False), mm(T.PN[:, 0:128], T.In[:, :], T.nd[:, 128 * t:128 * t + 128], False, True)],
+              ["Ib", "In", "nd", "XA0", "XA1", "XAf"], ["PN"])
+            if t:
+                p([mm(T.PN[:, 128:192], T.Ib[:, :], T.XB[:, 1 + i:1024:16], i == 0, False) for i in range(15)]
+                  + [mm(T.PN[:, 128:192], T.Ib[:, :], T.a15[:, :], False, True)], ["Ib", "XBa", "XBb", "a15"], ["PN"])
+        s(lambda: S.activation(T.eb[:, 0:128], T.XA[:, 1:2048:16], F_.Relu, bias=512.0, scale=-(2.0 ** 50)), ["XA0", "XA1"], ["eb"])
+        p([mm(T.PL[:, 0:128], T.Ib[:, :], T.XA[:, 1:2048:16], True, False), mm(T.PL[:, 0:128], T.I5[:, :], T.keep[:, 0:2048:16], False, False),
+           mm(T.PL[:, 0:128], T.Ib[:, :], T.eb[:, 0:128], False, True)], ["Ib", "I5", "XA0", "XA1", "keep0", "keep1", "eb"], ["PL0"])
+        scat(1)
+        if t and not last:
+            v(lambda: V.tensor_tensor(T.df[:, 128:192], T.PN[:, 128:192], T.N2[:, 0:1024:16], A_.add), ["PN", "N2"], ["dfb"])
+        if t:
+            scat(2)
+            s(lambda: S.activation(T.eb[:, 128:192], T.XB[:, 1:1024:16], F_.Relu, bias=512.0, scale=-(2.0 ** 50)), ["XBa", "XBb"], ["eb"])
+            p([mm(T.PL[:, 128:192], T.Ib[:, :], T.XB[:, 1:1024:16], True, False), mm(T.PL[:, 128:192], T.I5[:, :], T.keep[:, 2048:3072:16], False, False),
+               mm(T.PL[:, 128:192], T.Ib[:, :], T.eb[:, 128:192], False, True)], ["Ib", "I5", "XBa", "XBb", "keep2", "eb"], ["PL0"])
+        s(lambda: S.activation(T.bsb[:, 0:L], T.PL[:, 0:L], F_.Copy), ["PL0"], ["bsb"])
+        if not last:
+            s(lambda: S.activation(T.df[:, 0:128], T.PN[:, 0:128], F_.Copy), ["PN"], ["df"])
+            s(lambda: S.activation(T.um[:, 0:L], T.df[:, 0:L], F_.Relu, scale=-1.0), ["df", "dfb"], ["um"])
+            p(mm(T.PM[:, 0:L], T.OB[:, 16:144], T.um[:, 0:L], True, True), ["OB", "um"], ["PM"])
+            s(lambda: S.activation(T.us[:, 0:L], T.PM[:, 0:L], F_.Sign, bias=-0.5), ["PM"], ["us"])
+            s(lambda: S.activation(T.uf[:, 0:L], T.us[:, 0:L], F_.Relu), ["us"], ["uf"])
+            s(lambda: S.activation(T.ux[:, 0:L], T.uf[:, 0:L], F_.Copy, bias=8191.0, scale=-8192.0), ["uf"], ["ux"])
+            s(lambda: S.activation(T.N1[:, 0:2048:16], T.nd[:, 128 * t + 128:128 * t + 256], F_.Copy, scale=-1.0), ["nd"], ["N1"])
+        if t == 0:
+            s(lambda: S.activation(T.OB8[:, :], T.OB[:, 16:144], F_.Copy, scale=8192.0), ["OB"], ["OB8"])
+            s(lambda: S.activation(T.OBn[:, :], T.OB[:, 16:144], F_.Copy, scale=-8192.0), ["OB"], ["OBn"])
+            s(lambda: S.activation(T.T8[:, :], T.Tri[:, :], F_.Copy, scale=8192.0), ["Tri"], ["T8"])
+            prep_s(0)
+        v(lambda: V.tensor_copy(T.AG[:, 0:16 * H], win.indirect(T.mu[:, 0:H])), RD + ["mu"], ["AGa"])
+        s(lambda: S.activation(T.AG[:, 16 * H:16 * L], win.indirect(T.mu[:, H:L]), F_.Copy), RD + ["mu"], ["AGb"])
+        if last:
+            dma("Y", T.EL[:, :], T.SK[0:128:16, 0:NST], SKW, ["EL"])
+        for i in range(KV):
+            v(lambda: V.tensor_tensor(T.ge[:, L * i:L * i + L], T.AG[:, i:16 * L:16], T.PL[:, 0:L], A_.is_ge), ["AGa", "AGb", "PL0"], ["ge%d" % i])
+        order = list(range(4))
+        for k in range((16 - KV) // 2):
+            b = 512 * (2 + k)
+            i = KV + 2 * k
+            for h in range(2):
+                p([mm(T.PL[:, b + L * h:b + L * h + L], T.Ib[:, :], T.AG[:, i + h:16 * L:16], True, False),
+                   mm(T.PL[:, b + L * h:b + L * h + L], T.In[:, :], T.bsb[:, 0:L], False, True)], ["Ib", "In", "AGa", "AGb", "bsb"], ["PL%d" % (2 + k)])
+            s(lambda: S.activation(T.ge[:, L * i:L * i + 2 * L], T.PL[:, b:b + 2 * L], F_.Sign, bias=EPS / 2), ["PL%d" % (2 + k)], ["ge%d" % i, "ge%d" % (i + 1)])
+            order += [i, i + 1]
+            order += list(range(4 + 2 * k, min(6 + 2 * k, KV)))
+        order += [i for i in range(16) if i not in order]
+        for i in order:
+            p(mm(T.PL[:, 512:512 + L], T.Wb[:, 16 - i:144 - i], T.ge[:, L * i:L * i + L], i == order[0], i == order[-1]), ["Wb", "ge%d" % i], ["PL1"] if i in (order[0], order[-1]) else [])
+        if t == 0:
+            prep_c(0)
+            v(lambda: V.tensor_copy(T.OBh[:, :], T.OB[:, 16:144]), ["OB"], ["OBh"])
+        if not last:
+            v(lambda: V.tensor_tensor_scan(T.cum[:, 0:L], T.uf[:, 0:L], T.uf[:, 0:L], 0.0, A_.add, A_.max), ["uf"], ["cum"])
+            prep_m(t + 1)
+        v(lambda: V.tensor_scalar(T.Fb[:, 0:L], T.PL[:, 512:512 + L], T.thr[:, 0:1], None, A_.is_ge), ["PL1", "thr"], ["Fb"])
+        p(mm(T.PL[:, 1024:1024 + L], T.Tri[:, :], T.Fb[:, 0:L], True, True), ["Tri", "Fb"], ["PL2"])
+        if not last:
+            p([mm(T.PM[:, 0:L], T.Ib[:, :], T.OD[:, 0:L], True, False), mm(T.PM[:, 0:L], T.Ib[:, :], T.ux[:, 0:L], False, False),
+               mm(T.PM[:, 0:L], T.Ib[:, :], T.cum[:, 0:L], False, True)], ["Ib", "OD", "ux", "cum"], ["PM"])
+        else:
+            v(lambda: V.tensor_scalar(T.ef[:, :], T.EL[:, :], 0.0, 2047.0, A_.is_equal, A_.mult), ["EL"], ["ef"])
+        v(lambda: V.tensor_tensor(T.sel[:, 0:L], T.PL[:, 1024:1024 + L], T.Fb[:, 0:L], A_.is_lt), ["PL2", "Fb"], ["sel"])
+        v(lambda: V.tensor_tensor(T.selm[:, 0:L], T.sel[:, 0:L], T.code16[:, 0:L], A_.mult), ["sel", "code16"], ["selm"])
+        p(mm(T.PL[:, 1536:1536 + L], T.OBh[:, :], T.selm[:, 0:L], True, True), ["OBh", "selm"], ["PL3"])
+        p([mm(T.PL[:, 2048:2048 + C], T.Wh[:, 16 - i:144 - i], T.selm[:, i:L:16], i == 0, i == 15) for i in range(16)], ["Wh", "selm"], ["PL4"])
+        if not last:
+            sw = T["SW%d" % t]
+            v(lambda: V.tensor_tensor_scan(T.uy[:, 0:L], T.DU[:, 0:L], T.PM[:, 0:L], 0.0, A_.max, A_.min), ["DU", "PM"], ["uy"])
+            v(lambda: V.tensor_copy(T.ul[:, 0:C], T.uy[:, 15:L:16]), ["uy"], ["ul"])
+            v(lambda: V.tensor_copy(sw[:, :].indirect(T.ul[:, 0:C]), T.df[:, 0:L]), ["ul", "df", "dfb"], ["SW%d" % t])
+            before("G", ["SW%d" % t], [])
+            rid, pid, _se = topo.addr(nxt)
+            em = sum(1 << e for e in topo.engines(core, nxt)[:NE])
+            g.remote_dma(T["RC%d" % t][:, :], sw[:, 0:64], T.sem["arr%d" % t], T.sem.snt, pid, rid, em)
+        else:
+            v(lambda: V.tensor_tensor(T.YL[:, :], T.NL[:, :], T.ef[:, :], A_.max), ["NL", "ef"], ["YL"])
+            dma("Y", T.NUM[0:128:16, 0:NST], T.YL[:, :], ["YL"], ["NUM"])
+        v(lambda: V.tensor_copy(T.Rh[:, 0:L], T.PL[:, 1536:1536 + L]), ["PL3"], ["Rh"])
+        for c in range(C):
+            v(lambda: V.tensor_scalar(T.E2[:, c, 0:L - 16 * c], T.Rh[:, 16 * c:L], T.PL[:, 2048 + c:2049 + c], None, A_.is_equal), ["Rh", "PL4"], ["E%d" % c])
+        X = T.PL[:, 2560:2560 + L]
+        p([mm(X, T.Ib[:, :], T.TC[:, 0:L], True, False), mm(X, T.OBh[:, :], T.selm[:, 0:L], False, False),
+           mm(X, T.OBn[:, :], T.sel[:, 0:L], False, False)], ["Ib", "TC", "OBh", "selm", "OBn", "sel"], ["PL5"])
+        for c in range(C - 1):
+            p(mm(T.PL[:, 2560 + 16 * c + 16:2560 + L], T.OB8[:, :], T.E2[:, c, 16:L - 16 * c], False, False), ["OB8", "E%d" % c], [])
+        p(mm(X, T.T8[:, :], T.E2[:, 0:C, 0:16], False, True), ["T8"] + ["E%d" % c for c in range(C)], ["PL5"])
+        if not last:
+            prep_s(t + 1)
+        v(lambda: V.tensor_tensor_scan(T.vx[:, 0:L], T.DT[:, 0:L], X, 0.0, A_.max, A_.min), ["DT", "PL5"], ["vx"])
+        v(lambda: V.tensor_scalar(T.tg[:, 0:C], T.vx[:, 15:L:16], 2048.0, -1.0, A_.is_gt, A_.mult), ["vx"], ["tg"])
+        v(lambda: V.tensor_tensor(T.offf[:, 0:C], T.vx[:, 15:L:16], T.tg[:, 0:C], A_.add), ["vx", "tg"], ["offf"])
+        v(lambda: V.tensor_copy(LL[:, C:2 * C], T.offf[:, 0:C]), ["offf"], ["LLb"])
+        if not last:
+            s(lambda: S.activation(sv[:, 0:L], win.indirect(LL[:, C:2 * C]), F_.Copy), RD + ["LLb"], ["sv" + kv])
+        s(lambda: S.activation(T.nv[:, 0:L], T.NUM[:, 0:NDUMP].indirect(LL[:, C:2 * C]), F_.Copy), ["NUM", "LLb"], ["nv"])
+        v(lambda: V.tensor_scalar(T.tu[:, 0:C], T.vx[:, 15:L:16], 4096.5, float(NWIN), A_.is_gt, A_.mult), ["vx"], ["tu"])
+        v(lambda: V.tensor_tensor(T.slf[:, 0:C], T.tu[:, 0:C], T.L0f[:, 12 * t:12 * t + C], A_.add), ["tu", "L0f"], ["slf"])
+        v(lambda: V.tensor_copy(LL[:, 0:C], T.slf[:, 0:C]), ["slf"], ["LLa"])
+        if t == 0:
+            v(lambda: V.memset(T.sv0[:, 128:256], 0.0), [], ["sv0z"])
+        if not last:
+            v(lambda: V.tensor_copy(T.SK[:, :].indirect(LL[:, 0:2 * C]), sv[:, 0:2 * L]), ["LLa", "LLb", "sv" + kv, "sv%sz" % kv], SKW)
+        if t == 0:
+            v(lambda: V.tensor_scalar(T.cm[:, 192:576], T.cs32[:, 192:576], T.pk[:, 0:1], T.pz[:, 0:1], A_.mult, A_.add), ["cs32a", "cs32b", "pk", "pz"], ["cm1"])
+            v(lambda: V.tensor_copy(T.cu[:, 192:576], T.cd32[:, 192:576]), ["cd32"], ["cu1"])
+            v(lambda: V.memset(T.sv1[:, 192:384], 0.0), [], ["sv1z"])
+            v(lambda: V.memset(T.nv[:, 192:384], 2047.0), [], ["nvz"])
+        K = 2 if last else 1
+        v(lambda: V.tensor_copy(T.NUM[:, :].indirect(LL[:, 0:K * C]), T.nv[:, 0:K * L]), ["LLa", "LLb", "nv", "nvz"], ["NUM"])
+        if t == 1:
+            dma("Y", T.NL[:, :], T.NUM[0:128:16, 0:NST], ["NUM"], ["NL"])
+    dma("Y", T.y[:, :], T.NUM[0:128:16, 0:NST], ["NUM"], ["y"])
+    g.wait_ge(T.sem.snt, 2 * NE)
+    finish()

@@ -1,25 +1,33 @@
 from concourse.mybir import dt, AluOpType as A_, ActivationFunctionType as F_
 
 EPS = 2.0 ** -40
-BIGS = 8192.0
-NST, NDUMP, NWIN = 4096, 4480, 4496
-KV = 12
+NST = 4096
+NBG = NST + 8
+NRD = NST + 16
+NKP = 4608
+KV = 10
+VCALLS = [4, 3, 2, 1]
+CHUNKS = {128: [0, 32, 80, 128], 192: [0, 40, 96, 144, 192]}
+VLANES = {128: 56, 192: 88}
+KS = 136
 
 TYPES = {"b": "bfloat16", "f": "float32", "i": "int32", "u": "uint16", "h": "float16"}
-BUFS = """b skw 2048  i occ32 256  f occf 256  u bof 256  b skp 4096  b SK 8960  f NUM 8960  i cov 4096  i cd32 576
-i cs32 576  u cu 576  u cm 576  h ch 576  b nd 384  b XA 2064  b XB 1040  b a15 64  b N1 2048  f N2 1024  b R1 2048  b R2 1024
-b keep 3072  b AG 3072  b ge 3072  f mf 192  f ms 192  u mu 192  h code16 192  b eb 192  b bsb 192  b Fb 192  b sel 192
-h selm 192  h Rh 192  f vx 192  f tg 12  f offf 12  f tu 12  f slf 12  u LL0 16  u LL1 24  u LL2 24  b sv0 256  b sv1 384
-f nv 384  b um 192  f us 192  f uf 192  b ux 192  b cum 192  f uy 192  u ul 12  f df 192  f SW0 384  f SW1 384  f RC0 64
-f RC1 64  u L0u 72  f L0f 36  i pmi 1  i pmj 1  f pmf 1  f pk 1  f pz 1  f th0 1  f thr 1  i ia 192  i ic 192  i ib 192
-f dtf 192  f duf 192  f DT 192  f DU 192  b OD 192  b TC 192  b ones 160  b OB 160  b OBa 160  b OB8 128  b OBn 128
-h OBh 128  b Wb 160  h Wh 160  b Zb 160  h Zh 160  b Yb 160  h Yh 160  b Ib 128  b I5 128  b In 128  b Tri 128  b T8 128
-b EL 256  f NL 256  f ef 256  f YL 256""".split()
+BUFS = """b skw 2048  h tr 256  u bof 256  f SK 8704  f NUM 4320  f NF 8416  f dtf 192  i cov 4096  i cd32 576  u cu 576  h ch 576
+b X 3072  h N 3072  h R 3072  b x15 192  h R16 192  b Sb 128  h Sh 128  b Yb 160  h Yh 160  f pz 1  f cz 1
+b nd 384  f ZS 1024  f z16 8  f yl 64  u lst 192  h mf 192  h mt 192  u mu 192  b Br 768  b AG 1152  b ge 3072
+b eb 192  b nl 192  b Fb 192  h selm 192  h Rh 192  f v1 192  f v2 192  u LG 12  f la 12  u LL 24  f sv 384  f nv 384
+b uf 192  b cum 192  f uy 192  u ul 12  f SW0 400  f SW1 400  f RC0 64  f RC1 64  u L0u 60  f L0f 36
+i pmi 1  i pmj 1  i pmk 1  f pmf 1  f par0 1  f par1 1  f th0 1  f thr 1  f ca 1  f cb 1  i ia 192  i ic 192  f ib 192
+f duf 192  f DT 192  f DU 192  b OD 192  b O2 192  b T1 192  b CT 64  b ones 160  b OBa 160  b OB 160  h OBh 128  b OB16 128
+b Wb 160  h W8 160  b Zb 160  h Zh 160  b Iw 160  h Ih 128  h Iw0 160  h Iw1 160  b In 128  b In8 128  b Tri 128  b T16 128
+b Mn 128  b Ma 128  f EL 256  f NL 256  f YL 256""".split()
 SCRATCH = {BUFS[k + 1]: ("sbuf", [128, int(BUFS[k + 2])], TYPES[BUFS[k]]) for k in range(0, len(BUFS), 3)}
+SCRATCH["raw"] = ("sbuf", [128, 2, 128], "int32")
+SCRATCH["occf"] = ("sbuf", [128, 2, 128], "float32")
+SCRATCH["r16"] = ("sbuf", [128, 8, 32], "float16")
 SCRATCH["E2"] = ("sbuf", [128, 12, 192], "bfloat16")
-SCRATCH["PL"] = ("psum", [128, 3072], "float32")
-SCRATCH["PM"] = ("psum", [128, 512], "float32")
-SCRATCH["PN"] = ("psum", [128, 512], "float32")
+for _b in range(8):
+    SCRATCH["PS%d" % _b] = ("psum", [128, 512], "float32")
 SEMAPHORES = ["qV", "qS", "qP", "qG", "arr0", "arr1", "snt"] + ["d%d" % i for i in range(14)]
 
 
@@ -51,7 +59,7 @@ def tracker(g, T):
     def before(q, R, W):
         d = [lastw[r] for r in R if r in lastw]
         for r in R:
-            if r[:2] in ("PL", "PM", "PN"):
+            if r[:2] == "PS":
                 d += [x for x in readers.get(r, []) if x[0] != q]
         for w in W:
             if w in lastw and not (q == "P" and lastw[w][0] == "P"):
@@ -109,8 +117,10 @@ def rank_program(g, core, T, topo):
     op, dma, arrive, before, finish = tracker(g, T)
     arrive("arr0", NE, ["RC0"])
     arrive("arr1", NE, ["RC1"])
-    SKW = ["SK", "SKd"] + ["SK_%d" % i for i in range(16)]
-    RD = SKW + ["SKb"]
+    SKW = ["SKa", "SKb", "SKz", "SKy"]
+    NUMW = ["NUM0", "NUM1"]
+    PS = [T["PS%d" % b] for b in range(8)]
+    Ib, OB = T.Iw[:, 16:144], T.OB[:, 16:144]
 
     def v(fn, R, W):
         op("V", fn, R, W)
@@ -127,250 +137,264 @@ def rank_program(g, core, T, topo):
     def mm(out, l, r, a, b):
         return lambda: P.matmul(out, l, r, a, b)
 
-    dma("Y", T.occ32[:, :], T.occ[:, :], [], ["occ32"])
-    dma("S", T.cs32[1:128, :], T.cards[0:127, :], [], ["cs32a"])
+    def lanes(key, a, b):
+        return ["%s%d" % (key, k) for k in range(a // 8, (b + 7) // 8)]
+
+    dma("Y", T.raw[:, 0, :], T.occ[0:8:2, :], [], ["raw0"])
+    dma("S", T.raw[:, 1, :], T.occ[1:8:2, :], [], ["raw1"])
     dma("Y", T.skw[:, :], T.skill[:, :], [], ["skw"])
-    dma("S", T.cs32[0:1, :], T.cards[127:128, :], [], ["cs32b"])
     dma("S", T.cd32[:, :], T.cards[:, :], [], ["cd32"])
-    dma("S", T.nd[:, :], T.need[:, :], [], ["nd"])
+    dma("Y", T.nd[:, :], T.need[:, :], [], ["nd"])
     dma("Y", T.cov[:, :], T.cover[:, :], [], ["cov"])
 
     v(lambda: V.memset(T.ones[:, :], 1.0), [], ["ones"])
+    v(lambda: V.memset(T.z16[:, :], -200.0), [], ["z16"])
+    s(lambda: S.activation(T.SK[:, NST:NBG], T.z16[:, :], F_.Sigmoid), ["z16"], ["SKz"])
+    v(lambda: V.memset(T.SK[:, NBG:NRD], 8192.0), [], ["SKy"])
     gp(lambda: g.iota(T.pmi[:, :], [[0, 1]], 0, 1), [], ["pmi"])
-    gp(lambda: g.iota(T.ib[:, :], [[16, 12], [0, 16]], 4097, 0), [], ["ib"])
-    gp(lambda: g.iota(T.ia[:, :], [[1, 192]], 256, -1), [], ["ia"])
     gp(lambda: g.affine_select(T.OBa[:, :], T.ones[:, :], [[-16, 10], [0, 16]], A_.is_ge, 0.0, 16, 1), ["ones"], ["OBa"])
     gp(lambda: g.affine_select(T.OB[:, :], T.OBa[:, :], [[16, 10], [0, 16]], A_.is_ge, 0.0, -1, -1), ["OBa"], ["OB"])
     gp(lambda: g.affine_select(T.Wb[:, :], T.OB[:, :], [[0, 10], [1, 16]], A_.is_equal, 0.0, 0, 0), ["OB"], ["Wb"])
+    gp(lambda: g.affine_select(T.Iw[:, :], T.ones[:, :], [[1, 160]], A_.is_equal, 0.0, -16, -1), ["ones"], ["Iw"])
+    gp(lambda: g.affine_select(T.Sb[:, :], OB, [[1, 128]], A_.is_equal, 0.0, -1, -1), ["OB"], ["Sb"])
     gp(lambda: g.affine_select(T.Zb[:, :], T.Wb[:, :], [[1, 160]], A_.is_equal, 0.0, -16, -1), ["Wb"], ["Zb"])
     gp(lambda: g.affine_select(T.Yb[:, :], T.Wb[:, :], [[1, 160]], A_.is_equal, 0.0, -1, -1), ["Wb"], ["Yb"])
-    gp(lambda: g.affine_select(T.Ib[:, :], T.ones[:, 0:128], [[1, 128]], A_.is_equal, 0.0, 0, -1), ["ones"], ["Ib"])
-    gp(lambda: g.affine_select(T.Tri[:, :], T.OB[:, 16:144], [[1, 128]], A_.is_gt, 0.0, 0, -1), ["OB"], ["Tri"])
-    v(lambda: V.memset(T.SK[:, NST:NDUMP], 0.0), [], ["SKd"])
-    v(lambda: V.memset(T.SK[:, NDUMP:NWIN], BIGS), [], ["SKb"])
-    v(lambda: V.memset(T.N1[:, :], 0.0), [], ["N1"])
+    gp(lambda: g.affine_select(T.Tri[:, :], OB, [[1, 128]], A_.is_gt, 0.0, 0, -1), ["OB"], ["Tri"])
+    gp(lambda: g.iota(T.ib[:, :], [[16, 12], [0, 16]], 193, 0, allow_small_or_imprecise_dtypes=True), [], ["ib"])
+    gp(lambda: g.iota(T.ZS[:, :], [[0, 1024]], -200, 0, allow_small_or_imprecise_dtypes=True), [], ["ZS"])
+    gp(lambda: g.iota(T.ia[:, :], [[1, 192]], 256, -1), [], ["ia"])
+    v(lambda: V.memset(T.X[:, 0:1024], 2048.0), [], lanes("X", 0, 64))
+    for a in (0, 64):
+        v(lambda: V.tensor_copy(T.N[:, 16 * a:16 * a + 1024], T.X[:, 0:1024]), lanes("X", 0, 64), lanes("N", a, a + 64))
     v(lambda: V.tensor_scalar(T.pmj[:, :], T.pmi[:, :], 15, None, A_.bitwise_and), ["pmi"], ["pmj"])
-    v(lambda: V.memset(T.N2[:, :], 0.0), [], ["N2"])
+    v(lambda: V.tensor_scalar(T.pmk[:, :], T.pmi[:, :], 16, None, A_.bitwise_and), ["pmi"], ["pmk"])
+    v(lambda: V.tensor_copy(T.N[:, 2048:3072], T.X[:, 0:1024]), lanes("X", 0, 64), lanes("N", 128, 192))
+    v(lambda: V.tensor_scalar(T.ca[:, :], T.pmj[:, :], 8.0, -(2.0 ** 25), A_.is_lt, A_.mult), ["pmj"], ["ca"])
+    v(lambda: V.tensor_scalar(T.cb[:, :], T.pmj[:, :], 8.0, float(NKP), A_.is_equal, A_.mult), ["pmj"], ["cb"])
+    v(lambda: V.tensor_scalar(T.pz[:, :], T.pmj[:, :], 0.0, float(NBG - 2048), A_.is_equal, A_.mult), ["pmj"], ["pz"])
+    v(lambda: V.tensor_scalar(T.cz[:, :], T.pz[:, :], 2048.0, None, A_.add), ["pz"], ["cz"])
     v(lambda: V.tensor_copy(T.pmf[:, :], T.pmj[:, :]), ["pmj"], ["pmf"])
-    v(lambda: V.tensor_scalar(T.ic[:, :], T.ia[:, :], 15, None, A_.bitwise_and), ["ia"], ["ic"])
-    v(lambda: V.tensor_scalar(T.pk[:, :], T.pmf[:, :], 0.0, None, A_.is_gt), ["pmf"], ["pk"])
-    v(lambda: V.tensor_scalar(T.pz[:, :], T.pmf[:, :], 0.0, float(NDUMP), A_.is_equal, A_.mult), ["pmf"], ["pz"])
-    v(lambda: V.tensor_scalar(T.th0[:, :], T.pmf[:, :], float(KV), 8.0, A_.is_lt, A_.mult), ["pmf"], ["th0"])
-    v(lambda: V.tensor_copy(T.bof[:, :], T.occ32[:, :]), ["occ32"], ["bof"])
-    v(lambda: V.tensor_scalar(T.cm[:, 0:192], T.cs32[:, 0:192], T.pk[:, 0:1], T.pz[:, 0:1], A_.mult, A_.add), ["cs32a", "cs32b", "pk", "pz"], ["cm0"])
-    v(lambda: V.tensor_scalar(T.dtf[:, :], T.ib[:, :], T.pmf[:, 0:1], None, A_.add), ["ib", "pmf"], ["dtf"])
-    v(lambda: V.tensor_scalar(T.OD[:, :], T.ic[:, :], 0.0, BIGS, A_.not_equal, A_.mult), ["ic"], ["OD"])
-    v(lambda: V.tensor_scalar(T.thr[:, :], T.th0[:, :], -0.5, None, A_.add), ["th0"], ["thr"])
-    v(lambda: V.tensor_scalar(T.duf[:, :], T.dtf[:, :], -3905.0, None, A_.add), ["dtf"], ["duf"])
-    v(lambda: V.tensor_copy(T.Wh[:, :], T.Wb[:, :]), ["Wb"], ["Wh"])
-    v(lambda: V.tensor_scalar(T.TC[:, :], T.OD[:, :], 10240.0, None, A_.add), ["OD"], ["TC"])
-    v(lambda: V.memset(T.SW0[:, 0:64], 0.0), [], ["SW0"])
-    v(lambda: V.memset(T.SW1[:, 0:64], 0.0), [], ["SW1"])
-    gp(lambda: g.affine_select(T.DT[:, :], T.dtf[:, :], [[0, 12], [1, 16]], A_.is_equal, 0.0, 0, 0), ["dtf"], ["DT"])
+    for out, src, key, k in (("OB16", OB, "OB", 16384.0), ("In", Ib, "Iw", -1.0), ("In8", Ib, "Iw", -8192.0),
+                             ("T16", T.Tri[:, :], "Tri", 16384.0), ("Ma", T.Tri[:, :], "Tri", 8192.0)):
+        s(lambda: S.activation(T[out][:, :], src, F_.Copy, scale=k), [key], [out])
+    s(lambda: S.activation(T.duf[:, :], T.ib[:, :], F_.Identity, bias=T.pmf[:, 0:1]), ["ib", "pmf"], ["duf"])
+    s(lambda: S.activation(T.dtf[:, :], T.duf[:, :], F_.Copy, bias=float(NRD - 192)), ["duf"], ["dtf"])
+    gp(lambda: g.affine_select(T.Mn[:, :], T.Ma[:, :], [[1, 128]], A_.not_equal, -8192.0, 0, -1), ["Ma"], ["Mn"])
     gp(lambda: g.affine_select(T.DU[:, :], T.duf[:, :], [[0, 12], [1, 16]], A_.is_equal, 0.0, 0, 0), ["duf"], ["DU"])
-    gp(lambda: g.iota(T.NUM[:, 0:NDUMP], [[0, NDUMP]], 0, 0, allow_small_or_imprecise_dtypes=True), [], ["NUM"])
-    v(lambda: V.memset(T.skw[:, 2047:2048], -1.0), [], ["skw"])
-    v(lambda: V.tensor_scalar(T.skp[:, 0:2048], T.skw[:, :].indirect(T.bof[:, 0:128]), EPS, 0.0, A_.add, A_.max), ["skw", "bof"], ["skpa"])
-    s(lambda: S.activation(T.skp[:, 2048:4096], T.skw[:, :].indirect(T.bof[:, 128:256]), F_.Relu, bias=EPS), ["skw", "bof"], ["skpb"])
-    v(lambda: V.tensor_scalar(T.N1[:, 0:2048:16], T.nd[:, 0:128], -1.0, None, A_.mult), ["nd"], ["N1"])
-    v(lambda: V.tensor_scalar(T.ch[:, :], T.cd32[:, :], -2048.0, None, A_.add), ["cd32"], ["ch"])
+    gp(lambda: g.affine_select(T.DT[:, :], T.dtf[:, :], [[0, 12], [1, 16]], A_.is_equal, -8192.0, 0, 0), ["dtf"], ["DT"])
+    for buf, a, b, val in (("SW0", 0, 64, 2048), ("SW1", 0, 64, 2048), ("sv", 192, 384, 0), ("nv", 192, 384, 2047), ("NUM", 0, NRD, 2047)):
+        gp(lambda: g.iota(T[buf][:, a:b], [[0, b - a]], val, 0, allow_small_or_imprecise_dtypes=True), [], [buf + "z" if a else buf])
+    for h in range(2):
+        v(lambda: V.tensor_copy(T.r16[:, :, 16 * h:16 * h + 16], T.raw[:, h, :]), ["raw%d" % h], ["r16%d" % h])
+    for b in range(8):
+        v(lambda: V.transpose(T.tr[:, b:256:8], T.r16[:, b, :]), ["r160", "r161"], ["tr%d" % b])
+    v(lambda: V.tensor_copy(T.bof[:, :], T.tr[:, :]), ["tr%d" % b for b in range(8)], ["bof"])
+    v(lambda: V.tensor_scalar(T.W8[:, :], T.Wb[:, :], 8192.0, None, A_.mult), ["Wb"], ["W8"])
+    v(lambda: V.tensor_copy(T.Ih[:, :], Ib), ["Iw"], ["Ih"])
+    v(lambda: V.tensor_scalar(T.CT[:, :], T.ones[:, 0:64], T.ca[:, 0:1], T.cb[:, 0:1], A_.mult, A_.add), ["ones", "ca", "cb"], ["CT"])
+    v(lambda: V.tensor_copy(T.Sh[:, :], T.Sb[:, :]), ["Sb"], ["Sh"])
     v(lambda: V.tensor_copy(T.Zh[:, :], T.Zb[:, :]), ["Zb"], ["Zh"])
     v(lambda: V.tensor_copy(T.Yh[:, :], T.Yb[:, :]), ["Yb"], ["Yh"])
-    p([mm(T.PN[:, 0:36], T.Zh[:, 16 - i:144 - i], T.ch[:, i:576:16], i == 0, i == 15) for i in range(16)], ["Zh", "ch"], ["PN"])
-    p([mm(T.PN[:, 36:72], T.Yh[:, 16 - i:144 - i], T.ch[:, i:576:16], i == 0, i == 15) for i in range(16)], ["Yh", "ch"], ["PN"])
-    for i in range(16):
-        if i < 10:
-            v(lambda: V.tensor_copy(T.SK[:, 256 * i:256 * i + 256], T.skp[:, i:4096:16]), ["skpa", "skpb"], ["SK_%d" % i])
-        else:
-            s(lambda: S.activation(T.SK[:, 256 * i:256 * i + 256], T.skp[:, i:4096:16], F_.Copy), ["skpa", "skpb"], ["SK_%d" % i])
-    v(lambda: V.tensor_scalar(T.L0u[:, :], T.PN[:, 0:72], 2048.0, None, A_.add), ["PN"], ["L0u"])
+    v(lambda: V.tensor_copy(T.OBh[:, :], OB), ["OB"], ["OBh"])
+    v(lambda: V.tensor_scalar(T.par0[:, :], T.pmk[:, :], 0.0, None, A_.is_equal), ["pmk"], ["par0"])
+    v(lambda: V.tensor_scalar(T.par1[:, :], T.pmk[:, :], 0.0, None, A_.is_gt), ["pmk"], ["par1"])
+    v(lambda: V.tensor_scalar(T.th0[:, :], T.pmj[:, :], float(KV), 8.0, A_.is_lt, A_.mult), ["pmj"], ["th0"])
+    v(lambda: V.tensor_scalar(T.Iw0[:, :], T.Iw[:, :], T.par0[:, 0:1], None, A_.mult), ["Iw", "par0"], ["Iw0"])
+    v(lambda: V.tensor_scalar(T.Iw1[:, :], T.Iw[:, :], T.par1[:, 0:1], None, A_.mult), ["Iw", "par1"], ["Iw1"])
+    v(lambda: V.tensor_scalar(T.thr[:, :], T.th0[:, :], -0.5, None, A_.add), ["th0"], ["thr"])
+    v(lambda: V.memset(T.skw[:, 2047:2048], -1.0), [], ["skw"])
+    s(lambda: S.activation(T.SK[:, 0:16 * KS], T.skw[:, :].indirect(T.bof[:, 0:KS]), F_.Relu, bias=EPS), ["skw", "bof"], ["SKa"])
+    v(lambda: V.tensor_scalar(T.ch[:, 0:128], T.cd32[:, 0:128], -2048.0, None, A_.add), ["cd32"], ["ch0"])
+    p([mm(PS[3][:, 0:128], T.Sh[:, :], T.ch[:, 0:128], True, True)]
+      + [mm(PS[3][:, 128:136], T.Yh[:, 16 - i:144 - i], T.ch[:, i:128:16], i == 0, i == 15) for i in range(16)], ["Sh", "Yh", "ch0"], ["PS3"])
+    v(lambda: V.tensor_scalar(T.SK[:, 16 * KS:NST], T.skw[:, :].indirect(T.bof[:, KS:256]), EPS, 0.0, A_.add, A_.max), ["skw", "bof"], ["SKb"])
+    v(lambda: V.tensor_scalar(T.cu[:, 0:128], PS[3][:, 0:128], T.cz[:, 0:1], None, A_.add), ["PS3", "cz"], ["cu0"])
+    v(lambda: V.tensor_scalar(T.L0u[:, 36:44], PS[3][:, 128:136], 2048.0, None, A_.add), ["PS3"], ["L15"])
 
-    def prep_m(t):
-        L = 128 if t == 0 else 192
-        v(lambda: V.tensor_copy(T.mf[:, 0:L], T.cov[:, :].indirect(T.L0u[:, 12 * t:12 * t + L // 16])), ["cov", "L0u"], ["mf"])
-        v(lambda: V.tensor_copy(T.mu[:, 0:L], T.mf[:, 0:L]), ["mf"], ["mu"])
+    def own_needs(t):
+        v(lambda: V.tensor_scalar(T.N[:, 0:2048:16], T.nd[:, 128 * t:128 * t + 128], -1.0, 2048.0, A_.mult, A_.add), ["nd"], lanes("N", 0, 128))
 
-    def prep_s(t):
-        L = 128 if t == 0 else 192
-        s(lambda: S.activation(T.ms[:, 0:L], T.mf[:, 0:L], F_.Sign, bias=-2047.5), ["mf"], ["ms"])
-        s(lambda: S.activation(T.PN[:, 256:256 + L], T.ms[:, 0:L], F_.Copy, bias=-2047.5, scale=0.5), ["ms"], ["PN"])
-
-    def prep_c(t):
-        L = 128 if t == 0 else 192
-        v(lambda: V.tensor_tensor(T.code16[:, 0:L], T.mf[:, 0:L], T.PN[:, 256:256 + L], A_.add), ["mf", "PN"], ["code16"])
-
-    win = T.SK[:, 0:NWIN]
+    win = T.SK[:, 0:NRD]
 
     for t in range(3):
         last = t == 2
         L = 128 if t == 0 else 192
         C = L // 16
-        H = L // 2
         c0 = 192 * t
-        LL = T["LL%d" % t]
-        sv = T.sv0 if t == 0 else T.sv1
-        kv = "0" if t == 0 else "1"
-        cuk, cmk = (["cu0"], ["cm0"]) if t == 0 else (["cu1"], ["cm1"])
+        kc = "0" if t == 0 else "1"
+        ch = CHUNKS[L]
+        vl = VLANES[L]
+        L0u, L0f = T.L0u[:, 12 * t:12 * t + C], T.L0f[:, 12 * t:12 * t + C]
+        B = T.X[:, 1:16 * L:16]
 
-        def leave(b, src, key):
-            p(mm(T.PL[:, 512 * b:512 * b + 512], T.OB[:, 16:144], src, True, True), ["OB", key], ["PL%d" % b])
+        def scan(k):
+            a, b = ch[k], ch[k + 1]
+            Y = PS[k % 2][:, 0:b - a]
+            v(lambda: V.tensor_tensor_scan(T.R[:, 16 * a:16 * b], T.X[:, 16 * a:16 * b], T.N[:, 16 * a:16 * b], 0.0, A_.add, A_.min),
+              lanes("X", a, b) + lanes("N", a, b), lanes("R", a, b))
+            p(mm(Y, OB, T.CT[:, 0:b - a], True, False), ["OB", "CT"], ["PS%d" % (k % 2)])
+            p([mm(Y, T.W8[:, 16 - i:144 - i], T.R[:, 16 * a + i:16 * b:16], False, False) for i in range(16)]
+              + [mm(Y, T.Ih[:, :], T.ch[:, c0 + a:c0 + b], False, True)], ["W8", "Ih", "ch" + kc] + lanes("R", a, b), ["PS%d" % (k % 2)])
 
-        def scat(k):
-            src = T.XA[:, 1 + 1024 * k:1025 + 1024 * k] if k < 2 else T.XB[:, 1:1025]
-            v(lambda: V.tensor_tensor(win.indirect(T.cu[:, c0 + 64 * k:c0 + 64 * k + 64]), src, T.keep[:, 1024 * k:1024 * k + 1024], A_.mult),
-              cuk + ["keep%d" % k] + (["XA0", "XA1", "XAf"] if k < 2 else ["XBa", "XBb", "XBf"]), SKW)
+        def empty(k):
+            a, b = ch[k], ch[k + 1]
+            v(lambda: V.tensor_tensor(T.yl[:, 0:b - a], PS[k % 2][:, 0:b - a], T.ch[:, c0 + a:c0 + b], A_.max), ["PS%d" % (k % 2), "ch" + kc], ["yl"])
+            v(lambda: V.tensor_scalar(T.lst[:, a:b], T.yl[:, 0:b - a], 2048.0, None, A_.add), ["yl"], ["lst%d" % k])
+            s(lambda: S.activation(T.SK[:, :].indirect(T.lst[:, a:b]), T.ZS[:, 0:16 * (b - a)], F_.Sigmoid), ["lst%d" % k, "ZS"], SKW)
 
-        v(lambda: V.tensor_copy(T.XA[:, 0:1024], win.indirect(T.cm[:, c0:c0 + 64])), RD + cmk, ["XA0"])
-        s(lambda: S.activation(T.XA[:, 1024:2048], win.indirect(T.cm[:, c0 + 64:c0 + 128]), F_.Copy), RD + cmk, ["XA1"])
-        if t:
-            s(lambda: S.activation(T.XB[:, 512:1024], win.indirect(T.cm[:, c0 + 160:c0 + 192]), F_.Copy), RD + cmk, ["XBb"])
-        v(lambda: V.tensor_tensor_scan(T.R1[:, 0:1024], T.XA[:, 0:1024], T.N1[:, 0:1024], 0.0, A_.add, A_.min), ["XA0", "XAf", "N1"], ["R1a"])
-        for b in range(2):
-            leave(b, T.R1[:, 512 * b:512 * b + 512], "R1a")
-        if t:
-            v(lambda: V.tensor_copy(T.XB[:, 0:512], win.indirect(T.cm[:, c0 + 128:c0 + 160])), RD + cmk, ["XBa"])
-        s(lambda: S.activation(T.keep[:, 0:1024], T.PL[:, 0:1024], F_.Relu, bias=1.0), ["PL0", "PL1"], ["keep0"])
-        if t:
-            v(lambda: V.tensor_copy(T.a15[:, 0:64], win.indirect(T.L0u[:, 44 + 12 * t:48 + 12 * t])), RD + ["L0u"], ["a15"])
-        v(lambda: V.tensor_tensor_scan(T.R1[:, 1024:2048], T.XA[:, 1024:2048], T.N1[:, 1024:2048], 0.0, A_.add, A_.min), ["XA1", "XAf", "N1"], ["R1b"])
-        for b in range(2, 4):
-            leave(b, T.R1[:, 512 * b:512 * b + 512], "R1b")
-        s(lambda: S.activation(T.keep[:, 1024:2048], T.PL[:, 1024:2048], F_.Relu, bias=1.0), ["PL2", "PL3"], ["keep1"])
-        v(lambda: V.tensor_copy(T.XA[:, 16:2064:16], win.indirect(T.L0u[:, 36 + 12 * t:44 + 12 * t])), RD + ["L0u", "XA0", "XA1"], ["XAf"])
-        if t == 0:
-            v(lambda: V.tensor_copy(T.cu[:, 0:192], T.cd32[:, 0:192]), ["cd32"], ["cu0"])
-            v(lambda: V.tensor_scalar(T.L0f[:, :], T.PN[:, 0:36], 2048.0, None, A_.add), ["PN"], ["L0f"])
-            v(lambda: V.tensor_copy(T.occf[:, :], T.occ32[:, :]), ["occ32"], ["occf"])
-            dma("Y", T.NUM[0:128:16, 0:NST], T.occf[:, :], ["occf"], ["NUM"])
-        else:
-            prep_c(t)
-        scat(0)
-        if t == 0:
-            prep_m(0)
-            s(lambda: S.activation(T.I5[:, :], T.Ib[:, :], F_.Copy, scale=512.0), ["Ib"], ["I5"])
-            s(lambda: S.activation(T.In[:, :], T.Ib[:, :], F_.Copy, scale=-1.0), ["Ib"], ["In"])
-        else:
-            rc = T["RC%d" % (t - 1)]
-            v(lambda: V.tensor_scalar(T.N2[:, 0:1024:16], rc[:, :], 0.0, None, A_.min), ["RC%d" % (t - 1)], ["N2"])
-            v(lambda: V.tensor_tensor_scan(T.R2[:, :], T.XB[:, 0:1024], T.N2[:, :], 0.0, A_.add, A_.min), ["XBa", "XBb", "XBf", "N2"], ["R2"])
-            for b in range(4, 6):
-                leave(b, T.R2[:, 512 * (b - 4):512 * (b - 4) + 512], "R2")
-            s(lambda: S.activation(T.keep[:, 2048:3072], T.PL[:, 2048:3072], F_.Relu, bias=1.0), ["PL4", "PL5"], ["keep2"])
-            v(lambda: V.tensor_copy(T.XB[:, 16:1040:16], T.a15[:, :]), ["a15", "XBa", "XBb"], ["XBf"])
+        v(lambda: V.tensor_copy(T.X[:, 0:16 * ch[1]], win.indirect(T.cu[:, c0:c0 + ch[1]])), SKW + ["cu" + kc], lanes("X", 0, ch[1]))
+        s(lambda: S.activation(T.X[:, 16 * vl:16 * L], win.indirect(T.cu[:, c0 + vl:c0 + L]), F_.Copy), SKW + ["cu" + kc], lanes("X", vl, L))
         if not last:
-            p([mm(T.PN[:, 0:128], T.Ib[:, :], T.XA[:, 1 + i:2048:16], i == 0, False) for i in range(15)]
-              + [mm(T.PN[:, 0:128], T.Ib[:, :], T.XA[:, 16:2064:16], False, False), mm(T.PN[:, 0:128], T.In[:, :], T.nd[:, 128 * t:128 * t + 128], False, True)],
-              ["Ib", "In", "nd", "XA0", "XA1", "XAf"], ["PN"])
-            if t:
-                p([mm(T.PN[:, 128:192], T.Ib[:, :], T.XB[:, 1 + i:1024:16], i == 0, False) for i in range(15)]
-                  + [mm(T.PN[:, 128:192], T.Ib[:, :], T.a15[:, :], False, True)], ["Ib", "XBa", "XBb", "a15"], ["PN"])
-        s(lambda: S.activation(T.eb[:, 0:128], T.XA[:, 1:2048:16], F_.Relu, bias=512.0, scale=-(2.0 ** 50)), ["XA0", "XA1"], ["eb"])
-        p([mm(T.PL[:, 0:128], T.Ib[:, :], T.XA[:, 1:2048:16], True, False), mm(T.PL[:, 0:128], T.I5[:, :], T.keep[:, 0:2048:16], False, False),
-           mm(T.PL[:, 0:128], T.Ib[:, :], T.eb[:, 0:128], False, True)], ["Ib", "I5", "XA0", "XA1", "keep0", "keep1", "eb"], ["PL0"])
-        scat(1)
-        if t and not last:
-            v(lambda: V.tensor_tensor(T.df[:, 128:192], T.PN[:, 128:192], T.N2[:, 0:1024:16], A_.add), ["PN", "N2"], ["dfb"])
+            s(lambda: S.activation(T.x15[:, 0:L], win.indirect(T.L0u[:, 36 + 12 * t:36 + 12 * t + C]), F_.Copy), SKW + ["L15"], ["x15"])
+        if t == 0:
+            own_needs(0)
+        scan(0)
+        v(lambda: V.tensor_copy(T.X[:, 16 * ch[1]:16 * vl], win.indirect(T.cu[:, c0 + ch[1]:c0 + vl])), SKW + ["cu" + kc], lanes("X", ch[1], vl))
+        empty(0)
         if t:
-            scat(2)
-            s(lambda: S.activation(T.eb[:, 128:192], T.XB[:, 1:1024:16], F_.Relu, bias=512.0, scale=-(2.0 ** 50)), ["XBa", "XBb"], ["eb"])
-            p([mm(T.PL[:, 128:192], T.Ib[:, :], T.XB[:, 1:1024:16], True, False), mm(T.PL[:, 128:192], T.I5[:, :], T.keep[:, 2048:3072:16], False, False),
-               mm(T.PL[:, 128:192], T.Ib[:, :], T.eb[:, 128:192], False, True)], ["Ib", "I5", "XBa", "XBb", "keep2", "eb"], ["PL0"])
-        s(lambda: S.activation(T.bsb[:, 0:L], T.PL[:, 0:L], F_.Copy), ["PL0"], ["bsb"])
-        if not last:
-            s(lambda: S.activation(T.df[:, 0:128], T.PN[:, 0:128], F_.Copy), ["PN"], ["df"])
-            s(lambda: S.activation(T.um[:, 0:L], T.df[:, 0:L], F_.Relu, scale=-1.0), ["df", "dfb"], ["um"])
-            p(mm(T.PM[:, 0:L], T.OB[:, 16:144], T.um[:, 0:L], True, True), ["OB", "um"], ["PM"])
-            s(lambda: S.activation(T.us[:, 0:L], T.PM[:, 0:L], F_.Sign, bias=-0.5), ["PM"], ["us"])
-            s(lambda: S.activation(T.uf[:, 0:L], T.us[:, 0:L], F_.Relu), ["us"], ["uf"])
-            s(lambda: S.activation(T.ux[:, 0:L], T.uf[:, 0:L], F_.Copy, bias=8191.0, scale=-8192.0), ["uf"], ["ux"])
-            s(lambda: S.activation(T.N1[:, 0:2048:16], T.nd[:, 128 * t + 128:128 * t + 256], F_.Copy, scale=-1.0), ["nd"], ["N1"])
+            v(lambda: V.tensor_copy(T.N[:, 2048:3072:16], T["RC%d" % (t - 1)][:, :]), ["RC%d" % (t - 1)], lanes("N", 128, 192))
+        for k in range(1, len(ch) - 1):
+            scan(k)
+            if k > 1:
+                empty(k - 1)
         if t == 0:
-            s(lambda: S.activation(T.OB8[:, :], T.OB[:, 16:144], F_.Copy, scale=8192.0), ["OB"], ["OB8"])
-            s(lambda: S.activation(T.OBn[:, :], T.OB[:, 16:144], F_.Copy, scale=-8192.0), ["OB"], ["OBn"])
-            s(lambda: S.activation(T.T8[:, :], T.Tri[:, :], F_.Copy, scale=8192.0), ["Tri"], ["T8"])
-            prep_s(0)
-        v(lambda: V.tensor_copy(T.AG[:, 0:16 * H], win.indirect(T.mu[:, 0:H])), RD + ["mu"], ["AGa"])
-        s(lambda: S.activation(T.AG[:, 16 * H:16 * L], win.indirect(T.mu[:, H:L]), F_.Copy), RD + ["mu"], ["AGb"])
-        if last:
-            dma("Y", T.EL[:, :], T.SK[0:128:16, 0:NST], SKW, ["EL"])
-        for i in range(KV):
-            v(lambda: V.tensor_tensor(T.ge[:, L * i:L * i + L], T.AG[:, i:16 * L:16], T.PL[:, 0:L], A_.is_ge), ["AGa", "AGb", "PL0"], ["ge%d" % i])
-        order = list(range(4))
-        for k in range((16 - KV) // 2):
-            b = 512 * (2 + k)
-            i = KV + 2 * k
-            for h in range(2):
-                p([mm(T.PL[:, b + L * h:b + L * h + L], T.Ib[:, :], T.AG[:, i + h:16 * L:16], True, False),
-                   mm(T.PL[:, b + L * h:b + L * h + L], T.In[:, :], T.bsb[:, 0:L], False, True)], ["Ib", "In", "AGa", "AGb", "bsb"], ["PL%d" % (2 + k)])
-            s(lambda: S.activation(T.ge[:, L * i:L * i + 2 * L], T.PL[:, b:b + 2 * L], F_.Sign, bias=EPS / 2), ["PL%d" % (2 + k)], ["ge%d" % i, "ge%d" % (i + 1)])
-            order += [i, i + 1]
-            order += list(range(4 + 2 * k, min(6 + 2 * k, KV)))
-        order += [i for i in range(16) if i not in order]
-        for i in order:
-            p(mm(T.PL[:, 512:512 + L], T.Wb[:, 16 - i:144 - i], T.ge[:, L * i:L * i + L], i == order[0], i == order[-1]), ["Wb", "ge%d" % i], ["PL1"] if i in (order[0], order[-1]) else [])
+            v(lambda: V.tensor_scalar(T.ch[:, 192:576], T.cd32[:, 192:576], -2048.0, None, A_.add), ["cd32"], ["ch1"])
+        empty(len(ch) - 2)
         if t == 0:
-            prep_c(0)
-            v(lambda: V.tensor_copy(T.OBh[:, :], T.OB[:, 16:144]), ["OB"], ["OBh"])
+            p([mm(PS[3][:, 0:8], T.Zh[:, 16 - i:144 - i], T.ch[:, i:128:16], i == 0, i == 15) for i in range(16)]
+              + [mm(PS[3][:, 12:36], T.Zh[:, 16 - i:144 - i], T.ch[:, 192 + i:576:16], i == 0, i == 15) for i in range(16)]
+              + [mm(PS[3][:, 36:48], T.Yh[:, 16 - i:144 - i], T.ch[:, 192 + i:384:16], i == 0, i == 15) for i in range(16)]
+              + [mm(PS[3][:, 128:512], T.Sh[:, :], T.ch[:, 192:576], True, True)], ["Zh", "Yh", "Sh", "ch0", "ch1"], ["PS3"])
+            v(lambda: V.tensor_scalar(T.ic[:, :], T.ia[:, :], 15, None, A_.bitwise_and), ["ia"], ["ic"])
+            v(lambda: V.tensor_scalar(T.OD[:, :], T.ic[:, :], 0.0, 8192.0, A_.not_equal, A_.mult), ["ic"], ["OD"])
+            for a, b in ((0, 8), (12, 36)):
+                v(lambda: V.tensor_scalar(T.L0u[:, a:b], PS[3][:, a:b], 2048.0, None, A_.add), ["PS3"], ["L0u"])
+                v(lambda: V.tensor_scalar(T.L0f[:, a:b], PS[3][:, a:b], 2048.0, None, A_.add), ["PS3"], ["L0f"])
+            v(lambda: V.tensor_scalar(T.L0u[:, 48:60], PS[3][:, 36:48], 2048.0, None, A_.add), ["PS3"], ["L15"])
+            v(lambda: V.tensor_scalar(T.cu[:, 192:576], PS[3][:, 128:512], T.cz[:, 0:1], None, A_.add), ["PS3", "cz"], ["cu1"])
         if not last:
-            v(lambda: V.tensor_tensor_scan(T.cum[:, 0:L], T.uf[:, 0:L], T.uf[:, 0:L], 0.0, A_.add, A_.max), ["uf"], ["cum"])
-            prep_m(t + 1)
-        v(lambda: V.tensor_scalar(T.Fb[:, 0:L], T.PL[:, 512:512 + L], T.thr[:, 0:1], None, A_.is_ge), ["PL1", "thr"], ["Fb"])
-        p(mm(T.PL[:, 1024:1024 + L], T.Tri[:, :], T.Fb[:, 0:L], True, True), ["Tri", "Fb"], ["PL2"])
+            p([mm(PS[7][:, 0:L], Ib, T.x15[:, 0:L], True, False), mm(PS[7][:, 0:L], T.Ih[:, :], T.R[:, 15:16 * L:16], False, True)], ["Iw", "Ih", "x15"] + lanes("R", 0, L), ["PS7"])
+            v(lambda: V.tensor_scalar(T.R16[:, 0:L], PS[7][:, 0:L], 2048.0, None, A_.min), ["PS7"], ["R16"])
+        v(lambda: V.tensor_scalar(T.mf[:, 0:L], T.cov[:, :].indirect(L0u), -2048.0, None, A_.add), ["cov", "L0u"], ["mf"])
+        v(lambda: V.tensor_scalar(T.eb[:, 0:L], B, EPS / 2, 65536.0, A_.is_lt, A_.mult), lanes("X", 0, L), ["eb"])
+        v(lambda: V.transpose(T.mt[:, 0:L], T.mf[:, 0:L]), ["mf"], ["mt"])
+        p([mm(PS[2][:, 0:L], T.OBh[:, :], T.R[:, 0:16 * L:16], True, False), mm(PS[2][:, 0:L], Ib, T.eb[:, 0:L], False, True)]
+          + ([] if last else [mm(PS[2][:, 192:192 + L], T.OBh[:, :], T.R16[:, 0:L], True, True)]), ["OBh", "Iw", "eb", "R16"] + lanes("R", 0, L), ["PS2"])
+        p([mm(PS[3][:, c:16 * C:C], T["Iw%d" % (c % 2)][:, 16 + 16 * (c % 2 - h):144 + 16 * (c % 2 - h)], T.mt[:, 32 * (c // 2) + 16 * h:32 * (c // 2) + 16 * h + 16], h == 0, h == 1)
+           for c in range(C) for h in range(2)], ["Iw0", "Iw1", "mt"], ["PS3"])
+        for k in range(max(VCALLS)):
+            v(lambda: V.tensor_copy(T.Br[:, L * k:L * k + L], B), lanes("X", 0, L), ["Br%d" % k])
+        BR = ["Br%d" % k for k in range(max(VCALLS))]
+        v(lambda: V.tensor_scalar(T.nl[:, 0:L], PS[2][:, 0:L], 32767.5, 16384.0, A_.is_ge, A_.mult), ["PS2"], ["nl"])
         if not last:
-            p([mm(T.PM[:, 0:L], T.Ib[:, :], T.OD[:, 0:L], True, False), mm(T.PM[:, 0:L], T.Ib[:, :], T.ux[:, 0:L], False, False),
-               mm(T.PM[:, 0:L], T.Ib[:, :], T.cum[:, 0:L], False, True)], ["Ib", "OD", "ux", "cum"], ["PM"])
-        else:
-            v(lambda: V.tensor_scalar(T.ef[:, :], T.EL[:, :], 0.0, 2047.0, A_.is_equal, A_.mult), ["EL"], ["ef"])
-        v(lambda: V.tensor_tensor(T.sel[:, 0:L], T.PL[:, 1024:1024 + L], T.Fb[:, 0:L], A_.is_lt), ["PL2", "Fb"], ["sel"])
-        v(lambda: V.tensor_tensor(T.selm[:, 0:L], T.sel[:, 0:L], T.code16[:, 0:L], A_.mult), ["sel", "code16"], ["selm"])
-        p(mm(T.PL[:, 1536:1536 + L], T.OBh[:, :], T.selm[:, 0:L], True, True), ["OBh", "selm"], ["PL3"])
-        p([mm(T.PL[:, 2048:2048 + C], T.Wh[:, 16 - i:144 - i], T.selm[:, i:L:16], i == 0, i == 15) for i in range(16)], ["Wh", "selm"], ["PL4"])
+            v(lambda: V.tensor_scalar(T.uf[:, 0:L], PS[2][:, 192:192 + L], 32767.5, None, A_.is_lt), ["PS2"], ["uf"])
+        v(lambda: V.tensor_scalar(T.mu[:, 0:L], PS[3][:, 0:L], 2048.0, None, A_.add), ["PS3"], ["mu"])
+        if t == 0:
+            v(lambda: V.tensor_scalar(T.T1[:, :], T.OD[:, :], 2.0, -32768.0, A_.mult, A_.add), ["OD"], ["T1"])
+            v(lambda: V.tensor_scalar(T.O2[:, :], T.OD[:, :], 8192.0, None, A_.add), ["OD"], ["O2"])
+            v(lambda: V.tensor_copy(T.occf[:, :, :], T.raw[:, :, :]), ["raw0", "raw1"], ["occf"])
+            dma("Y", T.NUM[0:128:32, 0:NST], T.occf[:, 0, :], ["occf", "NUM"], ["NUM0"])
+            dma("Y", T.NUM[16:128:32, 0:NST], T.occf[:, 1, :], ["occf", "NUM"], ["NUM1"])
+        p(mm(PS[4][:, 0:L], T.In[:, :], T.nl[:, 0:L], True, False), ["In", "nl"], ["PS4"])
         if not last:
             sw = T["SW%d" % t]
-            v(lambda: V.tensor_tensor_scan(T.uy[:, 0:L], T.DU[:, 0:L], T.PM[:, 0:L], 0.0, A_.max, A_.min), ["DU", "PM"], ["uy"])
-            v(lambda: V.tensor_copy(T.ul[:, 0:C], T.uy[:, 15:L:16]), ["uy"], ["ul"])
-            v(lambda: V.tensor_copy(sw[:, :].indirect(T.ul[:, 0:C]), T.df[:, 0:L]), ["ul", "df", "dfb"], ["SW%d" % t])
+            v(lambda: V.tensor_tensor_scan(T.cum[:, 0:L], T.uf[:, 0:L], T.uf[:, 0:L], 0.0, A_.add, A_.max), ["uf"], ["cum"])
+            p([mm(PS[7][:, 0:L], Ib, T.O2[:, 0:L], True, False), mm(PS[7][:, 0:L], T.In8[:, :], T.uf[:, 0:L], False, False),
+               mm(PS[7][:, 0:L], Ib, T.cum[:, 0:L], False, True)], ["Iw", "In8", "O2", "uf", "cum"], ["PS7"])
+            own_needs(t + 1)
+            v(lambda: V.tensor_tensor_scan(T.uy[:, 0:L], T.DU[:, 0:L], PS[7][:, 0:L], 0.0, A_.max, A_.min), ["DU", "PS7"], ["uy"])
+            v(lambda: V.tensor_scalar(T.ul[:, 0:C], T.uy[:, 15:L:16], -1.0, None, A_.add), ["uy"], ["ul"])
+            v(lambda: V.tensor_copy(sw[:, :].indirect(T.ul[:, 0:C]), T.R16[:, 0:L]), ["ul", "R16"], ["SW%d" % t])
             before("G", ["SW%d" % t], [])
             rid, pid, _se = topo.addr(nxt)
             em = sum(1 << e for e in topo.engines(core, nxt)[:NE])
             g.remote_dma(T["RC%d" % t][:, :], sw[:, 0:64], T.sem["arr%d" % t], T.sem.snt, pid, rid, em)
-        else:
-            v(lambda: V.tensor_tensor(T.YL[:, :], T.NL[:, :], T.ef[:, :], A_.max), ["NL", "ef"], ["YL"])
-            dma("Y", T.NUM[0:128:16, 0:NST], T.YL[:, :], ["YL"], ["NUM"])
-        v(lambda: V.tensor_copy(T.Rh[:, 0:L], T.PL[:, 1536:1536 + L]), ["PL3"], ["Rh"])
+        if t:
+            Lb = 128 if t == 1 else 192
+            v(lambda: V.tensor_copy(T.NUM[:, :].indirect(T.LL[:, 0:Lb // 16]), T.nv[:, 192 - Lb:192]), ["LLa", "nv"], NUMW)
+        if last:
+            dma("Y", T.NL[:, :], T.NUM[0:128:16, 0:NST], NUMW, ["NL"])
+            dma("Y", T.EL[:, :], T.SK[0:128:16, 0:NST], SKW, ["EL"])
+        p(mm(PS[5][:, 0:L], T.Ih[:, :], T.mf[:, 0:L], True, False), ["Ih", "mf"], ["PS5"])
+        p(mm(PS[6][:, 0:L], Ib, T.T1[:, 0:L], True, False), ["Iw", "T1"], ["PS6"])
+        p([mm(PS[7][:, 0:L], Ib, T.T1[:, 0:L], True, False), mm(PS[7][:, 0:L], Ib, T.nl[:, 0:L], False, False)], ["Iw", "T1", "nl"], ["PS7"])
+        done = []
+
+        def count(cs):
+            for i in cs:
+                done.append(i)
+                p(mm(PS[4][:, 0:L], T.Wb[:, 16 - i:144 - i], T.ge[:, L * i:L * i + L], False, len(done) == 16), ["Wb", "ge%d" % i], ["PS4"] if len(done) == 16 else [])
+
+        def vcall(k):
+            a = sum(VCALLS[:k])
+            b = a + VCALLS[k]
+            v(lambda: V.tensor_tensor(T.ge[:, L * a:L * b], win.indirect(T.mu[:, C * a:C * b]), T.Br[:, 0:L * (b - a)], A_.is_ge),
+              SKW + ["mu"] + BR, ["ge%d" % i for i in range(a, b)])
+            return range(a, b)
+
+        def sgather(k):
+            i = KV + 2 * k
+            s(lambda: S.activation(T.AG[:, 2 * L * k:2 * L * k + 2 * L], win.indirect(T.mu[:, C * i:C * i + 2 * C]), F_.Copy), SKW + ["mu"], ["AG%d" % k])
+
+        def sdiff(k):
+            D = PS[k % 2]
+            p([mm(D[:, 0:2 * L], T.In[:, :], T.Br[:, 0:2 * L], True, False), mm(D[:, 0:2 * L], Ib, T.AG[:, 2 * L * k:2 * L * k + 2 * L], False, True)],
+              ["Iw", "In", "AG%d" % k] + BR, ["PS%d" % (k % 2)])
+
+        def ssign(k):
+            i = KV + 2 * k
+            s(lambda: S.activation(T.ge[:, L * i:L * i + 2 * L], PS[k % 2][:, 0:2 * L], F_.Sign, bias=EPS / 2), ["PS%d" % (k % 2)], ["ge%d" % i, "ge%d" % (i + 1)])
+            return [i, i + 1]
+
+        sgather(0)
+        va = vcall(0)
+        sdiff(0)
+        sgather(1)
+        sa = ssign(0)
+        vb = vcall(1)
+        sdiff(1)
+        count(va)
+        sgather(2)
+        count(sa)
+        sb = ssign(1)
+        vc = vcall(2)
+        count(vb)
+        sdiff(2)
+        sc = ssign(2)
+        count(sb)
+        vd = vcall(3)
+        count(vc)
+        count(vd)
+        count(sc)
+        if last:
+            s(lambda: S.activation(PS[2][:, 0:256], T.EL[:, :], F_.Relu, bias=2047.0, scale=-(2.0 ** 60)), ["EL"], ["PS2"])
+        v(lambda: V.tensor_scalar(T.Fb[:, 0:L], PS[4][:, 0:L], T.thr[:, 0:1], None, A_.is_ge), ["PS4", "thr"], ["Fb"])
+        p(mm(PS[5][:, 0:L], T.Mn[:, :], T.Fb[:, 0:L], False, True), ["Mn", "Fb"], ["PS5"])
+        v(lambda: V.tensor_scalar(T.selm[:, 0:L], PS[5][:, 0:L], 8192.0, 2048.0, A_.add, A_.min), ["PS5"], ["selm"])
+        p(mm(PS[6][:, 0:L], T.OBh[:, :], T.selm[:, 0:L], False, True), ["OBh", "selm"], ["PS6"])
+        p(mm(PS[0][:, 0:L], T.OBh[:, :], T.selm[:, 0:L], True, True), ["OBh", "selm"], ["PS0"])
+        p(mm(PS[7][:, 0:L], T.OBh[:, :], T.selm[:, 0:L], False, False), ["OBh", "selm"], ["PS7"])
+        v(lambda: V.tensor_tensor_scan(T.v1[:, 0:L], T.DT[:, 0:L], PS[6][:, 0:L], 0.0, A_.max, A_.min), ["DT", "PS6"], ["v1"])
+        s(lambda: S.activation(T.Rh[:, 0:L], PS[0][:, 0:L], F_.Copy, bias=-30720.0), ["PS0"], ["Rh"])
+        v(lambda: V.tensor_scalar(T.LG[:, 0:C], T.v1[:, 15:L:16], float(NST), None, A_.add), ["v1"], ["LG"])
+        if not last:
+            s(lambda: S.activation(T.sv[:, 192 - L:192], T.SK[:, 0:NRD].indirect(T.LG[:, 0:C]), F_.Copy), SKW + ["LG"], ["sv"])
+        s(lambda: S.activation(T.nv[:, 192 - L:192], T.NUM[:, 0:NRD].indirect(T.LG[:, 0:C]), F_.Copy), NUMW + ["LG"], ["nv"])
+        if last:
+            v(lambda: V.tensor_tensor(T.YL[:, :], PS[2][:, 0:256], T.NL[:, :], A_.max), ["NL", "PS2"], ["YL"])
+            dma("Y", T.NF[0:128:16, 0:NST], T.YL[:, :], ["YL"], ["NF"])
         for c in range(C):
-            v(lambda: V.tensor_scalar(T.E2[:, c, 0:L - 16 * c], T.Rh[:, 16 * c:L], T.PL[:, 2048 + c:2049 + c], None, A_.is_equal), ["Rh", "PL4"], ["E%d" % c])
-        X = T.PL[:, 2560:2560 + L]
-        p([mm(X, T.Ib[:, :], T.TC[:, 0:L], True, False), mm(X, T.OBh[:, :], T.selm[:, 0:L], False, False),
-           mm(X, T.OBn[:, :], T.sel[:, 0:L], False, False)], ["Ib", "TC", "OBh", "selm", "OBn", "sel"], ["PL5"])
-        for c in range(C - 1):
-            p(mm(T.PL[:, 2560 + 16 * c + 16:2560 + L], T.OB8[:, :], T.E2[:, c, 16:L - 16 * c], False, False), ["OB8", "E%d" % c], [])
-        p(mm(X, T.T8[:, :], T.E2[:, 0:C, 0:16], False, True), ["T8"] + ["E%d" % c for c in range(C)], ["PL5"])
+            v(lambda: V.tensor_scalar(T.E2[:, c, 0:L - 16 * c], T.Rh[:, 16 * c:L], -2048.0, T.v1[:, 16 * c + 15:16 * c + 16], A_.add, A_.is_equal), ["Rh", "v1"], ["E%d" % c])
+            if c < C - 1:
+                p(mm(PS[7][:, 16 * c + 16:L], T.OB16[:, :], T.E2[:, c, 16:L - 16 * c], False, False), ["OB16", "E%d" % c], [])
+        p(mm(PS[7][:, 0:L], T.T16[:, :], T.E2[:, 0:C, 0:16], False, True), ["T16"] + ["E%d" % c for c in range(C)], ["PS7"])
+        v(lambda: V.tensor_tensor_scan(T.v2[:, 0:L], T.DT[:, 0:L], PS[7][:, 0:L], 0.0, A_.max, A_.min), ["DT", "PS7"], ["v2"])
+        v(lambda: V.tensor_tensor(T.la[:, 0:C], T.v2[:, 15:L:16], L0f, A_.max), ["v2", "L0f"], ["la"])
+        v(lambda: V.tensor_scalar(T.LL[:, C:2 * C], T.v2[:, 15:L:16], float(NST), None, A_.add), ["v2"], ["LLb"])
+        v(lambda: V.tensor_copy(T.LL[:, 0:C], T.la[:, 0:C]), ["la"], ["LLa"])
         if not last:
-            prep_s(t + 1)
-        v(lambda: V.tensor_tensor_scan(T.vx[:, 0:L], T.DT[:, 0:L], X, 0.0, A_.max, A_.min), ["DT", "PL5"], ["vx"])
-        v(lambda: V.tensor_scalar(T.tg[:, 0:C], T.vx[:, 15:L:16], 2048.0, -1.0, A_.is_gt, A_.mult), ["vx"], ["tg"])
-        v(lambda: V.tensor_tensor(T.offf[:, 0:C], T.vx[:, 15:L:16], T.tg[:, 0:C], A_.add), ["vx", "tg"], ["offf"])
-        v(lambda: V.tensor_copy(LL[:, C:2 * C], T.offf[:, 0:C]), ["offf"], ["LLb"])
-        if not last:
-            s(lambda: S.activation(sv[:, 0:L], win.indirect(LL[:, C:2 * C]), F_.Copy), RD + ["LLb"], ["sv" + kv])
-        s(lambda: S.activation(T.nv[:, 0:L], T.NUM[:, 0:NDUMP].indirect(LL[:, C:2 * C]), F_.Copy), ["NUM", "LLb"], ["nv"])
-        v(lambda: V.tensor_scalar(T.tu[:, 0:C], T.vx[:, 15:L:16], 4096.5, float(NWIN), A_.is_gt, A_.mult), ["vx"], ["tu"])
-        v(lambda: V.tensor_tensor(T.slf[:, 0:C], T.tu[:, 0:C], T.L0f[:, 12 * t:12 * t + C], A_.add), ["tu", "L0f"], ["slf"])
-        v(lambda: V.tensor_copy(LL[:, 0:C], T.slf[:, 0:C]), ["slf"], ["LLa"])
-        if t == 0:
-            v(lambda: V.memset(T.sv0[:, 128:256], 0.0), [], ["sv0z"])
-        if not last:
-            v(lambda: V.tensor_copy(T.SK[:, :].indirect(LL[:, 0:2 * C]), sv[:, 0:2 * L]), ["LLa", "LLb", "sv" + kv, "sv%sz" % kv], SKW)
-        if t == 0:
-            v(lambda: V.tensor_scalar(T.cm[:, 192:576], T.cs32[:, 192:576], T.pk[:, 0:1], T.pz[:, 0:1], A_.mult, A_.add), ["cs32a", "cs32b", "pk", "pz"], ["cm1"])
-            v(lambda: V.tensor_copy(T.cu[:, 192:576], T.cd32[:, 192:576]), ["cd32"], ["cu1"])
-            v(lambda: V.memset(T.sv1[:, 192:384], 0.0), [], ["sv1z"])
-            v(lambda: V.memset(T.nv[:, 192:384], 2047.0), [], ["nvz"])
-        K = 2 if last else 1
-        v(lambda: V.tensor_copy(T.NUM[:, :].indirect(LL[:, 0:K * C]), T.nv[:, 0:K * L]), ["LLa", "LLb", "nv", "nvz"], ["NUM"])
-        if t == 1:
-            dma("Y", T.NL[:, :], T.NUM[0:128:16, 0:NST], ["NUM"], ["NL"])
-    dma("Y", T.y[:, :], T.NUM[0:128:16, 0:NST], ["NUM"], ["y"])
+            v(lambda: V.tensor_copy(T.SK[:, :].indirect(T.LL[:, 0:2 * C]), T.sv[:, 192 - L:192 + L]), ["LLa", "LLb", "sv", "svz"], SKW)
+    v(lambda: V.tensor_copy(T.NF[:, :].indirect(T.LL[:, 0:24]), T.nv[:, :]), ["LLa", "LLb", "nv", "nvz"], ["NF"])
+    dma("Y", T.y[:, :], T.NF[0:128:16, 0:NST], ["NF"], ["y"])
     g.wait_ge(T.sem.snt, 2 * NE)
     finish()

@@ -2,25 +2,26 @@ from concourse.mybir import dt, AluOpType as A_, ActivationFunctionType as F_
 
 EPS = 2.0 ** -40
 NST = 4096
-NBG = NST + 8
-NRD = NST + 16
+NBG = NST + 16
+NRD = NST + 32
 NKP = 4608
-KV = 10
-VCALLS = [4, 3, 2, 1]
-CHUNKS = {128: [0, 32, 80, 128], 192: [0, 40, 96, 144, 192]}
-VLANES = {128: 56, 192: 88}
+SC = 8192.0
+VCALLS = [4, 4, 2, 1]
+SCALLS = [2, 2, 1]
+KV = sum(VCALLS)
+CHUNKS = {128: [0, 24, 72, 128], 192: [0, 40, 112, 192]}
+VLANES = {128: (44, 50, 56), 192: (70, 78, 88)}
 KS = 136
 
 TYPES = {"b": "bfloat16", "f": "float32", "i": "int32", "u": "uint16", "h": "float16"}
-BUFS = """b skw 2048  h tr 256  u bof 256  f SK 8704  f NUM 4320  f NF 8416  f dtf 192  i cov 4096  i cd32 576  u cu 576  h ch 576
-b X 3072  h N 3072  h R 3072  b x15 192  h R16 192  b Sb 128  h Sh 128  b Yb 160  h Yh 160  f pz 1  f cz 1
-b nd 384  f ZS 1024  f z16 8  f yl 64  u lst 192  h mf 192  h mt 192  u mu 192  b Br 768  b AG 1152  b ge 3072
-b eb 192  b nl 192  b Fb 192  h selm 192  h Rh 192  f v1 192  f v2 192  u LG 12  f la 12  u LL 24  f sv 384  f nv 384
-b uf 192  b cum 192  f uy 192  u ul 12  f SW0 400  f SW1 400  f RC0 64  f RC1 64  u L0u 60  f L0f 36
-i pmi 1  i pmj 1  i pmk 1  f pmf 1  f par0 1  f par1 1  f th0 1  f thr 1  f ca 1  f cb 1  i ia 192  i ic 192  f ib 192
-f duf 192  f DT 192  f DU 192  b OD 192  b O2 192  b T1 192  b CT 64  b ones 160  b OBa 160  b OB 160  h OBh 128  b OB16 128
-b Wb 160  h W8 160  b Zb 160  h Zh 160  b Iw 160  h Ih 128  h Iw0 160  h Iw1 160  b In 128  b In8 128  b Tri 128  b T16 128
-b Mn 128  b Ma 128  f EL 256  f NL 256  f YL 256""".split()
+BUFS = """b skw 2064  h tr 256  u bof 256  f SK 8704  f NUM 4448  f NF 8544  i cov 4096  i cd32 576  u cu 576  h ch 576
+b X 3072  h N 3072  h R 3072  b x15 192  h R16 192  b nd 384  f ZS 1280  f z16 16  f yl 80  u lst 192  h mf 192  h mt 192
+u mu 192  b Br 768  b AG 1152  b ge 3072  b eb 192  b nl 192  b Fb 192  h selm 192  h Rh 192  f v1 192  f v2 192  u LG 12
+f la 12  u LL 24  f sv 384  f nv 384  b uf 192  b cum 192  f uy 192  u ul 12  f SW0 512  f SW1 512  f RC0 64  f RC1 64
+u L0u 60  f L0f 36  i pmi 1  i pmj 1  f th0 1  f thr 1  i ia 192  i ic 192  f duf 192  f dtf 192  f DT 192  f DU 192
+b OD 192  b O2 192  b T1 192  b CTa 80  b CTb 80  b CZ 384  b ones 160  b OBa 160  b OB 160  b OB16 128  b Sb 128  b Wb 160
+b Zb 160  b Yb 160  b Iw 160  b Iw0 160  b Iw1 160  b In 128  b In8 128  b Tri 128  b T16 128  b Mn 128  b Ma 128
+f EL 256  f NL 256  f YL 256""".split()
 SCRATCH = {BUFS[k + 1]: ("sbuf", [128, int(BUFS[k + 2])], TYPES[BUFS[k]]) for k in range(0, len(BUFS), 3)}
 SCRATCH["raw"] = ("sbuf", [128, 2, 128], "int32")
 SCRATCH["occf"] = ("sbuf", [128, 2, 128], "float32")
@@ -28,7 +29,7 @@ SCRATCH["r16"] = ("sbuf", [128, 8, 32], "float16")
 SCRATCH["E2"] = ("sbuf", [128, 12, 192], "bfloat16")
 for _b in range(8):
     SCRATCH["PS%d" % _b] = ("psum", [128, 512], "float32")
-SEMAPHORES = ["qV", "qS", "qP", "qG", "arr0", "arr1", "snt"] + ["d%d" % i for i in range(14)]
+SEMAPHORES = ["qV", "qS", "qP", "qG", "arr0", "arr1", "snt"] + ["d%d" % i for i in range(16)]
 
 
 def tracker(g, T):
@@ -140,79 +141,75 @@ def rank_program(g, core, T, topo):
     def lanes(key, a, b):
         return ["%s%d" % (key, k) for k in range(a // 8, (b + 7) // 8)]
 
+    def select(out, src, key, pattern, cmp, fill, base, mult):
+        gp(lambda: g.affine_select(T[out][:, :], src, pattern, cmp, fill, base, mult), [key], [out])
+
+    def count_up(out, key, pattern, base, mult):
+        gp(lambda: g.iota(out, pattern, base, mult, allow_small_or_imprecise_dtypes=True), [], [key])
+
+    def pick(out, lhs, a, b):
+        return [mm(out, lhs[:, 16 - i:144 - i], T.ch[:, a + i:b:16], i == 0, i == 15) for i in range(16)]
+
+    def shift(out, a, b):
+        return [mm(out, T.Zb[:, 16:144], T.CZ[:, 0:b - a], True, False), mm(out, T.Sb[:, :], T.ch[:, a:b], False, True)]
+
+    def station(out, src, R, W):
+        v(lambda: V.tensor_scalar(out, src, SC, 2048.0, A_.mult, A_.add), R, W)
+
+    def cards16(a, b, key):
+        v(lambda: V.tensor_scalar(T.ch[:, a:b], T.cd32[:, a:b], -2048.0, 1.0 / SC, A_.add, A_.mult), ["cd" + key], ["ch" + key])
+
+    def own_needs(t):
+        v(lambda: V.tensor_scalar(T.N[:, 0:2048:16], T.nd[:, 128 * t:128 * t + 128], -1.0, 2048.0, A_.mult, A_.add), ["nd"], lanes("N", 0, 128))
+
     dma("Y", T.raw[:, 0, :], T.occ[0:8:2, :], [], ["raw0"])
     dma("S", T.raw[:, 1, :], T.occ[1:8:2, :], [], ["raw1"])
-    dma("Y", T.skw[:, :], T.skill[:, :], [], ["skw"])
-    dma("S", T.cd32[:, :], T.cards[:, :], [], ["cd32"])
+    dma("Y", T.skw[:, 0:2048], T.skill[:, :], [], ["skw"])
+    dma("S", T.cd32[:, 0:128], T.cards[:, 0:128], [], ["cd0"])
     dma("Y", T.nd[:, :], T.need[:, :], [], ["nd"])
+    dma("Y", T.cd32[:, 192:576], T.cards[:, 192:576], [], ["cd1"])
     dma("Y", T.cov[:, :], T.cover[:, :], [], ["cov"])
 
     v(lambda: V.memset(T.ones[:, :], 1.0), [], ["ones"])
     v(lambda: V.memset(T.z16[:, :], -200.0), [], ["z16"])
     s(lambda: S.activation(T.SK[:, NST:NBG], T.z16[:, :], F_.Sigmoid), ["z16"], ["SKz"])
-    v(lambda: V.memset(T.SK[:, NBG:NRD], 8192.0), [], ["SKy"])
-    gp(lambda: g.iota(T.pmi[:, :], [[0, 1]], 0, 1), [], ["pmi"])
-    gp(lambda: g.affine_select(T.OBa[:, :], T.ones[:, :], [[-16, 10], [0, 16]], A_.is_ge, 0.0, 16, 1), ["ones"], ["OBa"])
-    gp(lambda: g.affine_select(T.OB[:, :], T.OBa[:, :], [[16, 10], [0, 16]], A_.is_ge, 0.0, -1, -1), ["OBa"], ["OB"])
-    gp(lambda: g.affine_select(T.Wb[:, :], T.OB[:, :], [[0, 10], [1, 16]], A_.is_equal, 0.0, 0, 0), ["OB"], ["Wb"])
-    gp(lambda: g.affine_select(T.Iw[:, :], T.ones[:, :], [[1, 160]], A_.is_equal, 0.0, -16, -1), ["ones"], ["Iw"])
-    gp(lambda: g.affine_select(T.Sb[:, :], OB, [[1, 128]], A_.is_equal, 0.0, -1, -1), ["OB"], ["Sb"])
-    gp(lambda: g.affine_select(T.Zb[:, :], T.Wb[:, :], [[1, 160]], A_.is_equal, 0.0, -16, -1), ["Wb"], ["Zb"])
-    gp(lambda: g.affine_select(T.Yb[:, :], T.Wb[:, :], [[1, 160]], A_.is_equal, 0.0, -1, -1), ["Wb"], ["Yb"])
-    gp(lambda: g.affine_select(T.Tri[:, :], OB, [[1, 128]], A_.is_gt, 0.0, 0, -1), ["OB"], ["Tri"])
-    gp(lambda: g.iota(T.ib[:, :], [[16, 12], [0, 16]], 193, 0, allow_small_or_imprecise_dtypes=True), [], ["ib"])
-    gp(lambda: g.iota(T.ZS[:, :], [[0, 1024]], -200, 0, allow_small_or_imprecise_dtypes=True), [], ["ZS"])
+    select("OBa", T.ones[:, :], "ones", [[-16, 10], [0, 16]], A_.is_ge, 0.0, 16, 1)
+    select("OB", T.OBa[:, :], "OBa", [[16, 10], [0, 16]], A_.is_ge, 0.0, -1, -1)
+    select("Sb", OB, "OB", [[1, 128]], A_.is_equal, 0.0, -1, -1)
+    select("Wb", T.OB[:, :], "OB", [[0, 10], [1, 16]], A_.is_equal, 0.0, 0, 0)
+    select("Zb", T.Wb[:, :], "Wb", [[1, 160]], A_.is_equal, 0.0, -16, -1)
+    select("Yb", T.Wb[:, :], "Wb", [[1, 160]], A_.is_equal, 0.0, -1, -1)
+    select("Iw", T.ones[:, :], "ones", [[1, 160]], A_.is_equal, 0.0, -16, -1)
+    count_up(T.ZS[:, :], "ZS", [[0, 1280]], -200, 0)
+    select("Tri", OB, "OB", [[1, 128]], A_.is_gt, 0.0, 0, -1)
     gp(lambda: g.iota(T.ia[:, :], [[1, 192]], 256, -1), [], ["ia"])
+    gp(lambda: g.iota(T.pmi[:, :], [[0, 1]], 0, 1), [], ["pmi"])
+    for h in range(2):
+        select("Iw%d" % h, T.Iw[:, :], "Iw", [[0, 5], [1, 2], [0, 16]], A_.is_equal, 0.0, h - 1, 0)
+    count_up(T.duf[:, :], "duf", [[16, 12], [0, 16]], 193, 1)
+    select("DU", T.duf[:, :], "duf", [[0, 12], [1, 16]], A_.is_equal, 0.0, 0, 0)
+    count_up(T.SW0[:, 0:64], "SW0", [[0, 64]], 2048, 0)
+    count_up(T.dtf[:, :], "dtf", [[16, 12], [0, 16]], NRD + 1, 1)
+    select("DT", T.dtf[:, :], "dtf", [[0, 12], [1, 16]], A_.is_equal, -8192.0, 0, 0)
+    for buf, a, b, val in (("sv", 192, 384, 0), ("nv", 192, 384, 2047), ("SW1", 0, 64, 2048)):
+        count_up(T[buf][:, a:b], buf + "z" if a else buf, [[0, b - a]], val, 0)
     v(lambda: V.memset(T.X[:, 0:1024], 2048.0), [], lanes("X", 0, 64))
-    for a in (0, 64):
-        v(lambda: V.tensor_copy(T.N[:, 16 * a:16 * a + 1024], T.X[:, 0:1024]), lanes("X", 0, 64), lanes("N", a, a + 64))
-    v(lambda: V.tensor_scalar(T.pmj[:, :], T.pmi[:, :], 15, None, A_.bitwise_and), ["pmi"], ["pmj"])
-    v(lambda: V.tensor_scalar(T.pmk[:, :], T.pmi[:, :], 16, None, A_.bitwise_and), ["pmi"], ["pmk"])
-    v(lambda: V.tensor_copy(T.N[:, 2048:3072], T.X[:, 0:1024]), lanes("X", 0, 64), lanes("N", 128, 192))
-    v(lambda: V.tensor_scalar(T.ca[:, :], T.pmj[:, :], 8.0, -(2.0 ** 25), A_.is_lt, A_.mult), ["pmj"], ["ca"])
-    v(lambda: V.tensor_scalar(T.cb[:, :], T.pmj[:, :], 8.0, float(NKP), A_.is_equal, A_.mult), ["pmj"], ["cb"])
-    v(lambda: V.tensor_scalar(T.pz[:, :], T.pmj[:, :], 0.0, float(NBG - 2048), A_.is_equal, A_.mult), ["pmj"], ["pz"])
-    v(lambda: V.tensor_scalar(T.cz[:, :], T.pz[:, :], 2048.0, None, A_.add), ["pz"], ["cz"])
-    v(lambda: V.tensor_copy(T.pmf[:, :], T.pmj[:, :]), ["pmj"], ["pmf"])
-    for out, src, key, k in (("OB16", OB, "OB", 16384.0), ("In", Ib, "Iw", -1.0), ("In8", Ib, "Iw", -8192.0),
-                             ("T16", T.Tri[:, :], "Tri", 16384.0), ("Ma", T.Tri[:, :], "Tri", 8192.0)):
-        s(lambda: S.activation(T[out][:, :], src, F_.Copy, scale=k), [key], [out])
-    s(lambda: S.activation(T.duf[:, :], T.ib[:, :], F_.Identity, bias=T.pmf[:, 0:1]), ["ib", "pmf"], ["duf"])
-    s(lambda: S.activation(T.dtf[:, :], T.duf[:, :], F_.Copy, bias=float(NRD - 192)), ["duf"], ["dtf"])
-    gp(lambda: g.affine_select(T.Mn[:, :], T.Ma[:, :], [[1, 128]], A_.not_equal, -8192.0, 0, -1), ["Ma"], ["Mn"])
-    gp(lambda: g.affine_select(T.DU[:, :], T.duf[:, :], [[0, 12], [1, 16]], A_.is_equal, 0.0, 0, 0), ["duf"], ["DU"])
-    gp(lambda: g.affine_select(T.DT[:, :], T.dtf[:, :], [[0, 12], [1, 16]], A_.is_equal, -8192.0, 0, 0), ["dtf"], ["DT"])
-    for buf, a, b, val in (("SW0", 0, 64, 2048), ("SW1", 0, 64, 2048), ("sv", 192, 384, 0), ("nv", 192, 384, 2047), ("NUM", 0, NRD, 2047)):
-        gp(lambda: g.iota(T[buf][:, a:b], [[0, b - a]], val, 0, allow_small_or_imprecise_dtypes=True), [], [buf + "z" if a else buf])
+    v(lambda: V.memset(T.SK[:, NBG:NRD], 8192.0), [], ["SKy"])
+    v(lambda: V.memset(T.skw[:, 2048:2064], -1.0), [], ["skz"])
+    v(lambda: V.tensor_copy(T.N[:, 0:1024], T.X[:, 0:1024]), lanes("X", 0, 64), lanes("N", 0, 64))
     for h in range(2):
         v(lambda: V.tensor_copy(T.r16[:, :, 16 * h:16 * h + 16], T.raw[:, h, :]), ["raw%d" % h], ["r16%d" % h])
     for b in range(8):
         v(lambda: V.transpose(T.tr[:, b:256:8], T.r16[:, b, :]), ["r160", "r161"], ["tr%d" % b])
-    v(lambda: V.tensor_copy(T.bof[:, :], T.tr[:, :]), ["tr%d" % b for b in range(8)], ["bof"])
-    v(lambda: V.tensor_scalar(T.W8[:, :], T.Wb[:, :], 8192.0, None, A_.mult), ["Wb"], ["W8"])
-    v(lambda: V.tensor_copy(T.Ih[:, :], Ib), ["Iw"], ["Ih"])
-    v(lambda: V.tensor_scalar(T.CT[:, :], T.ones[:, 0:64], T.ca[:, 0:1], T.cb[:, 0:1], A_.mult, A_.add), ["ones", "ca", "cb"], ["CT"])
-    v(lambda: V.tensor_copy(T.Sh[:, :], T.Sb[:, :]), ["Sb"], ["Sh"])
-    v(lambda: V.tensor_copy(T.Zh[:, :], T.Zb[:, :]), ["Zb"], ["Zh"])
-    v(lambda: V.tensor_copy(T.Yh[:, :], T.Yb[:, :]), ["Yb"], ["Yh"])
-    v(lambda: V.tensor_copy(T.OBh[:, :], OB), ["OB"], ["OBh"])
-    v(lambda: V.tensor_scalar(T.par0[:, :], T.pmk[:, :], 0.0, None, A_.is_equal), ["pmk"], ["par0"])
-    v(lambda: V.tensor_scalar(T.par1[:, :], T.pmk[:, :], 0.0, None, A_.is_gt), ["pmk"], ["par1"])
-    v(lambda: V.tensor_scalar(T.th0[:, :], T.pmj[:, :], float(KV), 8.0, A_.is_lt, A_.mult), ["pmj"], ["th0"])
-    v(lambda: V.tensor_scalar(T.Iw0[:, :], T.Iw[:, :], T.par0[:, 0:1], None, A_.mult), ["Iw", "par0"], ["Iw0"])
-    v(lambda: V.tensor_scalar(T.Iw1[:, :], T.Iw[:, :], T.par1[:, 0:1], None, A_.mult), ["Iw", "par1"], ["Iw1"])
-    v(lambda: V.tensor_scalar(T.thr[:, :], T.th0[:, :], -0.5, None, A_.add), ["th0"], ["thr"])
-    v(lambda: V.memset(T.skw[:, 2047:2048], -1.0), [], ["skw"])
-    s(lambda: S.activation(T.SK[:, 0:16 * KS], T.skw[:, :].indirect(T.bof[:, 0:KS]), F_.Relu, bias=EPS), ["skw", "bof"], ["SKa"])
-    v(lambda: V.tensor_scalar(T.ch[:, 0:128], T.cd32[:, 0:128], -2048.0, None, A_.add), ["cd32"], ["ch0"])
-    p([mm(PS[3][:, 0:128], T.Sh[:, :], T.ch[:, 0:128], True, True)]
-      + [mm(PS[3][:, 128:136], T.Yh[:, 16 - i:144 - i], T.ch[:, i:128:16], i == 0, i == 15) for i in range(16)], ["Sh", "Yh", "ch0"], ["PS3"])
-    v(lambda: V.tensor_scalar(T.SK[:, 16 * KS:NST], T.skw[:, :].indirect(T.bof[:, KS:256]), EPS, 0.0, A_.add, A_.max), ["skw", "bof"], ["SKb"])
-    v(lambda: V.tensor_scalar(T.cu[:, 0:128], PS[3][:, 0:128], T.cz[:, 0:1], None, A_.add), ["PS3", "cz"], ["cu0"])
-    v(lambda: V.tensor_scalar(T.L0u[:, 36:44], PS[3][:, 128:136], 2048.0, None, A_.add), ["PS3"], ["L15"])
-
-    def own_needs(t):
-        v(lambda: V.tensor_scalar(T.N[:, 0:2048:16], T.nd[:, 128 * t:128 * t + 128], -1.0, 2048.0, A_.mult, A_.add), ["nd"], lanes("N", 0, 128))
+    v(lambda: V.tensor_scalar(T.bof[:, :], T.tr[:, :], 1.0 + 0.5 / 2046.5, None, A_.mult), ["tr%d" % b for b in range(8)], ["bof"])
+    s(lambda: S.activation(T.SK[:, 0:16 * KS], T.skw[:, :].indirect(T.bof[:, 0:KS]), F_.Relu, bias=EPS), ["skw", "skz", "bof"], ["SKa"])
+    cards16(0, 128, "0")
+    v(lambda: V.memset(T.CZ[:, :], (NBG - 2048) / SC), [], ["CZ"])
+    p(shift(PS[3][:, 0:128], 0, 128) + pick(PS[3][:, 128:136], T.Yb, 0, 128) + pick(PS[3][:, 136:144], T.Zb, 0, 128), ["Sb", "Yb", "Zb", "CZ", "ch0"], ["PS3"])
+    v(lambda: V.tensor_copy(T.N[:, 1024:2048], T.X[:, 0:1024]), lanes("X", 0, 64), lanes("N", 64, 128))
+    v(lambda: V.tensor_scalar(T.SK[:, 16 * KS:NST], T.skw[:, :].indirect(T.bof[:, KS:256]), EPS, 0.0, A_.add, A_.max), ["skw", "skz", "bof"], ["SKb"])
+    station(T.cu[:, 0:128], PS[3][:, 0:128], ["PS3"], ["cu0"])
+    station(T.L0u[:, 36:44], PS[3][:, 128:136], ["PS3"], ["L15"])
 
     win = T.SK[:, 0:NRD]
 
@@ -223,7 +220,7 @@ def rank_program(g, core, T, topo):
         c0 = 192 * t
         kc = "0" if t == 0 else "1"
         ch = CHUNKS[L]
-        vl = VLANES[L]
+        vm, vn, vl = VLANES[L]
         L0u, L0f = T.L0u[:, 12 * t:12 * t + C], T.L0f[:, 12 * t:12 * t + C]
         B = T.X[:, 1:16 * L:16]
 
@@ -232,90 +229,115 @@ def rank_program(g, core, T, topo):
             Y = PS[k % 2][:, 0:b - a]
             v(lambda: V.tensor_tensor_scan(T.R[:, 16 * a:16 * b], T.X[:, 16 * a:16 * b], T.N[:, 16 * a:16 * b], 0.0, A_.add, A_.min),
               lanes("X", a, b) + lanes("N", a, b), lanes("R", a, b))
-            p(mm(Y, OB, T.CT[:, 0:b - a], True, False), ["OB", "CT"], ["PS%d" % (k % 2)])
-            p([mm(Y, T.W8[:, 16 - i:144 - i], T.R[:, 16 * a + i:16 * b:16], False, False) for i in range(16)]
-              + [mm(Y, T.Ih[:, :], T.ch[:, c0 + a:c0 + b], False, True)], ["W8", "Ih", "ch" + kc] + lanes("R", a, b), ["PS%d" % (k % 2)])
+            p([mm(Y, Ib, T.CTa[:, 0:b - a], True, False), mm(Y, Ib, T.CTb[:, 0:b - a], False, False)], ["Iw", "CT"], ["PS%d" % (k % 2)])
+            p([mm(Y, T.Wb[:, 16 - i:144 - i], T.R[:, 16 * a + i:16 * b:16], False, False) for i in range(16)]
+              + [mm(Y, Ib, T.ch[:, c0 + a:c0 + b], False, True)], ["Wb", "ch" + kc] + lanes("R", a, b), ["PS%d" % (k % 2)])
 
-        def empty(k):
+        def empty(k, mid=None, end=None):
             a, b = ch[k], ch[k + 1]
             v(lambda: V.tensor_tensor(T.yl[:, 0:b - a], PS[k % 2][:, 0:b - a], T.ch[:, c0 + a:c0 + b], A_.max), ["PS%d" % (k % 2), "ch" + kc], ["yl"])
-            v(lambda: V.tensor_scalar(T.lst[:, a:b], T.yl[:, 0:b - a], 2048.0, None, A_.add), ["yl"], ["lst%d" % k])
+            if mid:
+                mid()
+            station(T.lst[:, a:b], T.yl[:, 0:b - a], ["yl"], ["lst%d" % k])
+            if end:
+                end()
             s(lambda: S.activation(T.SK[:, :].indirect(T.lst[:, a:b]), T.ZS[:, 0:16 * (b - a)], F_.Sigmoid), ["lst%d" % k, "ZS"], SKW)
 
-        v(lambda: V.tensor_copy(T.X[:, 0:16 * ch[1]], win.indirect(T.cu[:, c0:c0 + ch[1]])), SKW + ["cu" + kc], lanes("X", 0, ch[1]))
+        def vgather(a, b):
+            v(lambda: V.tensor_copy(T.X[:, 16 * a:16 * b], win.indirect(T.cu[:, c0 + a:c0 + b])), SKW + ["cu" + kc], lanes("X", a, b))
+
+        vgather(0, ch[1])
         s(lambda: S.activation(T.X[:, 16 * vl:16 * L], win.indirect(T.cu[:, c0 + vl:c0 + L]), F_.Copy), SKW + ["cu" + kc], lanes("X", vl, L))
         if not last:
             s(lambda: S.activation(T.x15[:, 0:L], win.indirect(T.L0u[:, 36 + 12 * t:36 + 12 * t + C]), F_.Copy), SKW + ["L15"], ["x15"])
         if t == 0:
             own_needs(0)
+            v(lambda: V.memset(T.CTa[:, :], -32768.0), [], ["CT"])
+            v(lambda: V.memset(T.CTb[:, :], NKP / SC), [], ["CT"])
         scan(0)
-        v(lambda: V.tensor_copy(T.X[:, 16 * ch[1]:16 * vl], win.indirect(T.cu[:, c0 + ch[1]:c0 + vl])), SKW + ["cu" + kc], lanes("X", ch[1], vl))
-        empty(0)
+        vgather(ch[1], vm)
+        empty(0, lambda: vgather(vm, vn), lambda: vgather(vn, vl))
         if t:
             v(lambda: V.tensor_copy(T.N[:, 2048:3072:16], T["RC%d" % (t - 1)][:, :]), ["RC%d" % (t - 1)], lanes("N", 128, 192))
         for k in range(1, len(ch) - 1):
             scan(k)
             if k > 1:
                 empty(k - 1)
-        if t == 0:
-            v(lambda: V.tensor_scalar(T.ch[:, 192:576], T.cd32[:, 192:576], -2048.0, None, A_.add), ["cd32"], ["ch1"])
-        empty(len(ch) - 2)
-        if t == 0:
-            p([mm(PS[3][:, 0:8], T.Zh[:, 16 - i:144 - i], T.ch[:, i:128:16], i == 0, i == 15) for i in range(16)]
-              + [mm(PS[3][:, 12:36], T.Zh[:, 16 - i:144 - i], T.ch[:, 192 + i:576:16], i == 0, i == 15) for i in range(16)]
-              + [mm(PS[3][:, 36:48], T.Yh[:, 16 - i:144 - i], T.ch[:, 192 + i:384:16], i == 0, i == 15) for i in range(16)]
-              + [mm(PS[3][:, 128:512], T.Sh[:, :], T.ch[:, 192:576], True, True)], ["Zh", "Yh", "Sh", "ch0", "ch1"], ["PS3"])
-            v(lambda: V.tensor_scalar(T.ic[:, :], T.ia[:, :], 15, None, A_.bitwise_and), ["ia"], ["ic"])
-            v(lambda: V.tensor_scalar(T.OD[:, :], T.ic[:, :], 0.0, 8192.0, A_.not_equal, A_.mult), ["ic"], ["OD"])
-            for a, b in ((0, 8), (12, 36)):
-                v(lambda: V.tensor_scalar(T.L0u[:, a:b], PS[3][:, a:b], 2048.0, None, A_.add), ["PS3"], ["L0u"])
-                v(lambda: V.tensor_scalar(T.L0f[:, a:b], PS[3][:, a:b], 2048.0, None, A_.add), ["PS3"], ["L0f"])
-            v(lambda: V.tensor_scalar(T.L0u[:, 48:60], PS[3][:, 36:48], 2048.0, None, A_.add), ["PS3"], ["L15"])
-            v(lambda: V.tensor_scalar(T.cu[:, 192:576], PS[3][:, 128:512], T.cz[:, 0:1], None, A_.add), ["PS3", "cz"], ["cu1"])
-        if not last:
-            p([mm(PS[7][:, 0:L], Ib, T.x15[:, 0:L], True, False), mm(PS[7][:, 0:L], T.Ih[:, :], T.R[:, 15:16 * L:16], False, True)], ["Iw", "Ih", "x15"] + lanes("R", 0, L), ["PS7"])
-            v(lambda: V.tensor_scalar(T.R16[:, 0:L], PS[7][:, 0:L], 2048.0, None, A_.min), ["PS7"], ["R16"])
-        v(lambda: V.tensor_scalar(T.mf[:, 0:L], T.cov[:, :].indirect(L0u), -2048.0, None, A_.add), ["cov", "L0u"], ["mf"])
         v(lambda: V.tensor_scalar(T.eb[:, 0:L], B, EPS / 2, 65536.0, A_.is_lt, A_.mult), lanes("X", 0, L), ["eb"])
-        v(lambda: V.transpose(T.mt[:, 0:L], T.mf[:, 0:L]), ["mf"], ["mt"])
-        p([mm(PS[2][:, 0:L], T.OBh[:, :], T.R[:, 0:16 * L:16], True, False), mm(PS[2][:, 0:L], Ib, T.eb[:, 0:L], False, True)]
-          + ([] if last else [mm(PS[2][:, 192:192 + L], T.OBh[:, :], T.R16[:, 0:L], True, True)]), ["OBh", "Iw", "eb", "R16"] + lanes("R", 0, L), ["PS2"])
-        p([mm(PS[3][:, c:16 * C:C], T["Iw%d" % (c % 2)][:, 16 + 16 * (c % 2 - h):144 + 16 * (c % 2 - h)], T.mt[:, 32 * (c // 2) + 16 * h:32 * (c // 2) + 16 * h + 16], h == 0, h == 1)
-           for c in range(C) for h in range(2)], ["Iw0", "Iw1", "mt"], ["PS3"])
+        if t == 0:
+            station(L0u, PS[3][:, 136:144], ["PS3"], ["L0u"])
+            station(L0f, PS[3][:, 136:144], ["PS3"], ["L0f"])
+            cards16(192, 576, "1")
+        empty(len(ch) - 2)
+        if not last:
+            p([mm(PS[7][:, 0:L], Ib, T.x15[:, 0:L], True, False), mm(PS[7][:, 0:L], Ib, T.R[:, 15:16 * L:16], False, True)], ["Iw", "x15"] + lanes("R", 0, L), ["PS7"])
+        if t == 0:
+            p(shift(PS[3][:, 128:512], 192, 576) + pick(PS[3][:, 0:24], T.Zb, 192, 576) + pick(PS[3][:, 24:36], T.Yb, 192, 384), ["Zb", "Yb", "Sb", "CZ", "ch1"], ["PS3"])
         for k in range(max(VCALLS)):
             v(lambda: V.tensor_copy(T.Br[:, L * k:L * k + L], B), lanes("X", 0, L), ["Br%d" % k])
         BR = ["Br%d" % k for k in range(max(VCALLS))]
+        if not last:
+            v(lambda: V.tensor_scalar(T.R16[:, 0:L], PS[7][:, 0:L], 2048.0, None, A_.min), ["PS7"], ["R16"])
+        p([mm(PS[2][:, 0:L], OB, T.R[:, 0:16 * L:16], True, False), mm(PS[2][:, 0:L], Ib, T.eb[:, 0:L], False, True)]
+          + ([] if last else [mm(PS[2][:, 192:192 + L], OB, T.R16[:, 0:L], True, True)]), ["OB", "Iw", "eb", "R16"] + lanes("R", 0, L), ["PS2"])
+        if t == 0:
+            v(lambda: V.tensor_scalar(T.ic[:, :], T.ia[:, :], 15, None, A_.bitwise_and), ["ia"], ["ic"])
+            v(lambda: V.tensor_scalar(T.pmj[:, :], T.pmi[:, :], 15, None, A_.bitwise_and), ["pmi"], ["pmj"])
+            for out, src, key, k in (("In8", Ib, "Iw", -8192.0), ("In", Ib, "Iw", -1.0), ("Ma", T.Tri[:, :], "Tri", 8192.0),
+                                     ("OB16", OB, "OB", 16384.0), ("T16", T.Tri[:, :], "Tri", 16384.0)):
+                v(lambda: V.tensor_scalar(T[out][:, :], src, k, None, A_.mult), [key], [out])
+            v(lambda: V.tensor_scalar(T.OD[:, :], T.ic[:, :], 0.0, 8192.0, A_.not_equal, A_.mult), ["ic"], ["OD"])
+            v(lambda: V.tensor_scalar(T.th0[:, :], T.pmj[:, :], float(KV), 8.0, A_.is_lt, A_.mult), ["pmj"], ["th0"])
+            v(lambda: V.tensor_copy(T.occf[:, :, :], T.raw[:, :, :]), ["raw0", "raw1"], ["occf"])
+            v(lambda: V.tensor_scalar(T.O2[:, :], T.OD[:, :], 8192.0, None, A_.add), ["OD"], ["O2"])
+            v(lambda: V.tensor_scalar(T.T1[:, :], T.OD[:, :], 2.0, -32768.0, A_.mult, A_.add), ["OD"], ["T1"])
+            v(lambda: V.tensor_scalar(T.thr[:, :], T.th0[:, :], -0.5, None, A_.add), ["th0"], ["thr"])
+            select("Mn", T.Ma[:, :], "Ma", [[1, 128]], A_.not_equal, -8192.0, 0, -1)
         v(lambda: V.tensor_scalar(T.nl[:, 0:L], PS[2][:, 0:L], 32767.5, 16384.0, A_.is_ge, A_.mult), ["PS2"], ["nl"])
         if not last:
             v(lambda: V.tensor_scalar(T.uf[:, 0:L], PS[2][:, 192:192 + L], 32767.5, None, A_.is_lt), ["PS2"], ["uf"])
-        v(lambda: V.tensor_scalar(T.mu[:, 0:L], PS[3][:, 0:L], 2048.0, None, A_.add), ["PS3"], ["mu"])
         if t == 0:
-            v(lambda: V.tensor_scalar(T.T1[:, :], T.OD[:, :], 2.0, -32768.0, A_.mult, A_.add), ["OD"], ["T1"])
-            v(lambda: V.tensor_scalar(T.O2[:, :], T.OD[:, :], 8192.0, None, A_.add), ["OD"], ["O2"])
-            v(lambda: V.tensor_copy(T.occf[:, :, :], T.raw[:, :, :]), ["raw0", "raw1"], ["occf"])
-            dma("Y", T.NUM[0:128:32, 0:NST], T.occf[:, 0, :], ["occf", "NUM"], ["NUM0"])
-            dma("Y", T.NUM[16:128:32, 0:NST], T.occf[:, 1, :], ["occf", "NUM"], ["NUM1"])
-        p(mm(PS[4][:, 0:L], T.In[:, :], T.nl[:, 0:L], True, False), ["In", "nl"], ["PS4"])
+            station(T.cu[:, 192:576], PS[3][:, 128:512], ["PS3"], ["cu1"])
+            station(T.L0u[:, 12:36], PS[3][:, 0:24], ["PS3"], ["L0u"])
+            station(T.L0f[:, 12:36], PS[3][:, 0:24], ["PS3"], ["L0f"])
+            station(T.L0u[:, 48:60], PS[3][:, 24:36], ["PS3"], ["L15"])
         if not last:
             sw = T["SW%d" % t]
             v(lambda: V.tensor_tensor_scan(T.cum[:, 0:L], T.uf[:, 0:L], T.uf[:, 0:L], 0.0, A_.add, A_.max), ["uf"], ["cum"])
             p([mm(PS[7][:, 0:L], Ib, T.O2[:, 0:L], True, False), mm(PS[7][:, 0:L], T.In8[:, :], T.uf[:, 0:L], False, False),
                mm(PS[7][:, 0:L], Ib, T.cum[:, 0:L], False, True)], ["Iw", "In8", "O2", "uf", "cum"], ["PS7"])
+        p(mm(PS[4][:, 0:L], T.In[:, :], T.nl[:, 0:L], True, False), ["In", "nl"], ["PS4"])
+        v(lambda: V.tensor_scalar(T.mf[:, 0:L], T.cov[:, :].indirect(L0u), -2048.0, None, A_.add), ["cov", "L0u"], ["mf"])
+        if not last:
             own_needs(t + 1)
+        v(lambda: V.transpose(T.mt[:, 0:L], T.mf[:, 0:L]), ["mf"], ["mt"])
+        p([mm(PS[3][:, c:16 * C:C], T["Iw%d" % (c % 2)][:, 16 + 16 * (c % 2 - h):144 + 16 * (c % 2 - h)], T.mt[:, 32 * (c // 2) + 16 * h:32 * (c // 2) + 16 * h + 16], h == 0, h == 1)
+           for c in range(C) for h in range(2)], ["Iw0", "Iw1", "mt"], ["PS3"])
+        if not last:
             v(lambda: V.tensor_tensor_scan(T.uy[:, 0:L], T.DU[:, 0:L], PS[7][:, 0:L], 0.0, A_.max, A_.min), ["DU", "PS7"], ["uy"])
+            if t == 0:
+                v(lambda: V.tensor_scalar(T.N[:, 2048:3072], T.X[:, 0:1024], 0.0, 2048.0, A_.mult, A_.add), lanes("X", 0, 64), lanes("N", 128, 192))
             v(lambda: V.tensor_scalar(T.ul[:, 0:C], T.uy[:, 15:L:16], -1.0, None, A_.add), ["uy"], ["ul"])
+        v(lambda: V.tensor_scalar(T.mu[:, 0:L], PS[3][:, 0:L], 2048.0, None, A_.add), ["PS3"], ["mu"])
+        if not last:
             v(lambda: V.tensor_copy(sw[:, :].indirect(T.ul[:, 0:C]), T.R16[:, 0:L]), ["ul", "R16"], ["SW%d" % t])
             before("G", ["SW%d" % t], [])
             rid, pid, _se = topo.addr(nxt)
             em = sum(1 << e for e in topo.engines(core, nxt)[:NE])
             g.remote_dma(T["RC%d" % t][:, :], sw[:, 0:64], T.sem["arr%d" % t], T.sem.snt, pid, rid, em)
-        if t:
+        if t == 0:
+            count_up(T.NUM[:, 0:NRD], "NUM", [[0, NRD]], 2047, 0)
+            dma("Y", T.NUM[0:128:32, 0:NST], T.occf[:, 0, :], ["occf", "NUM"], ["NUM0"])
+            dma("Y", T.NUM[16:128:32, 0:NST], T.occf[:, 1, :], ["occf", "NUM"], ["NUM1"])
+        else:
             Lb = 128 if t == 1 else 192
+            if t == 1:
+                v(lambda: V.tensor_copy(T.nv[:, 64:192], T.NUM[:, 0:NRD].indirect(T.LG[:, 0:8])), NUMW + ["LG"], ["nv"])
             v(lambda: V.tensor_copy(T.NUM[:, :].indirect(T.LL[:, 0:Lb // 16]), T.nv[:, 192 - Lb:192]), ["LLa", "nv"], NUMW)
         if last:
             dma("Y", T.NL[:, :], T.NUM[0:128:16, 0:NST], NUMW, ["NL"])
             dma("Y", T.EL[:, :], T.SK[0:128:16, 0:NST], SKW, ["EL"])
-        p(mm(PS[5][:, 0:L], T.Ih[:, :], T.mf[:, 0:L], True, False), ["Ih", "mf"], ["PS5"])
+        p(mm(PS[5][:, 0:L], Ib, T.mf[:, 0:L], True, False), ["Iw", "mf"], ["PS5"])
         p(mm(PS[6][:, 0:L], Ib, T.T1[:, 0:L], True, False), ["Iw", "T1"], ["PS6"])
         p([mm(PS[7][:, 0:L], Ib, T.T1[:, 0:L], True, False), mm(PS[7][:, 0:L], Ib, T.nl[:, 0:L], False, False)], ["Iw", "T1", "nl"], ["PS7"])
         done = []
@@ -333,18 +355,18 @@ def rank_program(g, core, T, topo):
             return range(a, b)
 
         def sgather(k):
-            i = KV + 2 * k
-            s(lambda: S.activation(T.AG[:, 2 * L * k:2 * L * k + 2 * L], win.indirect(T.mu[:, C * i:C * i + 2 * C]), F_.Copy), SKW + ["mu"], ["AG%d" % k])
+            i, n = KV + sum(SCALLS[:k]), SCALLS[k]
+            s(lambda: S.activation(T.AG[:, 2 * L * k:2 * L * k + n * L], win.indirect(T.mu[:, C * i:C * (i + n)]), F_.Copy), SKW + ["mu"], ["AG%d" % k])
 
         def sdiff(k):
-            D = PS[k % 2]
-            p([mm(D[:, 0:2 * L], T.In[:, :], T.Br[:, 0:2 * L], True, False), mm(D[:, 0:2 * L], Ib, T.AG[:, 2 * L * k:2 * L * k + 2 * L], False, True)],
+            D, n = PS[k % 2][:, 0:SCALLS[k] * L], SCALLS[k]
+            p([mm(D, T.In[:, :], T.Br[:, 0:n * L], True, False), mm(D, Ib, T.AG[:, 2 * L * k:2 * L * k + n * L], False, True)],
               ["Iw", "In", "AG%d" % k] + BR, ["PS%d" % (k % 2)])
 
         def ssign(k):
-            i = KV + 2 * k
-            s(lambda: S.activation(T.ge[:, L * i:L * i + 2 * L], PS[k % 2][:, 0:2 * L], F_.Sign, bias=EPS / 2), ["PS%d" % (k % 2)], ["ge%d" % i, "ge%d" % (i + 1)])
-            return [i, i + 1]
+            i, n = KV + sum(SCALLS[:k]), SCALLS[k]
+            s(lambda: S.activation(T.ge[:, L * i:L * (i + n)], PS[k % 2][:, 0:n * L], F_.Sign, bias=EPS / 2), ["PS%d" % (k % 2)], ["ge%d" % j for j in range(i, i + n)])
+            return range(i, i + n)
 
         sgather(0)
         va = vcall(0)
@@ -358,35 +380,37 @@ def rank_program(g, core, T, topo):
         count(sa)
         sb = ssign(1)
         vc = vcall(2)
-        count(vb)
         sdiff(2)
+        count(vb)
         sc = ssign(2)
         count(sb)
         vd = vcall(3)
         count(vc)
-        count(vd)
         count(sc)
+        count(vd)
         if last:
             s(lambda: S.activation(PS[2][:, 0:256], T.EL[:, :], F_.Relu, bias=2047.0, scale=-(2.0 ** 60)), ["EL"], ["PS2"])
         v(lambda: V.tensor_scalar(T.Fb[:, 0:L], PS[4][:, 0:L], T.thr[:, 0:1], None, A_.is_ge), ["PS4", "thr"], ["Fb"])
         p(mm(PS[5][:, 0:L], T.Mn[:, :], T.Fb[:, 0:L], False, True), ["Mn", "Fb"], ["PS5"])
         v(lambda: V.tensor_scalar(T.selm[:, 0:L], PS[5][:, 0:L], 8192.0, 2048.0, A_.add, A_.min), ["PS5"], ["selm"])
-        p(mm(PS[6][:, 0:L], T.OBh[:, :], T.selm[:, 0:L], False, True), ["OBh", "selm"], ["PS6"])
-        p(mm(PS[0][:, 0:L], T.OBh[:, :], T.selm[:, 0:L], True, True), ["OBh", "selm"], ["PS0"])
-        p(mm(PS[7][:, 0:L], T.OBh[:, :], T.selm[:, 0:L], False, False), ["OBh", "selm"], ["PS7"])
-        v(lambda: V.tensor_tensor_scan(T.v1[:, 0:L], T.DT[:, 0:L], PS[6][:, 0:L], 0.0, A_.max, A_.min), ["DT", "PS6"], ["v1"])
-        s(lambda: S.activation(T.Rh[:, 0:L], PS[0][:, 0:L], F_.Copy, bias=-30720.0), ["PS0"], ["Rh"])
-        v(lambda: V.tensor_scalar(T.LG[:, 0:C], T.v1[:, 15:L:16], float(NST), None, A_.add), ["v1"], ["LG"])
-        if not last:
-            s(lambda: S.activation(T.sv[:, 192 - L:192], T.SK[:, 0:NRD].indirect(T.LG[:, 0:C]), F_.Copy), SKW + ["LG"], ["sv"])
-        s(lambda: S.activation(T.nv[:, 192 - L:192], T.NUM[:, 0:NRD].indirect(T.LG[:, 0:C]), F_.Copy), NUMW + ["LG"], ["nv"])
+        p(mm(PS[6][:, 0:L], OB, T.selm[:, 0:L], False, True), ["OB", "selm"], ["PS6"])
+        p(mm(PS[0][:, 0:L], OB, T.selm[:, 0:L], True, True), ["OB", "selm"], ["PS0"])
+        p(mm(PS[7][:, 0:L], OB, T.selm[:, 0:L], False, False), ["OB", "selm"], ["PS7"])
         if last:
             v(lambda: V.tensor_tensor(T.YL[:, :], PS[2][:, 0:256], T.NL[:, :], A_.max), ["NL", "PS2"], ["YL"])
             dma("Y", T.NF[0:128:16, 0:NST], T.YL[:, :], ["YL"], ["NF"])
+        v(lambda: V.tensor_tensor_scan(T.v1[:, 0:L], T.DT[:, 0:L], PS[6][:, 0:L], 0.0, A_.max, A_.min), ["DT", "PS6"], ["v1"])
+        s(lambda: S.activation(T.Rh[:, 0:L], PS[0][:, 0:L], F_.Copy, bias=-30720.0), ["PS0"], ["Rh"])
         for c in range(C):
             v(lambda: V.tensor_scalar(T.E2[:, c, 0:L - 16 * c], T.Rh[:, 16 * c:L], -2048.0, T.v1[:, 16 * c + 15:16 * c + 16], A_.add, A_.is_equal), ["Rh", "v1"], ["E%d" % c])
             if c < C - 1:
                 p(mm(PS[7][:, 16 * c + 16:L], T.OB16[:, :], T.E2[:, c, 16:L - 16 * c], False, False), ["OB16", "E%d" % c], [])
+            if c == 1:
+                v(lambda: V.tensor_scalar(T.LG[:, 0:C], T.v1[:, 15:L:16], float(NST), None, A_.add), ["v1"], ["LG"])
+                if not last:
+                    s(lambda: S.activation(T.sv[:, 192 - L:192], win.indirect(T.LG[:, 0:C]), F_.Copy), SKW + ["LG"], ["sv"])
+                if t:
+                    s(lambda: S.activation(T.nv[:, 0:192], T.NUM[:, 0:NRD].indirect(T.LG[:, 0:C]), F_.Copy), NUMW + ["LG"], ["nv"])
         p(mm(PS[7][:, 0:L], T.T16[:, :], T.E2[:, 0:C, 0:16], False, True), ["T16"] + ["E%d" % c for c in range(C)], ["PS7"])
         v(lambda: V.tensor_tensor_scan(T.v2[:, 0:L], T.DT[:, 0:L], PS[7][:, 0:L], 0.0, A_.max, A_.min), ["DT", "PS7"], ["v2"])
         v(lambda: V.tensor_tensor(T.la[:, 0:C], T.v2[:, 15:L:16], L0f, A_.max), ["v2", "L0f"], ["la"])

@@ -6,30 +6,33 @@ NBG = NST + 16
 NRD = NST + 32
 NKP = 4608
 SC = 8192.0
-VCALLS = [4, 4, 2, 1]
-SCALLS = [2, 2, 1]
+VCALLS = [3, 3, 3, 1]
 KV = sum(VCALLS)
-CHUNKS = {128: [0, 24, 72, 128], 192: [0, 40, 112, 192]}
-VLANES = {128: (44, 50, 56), 192: (70, 78, 88)}
+CHUNKS = {128: [0, 24, 64, 128], 192: [0, 24, 64, 128, 192]}
+VLANES = (76, 88)
+SLANES = 104
+VG = 156
+CP = ((1408, 2304, 3200), (1664, 2304, 3200))
 KS = 136
 
 TYPES = {"b": "bfloat16", "f": "float32", "i": "int32", "u": "uint16", "h": "float16"}
-BUFS = """b skw 2064  h tr 256  u bof 256  f SK 8704  f NUM 4448  f NF 8544  i cov 4096  i cd32 576  u cu 576  h ch 576
-b X 3072  h N 3072  h R 3072  b x15 192  h R16 192  b nd 384  f ZS 1280  f z16 16  f yl 80  u lst 192  h mf 192  h mt 192
-u mu 192  b Br 768  b AG 1152  b ge 3072  b eb 192  b nl 192  b Fb 192  h selm 192  h Rh 192  f v1 192  f v2 192  u LG 12
-f la 12  u LL 24  f sv 384  f nv 384  b uf 192  b cum 192  f uy 192  u ul 12  f SW0 512  f SW1 512  f RC0 64  f RC1 64
-u L0u 60  f L0f 36  i pmi 1  i pmj 1  f th0 1  f thr 1  i ia 192  i ic 192  f duf 192  f dtf 192  f DT 192  f DU 192
-b OD 192  b O2 192  b T1 192  b CTa 80  b CTb 80  b CZ 384  b ones 160  b OBa 160  b OB 160  b OB16 128  b Sb 128  b Wb 160
-b Zb 160  b Yb 160  b Iw 160  b Iw0 160  b Iw1 160  b In 128  b In8 128  b Tri 128  b T16 128  b Mn 128  b Ma 128
-f EL 256  f NL 256  f YL 256""".split()
+BUFS = """b skw 2064  h tr 256  u bof 256  f SK 8704  f NUM 4448  f SKC 8544  i cov 4096  i cd32 576  u cu 576  h ch 576
+b X 3072  h N 3072  h R 3072  b x15 192  h R16 192  b nd 384  f ZS 1024  f z16 16  f yl 64  u lst 192  h mf 192  h mt 192
+u mu 192  b Br 768  b AG 1152  b ge 3072  b eb 192  b Fb 192  f v1 204  f v2 204  f dtf 204  f DT 204  b T1 204  h Rh 204  u LG 36
+u LL 72  f sv 192  f nv 384  b uf 192  b cum 192  f uy 192  u ul 12  f SW0 512  f SW1 512  f RC0 64  f RC1 64
+u L0u 60  f duf 192  f DU 192  b O2 192  b CTa 64  b CTb 64  b CZ 192  b ones 192  b J 128  b TH 192
+b OBa 160  b OB 160  b OB16 128  b Sb 128  b Wb 160  b Zb 160  b Yb 160  b Iw 160  b Iw0 160  b Iw1 160  b In 128
+b In8 128  b Tri 128  b T16 128  b Mn 128  f EL 256  f NL 256  f YL 256""".split()
 SCRATCH = {BUFS[k + 1]: ("sbuf", [128, int(BUFS[k + 2])], TYPES[BUFS[k]]) for k in range(0, len(BUFS), 3)}
 SCRATCH["raw"] = ("sbuf", [128, 2, 128], "int32")
 SCRATCH["occf"] = ("sbuf", [128, 2, 128], "float32")
 SCRATCH["r16"] = ("sbuf", [128, 8, 32], "float16")
-SCRATCH["E2"] = ("sbuf", [128, 12, 192], "bfloat16")
+SCRATCH["E2"] = ("sbuf", [128, 12, 204], "bfloat16")
+for _n, _t in (("selm", "float16"), ("nl", "bfloat16"), ("c16", "bfloat16")):
+    SCRATCH[_n] = ("sbuf", [128, 12, 17], _t)
 for _b in range(8):
     SCRATCH["PS%d" % _b] = ("psum", [128, 512], "float32")
-SEMAPHORES = ["qV", "qS", "qP", "qG", "arr0", "arr1", "snt"] + ["d%d" % i for i in range(16)]
+SEMAPHORES = ["qV", "qS", "qP", "qG", "arr0", "arr1", "snt"] + ["d%d" % i for i in range(18)]
 
 
 def tracker(g, T):
@@ -119,9 +122,12 @@ def rank_program(g, core, T, topo):
     arrive("arr0", NE, ["RC0"])
     arrive("arr1", NE, ["RC1"])
     SKW = ["SKa", "SKb", "SKz", "SKy"]
+    SCW = ["SCa", "SCb", "SCc", "SCd"]
     NUMW = ["NUM0", "NUM1"]
+    BR = ["Br%d" % k for k in range(max(VCALLS))]
     PS = [T["PS%d" % b] for b in range(8)]
     Ib, OB = T.Iw[:, 16:144], T.OB[:, 16:144]
+    win = T.SK[:, 0:NRD]
 
     def v(fn, R, W):
         op("V", fn, R, W)
@@ -150,49 +156,89 @@ def rank_program(g, core, T, topo):
     def pick(out, lhs, a, b):
         return [mm(out, lhs[:, 16 - i:144 - i], T.ch[:, a + i:b:16], i == 0, i == 15) for i in range(16)]
 
-    def shift(out, a, b):
-        return [mm(out, T.Zb[:, 16:144], T.CZ[:, 0:b - a], True, False), mm(out, T.Sb[:, :], T.ch[:, a:b], False, True)]
-
     def station(out, src, R, W):
         v(lambda: V.tensor_scalar(out, src, SC, 2048.0, A_.mult, A_.add), R, W)
 
     def cards16(a, b, key):
         v(lambda: V.tensor_scalar(T.ch[:, a:b], T.cd32[:, a:b], -2048.0, 1.0 / SC, A_.add, A_.mult), ["cd" + key], ["ch" + key])
 
+    def shift(t):
+        a, n = 192 * t, 192 if t else 128
+        p([mm(PS[6][:, 128:128 + n], T.Zb[:, 16:144], T.CZ[:, 0:n], True, False), mm(PS[6][:, 128:128 + n], T.Sb[:, :], T.ch[:, a:a + n], False, True)],
+          ["Zb", "Sb", "CZ", "ch1" if t else "ch0"], ["PS6"])
+
+    def ends(t):
+        a, b, c = (192, 384, 576) if t else (0, 128, 128)
+        p(pick(PS[4][:, 216:216 + (b - a) // 16], T.Yb, a, b) + pick(PS[4][:, 192:192 + (c - a) // 16], T.Zb, a, c), ["Zb", "Yb", "ch%d" % t], ["PS4"])
+
+    def shifted(t):
+        n = 192 if t else 128
+        station(T.cu[:, 192 * t:192 * t + n], PS[6][:, 128:128 + n], ["PS6"], ["cu%d" % t])
+
+    def firsts(t):
+        n = 24 if t else 8
+        station(T.L0u[:, 12 * t:12 * t + n], PS[4][:, 192:192 + n], ["PS4"], ["L0u%d" % t])
+
+    def lasts(t):
+        C = 12 if t else 8
+        station(T.L0u[:, 36 + 12 * t:36 + 12 * t + C], PS[4][:, 216:216 + C], ["PS4"], ["L15"])
+
     def own_needs(t):
-        v(lambda: V.tensor_scalar(T.N[:, 0:2048:16], T.nd[:, 128 * t:128 * t + 128], -1.0, 2048.0, A_.mult, A_.add), ["nd"], lanes("N", 0, 128))
+        v(lambda: V.tensor_scalar(T.N[:, 0:2048:16], T.nd[:, 128 * t:128 * t + 128], -1.0, 2048.0, A_.mult, A_.add), ["nd1" if t else "nd0"], lanes("N", 0, 128))
+
+    def covers(t):
+        C = 12 if t else 8
+        v(lambda: V.tensor_scalar(T.mf[:, 0:16 * C], T.cov[:, :].indirect(T.L0u[:, 12 * t:12 * t + C]), -2048.0, None, A_.add), ["cov", "L0u1" if t else "L0u0"], ["mf"])
+
+    def turn(t):
+        C = 12 if t else 8
+        v(lambda: V.transpose(T.mt[:, 0:16 * C], T.mf[:, 0:16 * C]), ["mf"], ["mt"])
+        p([mm(PS[3][:, c:16 * C:C], T["Iw%d" % (c % 2)][:, 16 + 16 * (c % 2 - h):144 + 16 * (c % 2 - h)], T.mt[:, 32 * (c // 2) + 16 * h:32 * (c // 2) + 16 * h + 16], h == 0, h == 1)
+           for c in range(C) for h in range(2)], ["Iw0", "Iw1", "mt"], ["PS3"])
+
+    def cover_lists(t):
+        L = 192 if t else 128
+        v(lambda: V.tensor_scalar(T.mu[:, 0:L], PS[3][:, 0:L], 2048.0, None, A_.add), ["PS3"], ["mu"])
 
     dma("Y", T.raw[:, 0, :], T.occ[0:8:2, :], [], ["raw0"])
     dma("S", T.raw[:, 1, :], T.occ[1:8:2, :], [], ["raw1"])
     dma("Y", T.skw[:, 0:2048], T.skill[:, :], [], ["skw"])
     dma("S", T.cd32[:, 0:128], T.cards[:, 0:128], [], ["cd0"])
-    dma("Y", T.nd[:, :], T.need[:, :], [], ["nd"])
+    dma("S", T.nd[:, 0:128], T.need[:, 0:128], [], ["nd0"])
     dma("Y", T.cd32[:, 192:576], T.cards[:, 192:576], [], ["cd1"])
     dma("Y", T.cov[:, :], T.cover[:, :], [], ["cov"])
+    dma("Y", T.nd[:, 128:384], T.need[:, 128:384], [], ["nd1"])
 
     v(lambda: V.memset(T.ones[:, :], 1.0), [], ["ones"])
     v(lambda: V.memset(T.z16[:, :], -200.0), [], ["z16"])
+    v(lambda: V.memset(T.c16[:, :, :], 16384.0), [], ["c16"])
     s(lambda: S.activation(T.SK[:, NST:NBG], T.z16[:, :], F_.Sigmoid), ["z16"], ["SKz"])
-    select("OBa", T.ones[:, :], "ones", [[-16, 10], [0, 16]], A_.is_ge, 0.0, 16, 1)
+    select("OBa", T.ones[:, 0:160], "ones", [[-16, 10], [0, 16]], A_.is_ge, 0.0, 16, 1)
     select("OB", T.OBa[:, :], "OBa", [[16, 10], [0, 16]], A_.is_ge, 0.0, -1, -1)
+    select("Iw", T.ones[:, 0:160], "ones", [[1, 160]], A_.is_equal, 0.0, -16, -1)
+    select("Tri", OB, "OB", [[1, 128]], A_.is_gt, 0.0, 0, -1)
+    for out, src, key, k in (("OB16", OB, "OB", 16384.0), ("In8", Ib, "Iw", -8192.0), ("In", Ib, "Iw", -1.0), ("T16", T.Tri[:, :], "Tri", 16384.0)):
+        s(lambda: S.activation(T[out][:, :], src, F_.Copy, scale=k), [key], [out])
+    for buf in ("SW0", "SW1"):
+        s(lambda: S.activation(T[buf][:, 0:64], T.ones[:, 0:64], F_.Copy, scale=2048.0), ["ones"], [buf])
     select("Sb", OB, "OB", [[1, 128]], A_.is_equal, 0.0, -1, -1)
     select("Wb", T.OB[:, :], "OB", [[0, 10], [1, 16]], A_.is_equal, 0.0, 0, 0)
     select("Zb", T.Wb[:, :], "Wb", [[1, 160]], A_.is_equal, 0.0, -16, -1)
     select("Yb", T.Wb[:, :], "Wb", [[1, 160]], A_.is_equal, 0.0, -1, -1)
-    select("Iw", T.ones[:, :], "ones", [[1, 160]], A_.is_equal, 0.0, -16, -1)
-    count_up(T.ZS[:, :], "ZS", [[0, 1280]], -200, 0)
-    select("Tri", OB, "OB", [[1, 128]], A_.is_gt, 0.0, 0, -1)
-    gp(lambda: g.iota(T.ia[:, :], [[1, 192]], 256, -1), [], ["ia"])
-    gp(lambda: g.iota(T.pmi[:, :], [[0, 1]], 0, 1), [], ["pmi"])
+    count_up(T.ZS[:, :], "ZS", [[0, 1024]], -200, 0)
+    select("J", T.ones[:, 0:128], "ones", [[0, 8], [1, 16]], A_.is_equal, 0.0, 0, -1)
+    select("O2", T.c16[:, :, 0:16], "c16", [[0, 12], [1, 16]], A_.not_equal, 8192.0, 0, -1)
     for h in range(2):
         select("Iw%d" % h, T.Iw[:, :], "Iw", [[0, 5], [1, 2], [0, 16]], A_.is_equal, 0.0, h - 1, 0)
     count_up(T.duf[:, :], "duf", [[16, 12], [0, 16]], 193, 1)
     select("DU", T.duf[:, :], "duf", [[0, 12], [1, 16]], A_.is_equal, 0.0, 0, 0)
-    count_up(T.SW0[:, 0:64], "SW0", [[0, 64]], 2048, 0)
-    count_up(T.dtf[:, :], "dtf", [[16, 12], [0, 16]], NRD + 1, 1)
-    select("DT", T.dtf[:, :], "dtf", [[0, 12], [1, 16]], A_.is_equal, -8192.0, 0, 0)
-    for buf, a, b, val in (("sv", 192, 384, 0), ("nv", 192, 384, 2047), ("SW1", 0, 64, 2048)):
-        count_up(T[buf][:, a:b], buf + "z" if a else buf, [[0, b - a]], val, 0)
+    select("TH", T.ones[:, :], "ones", [[0, 192]], A_.is_ge, -7.0, -KV, 1)
+    select("T1", T.c16[:, :, :], "c16", [[0, 12], [1, 17]], A_.not_equal, -32768.0, 0, -1)
+    count_up(T.dtf[:, :], "dtf", [[16, 12], [0, 17]], NRD + 1, 1)
+    select("DT", T.dtf[:, :], "dtf", [[0, 12], [1, 17]], A_.is_equal, -8192.0, 0, 0)
+    for buf in (T.selm, T.nl):
+        gp(lambda: g.affine_select(buf[:, :, 16], T.ones[:, 0:12], [[0, 12]], A_.is_gt, 0.0, 0, 0), ["ones"], ["pad"])
+    select("Mn", T.T16[:, :], "T16", [[1, 128]], A_.not_equal, -16384.0, 0, -1)
     v(lambda: V.memset(T.X[:, 0:1024], 2048.0), [], lanes("X", 0, 64))
     v(lambda: V.memset(T.SK[:, NBG:NRD], 8192.0), [], ["SKy"])
     v(lambda: V.memset(T.skw[:, 2048:2064], -1.0), [], ["skz"])
@@ -203,25 +249,25 @@ def rank_program(g, core, T, topo):
         v(lambda: V.transpose(T.tr[:, b:256:8], T.r16[:, b, :]), ["r160", "r161"], ["tr%d" % b])
     v(lambda: V.tensor_scalar(T.bof[:, :], T.tr[:, :], 1.0 + 0.5 / 2046.5, None, A_.mult), ["tr%d" % b for b in range(8)], ["bof"])
     s(lambda: S.activation(T.SK[:, 0:16 * KS], T.skw[:, :].indirect(T.bof[:, 0:KS]), F_.Relu, bias=EPS), ["skw", "skz", "bof"], ["SKa"])
-    cards16(0, 128, "0")
     v(lambda: V.memset(T.CZ[:, :], (NBG - 2048) / SC), [], ["CZ"])
-    p(shift(PS[3][:, 0:128], 0, 128) + pick(PS[3][:, 128:136], T.Yb, 0, 128) + pick(PS[3][:, 136:144], T.Zb, 0, 128), ["Sb", "Yb", "Zb", "CZ", "ch0"], ["PS3"])
+    cards16(0, 128, "0")
+    shift(0)
+    ends(0)
     v(lambda: V.tensor_copy(T.N[:, 1024:2048], T.X[:, 0:1024]), lanes("X", 0, 64), lanes("N", 64, 128))
+    v(lambda: V.memset(T.CTa[:, :], -32768.0), [], ["CTa"])
+    v(lambda: V.memset(T.CTb[:, :], NKP / SC), [], ["CTb"])
     v(lambda: V.tensor_scalar(T.SK[:, 16 * KS:NST], T.skw[:, :].indirect(T.bof[:, KS:256]), EPS, 0.0, A_.add, A_.max), ["skw", "skz", "bof"], ["SKb"])
-    station(T.cu[:, 0:128], PS[3][:, 0:128], ["PS3"], ["cu0"])
-    station(T.L0u[:, 36:44], PS[3][:, 128:136], ["PS3"], ["L15"])
-
-    win = T.SK[:, 0:NRD]
+    shifted(0)
 
     for t in range(3):
         last = t == 2
         L = 128 if t == 0 else 192
         C = L // 16
-        c0 = 192 * t
-        kc = "0" if t == 0 else "1"
+        H, D, M = L // 2, C // 2, 17 * C
+        c0, kc = 192 * t, "ch1" if t else "ch0"
+        LG, LA, LB = T.LG[:, 12 * t:12 * t + C], T.LL[:, 24 * t:24 * t + C], T.LL[:, 24 * t + C:24 * t + 2 * C]
         ch = CHUNKS[L]
-        vm, vn, vl = VLANES[L]
-        L0u, L0f = T.L0u[:, 12 * t:12 * t + C], T.L0f[:, 12 * t:12 * t + C]
+        cw, CW = (win, SKW) if t == 0 else (T.SKC[:, 0:NRD], SCW)
         B = T.X[:, 1:16 * L:16]
 
         def scan(k):
@@ -229,13 +275,13 @@ def rank_program(g, core, T, topo):
             Y = PS[k % 2][:, 0:b - a]
             v(lambda: V.tensor_tensor_scan(T.R[:, 16 * a:16 * b], T.X[:, 16 * a:16 * b], T.N[:, 16 * a:16 * b], 0.0, A_.add, A_.min),
               lanes("X", a, b) + lanes("N", a, b), lanes("R", a, b))
-            p([mm(Y, Ib, T.CTa[:, 0:b - a], True, False), mm(Y, Ib, T.CTb[:, 0:b - a], False, False)], ["Iw", "CT"], ["PS%d" % (k % 2)])
+            p([mm(Y, Ib, T.CTa[:, 0:b - a], True, False), mm(Y, Ib, T.CTb[:, 0:b - a], False, False)], ["Iw", "CTa", "CTb"], ["PS%d" % (k % 2)])
             p([mm(Y, T.Wb[:, 16 - i:144 - i], T.R[:, 16 * a + i:16 * b:16], False, False) for i in range(16)]
-              + [mm(Y, Ib, T.ch[:, c0 + a:c0 + b], False, True)], ["Wb", "ch" + kc] + lanes("R", a, b), ["PS%d" % (k % 2)])
+              + [mm(Y, Ib, T.ch[:, c0 + a:c0 + b], False, True)], ["Wb", kc] + lanes("R", a, b), ["PS%d" % (k % 2)])
 
         def empty(k, mid=None, end=None):
             a, b = ch[k], ch[k + 1]
-            v(lambda: V.tensor_tensor(T.yl[:, 0:b - a], PS[k % 2][:, 0:b - a], T.ch[:, c0 + a:c0 + b], A_.max), ["PS%d" % (k % 2), "ch" + kc], ["yl"])
+            v(lambda: V.tensor_tensor(T.yl[:, 0:b - a], PS[k % 2][:, 0:b - a], T.ch[:, c0 + a:c0 + b], A_.max), ["PS%d" % (k % 2), kc], ["yl"])
             if mid:
                 mid()
             station(T.lst[:, a:b], T.yl[:, 0:b - a], ["yl"], ["lst%d" % k])
@@ -244,102 +290,151 @@ def rank_program(g, core, T, topo):
             s(lambda: S.activation(T.SK[:, :].indirect(T.lst[:, a:b]), T.ZS[:, 0:16 * (b - a)], F_.Sigmoid), ["lst%d" % k, "ZS"], SKW)
 
         def vgather(a, b):
-            v(lambda: V.tensor_copy(T.X[:, 16 * a:16 * b], win.indirect(T.cu[:, c0 + a:c0 + b])), SKW + ["cu" + kc], lanes("X", a, b))
+            v(lambda: V.tensor_copy(T.X[:, 16 * a:16 * b], cw.indirect(T.cu[:, c0 + a:c0 + b])), CW + ["cu%d" % t], lanes("X", a, b))
 
-        vgather(0, ch[1])
-        s(lambda: S.activation(T.X[:, 16 * vl:16 * L], win.indirect(T.cu[:, c0 + vl:c0 + L]), F_.Copy), SKW + ["cu" + kc], lanes("X", vl, L))
-        if not last:
-            s(lambda: S.activation(T.x15[:, 0:L], win.indirect(T.L0u[:, 36 + 12 * t:36 + 12 * t + C]), F_.Copy), SKW + ["L15"], ["x15"])
-        if t == 0:
-            own_needs(0)
-            v(lambda: V.memset(T.CTa[:, :], -32768.0), [], ["CT"])
-            v(lambda: V.memset(T.CTb[:, :], NKP / SC), [], ["CT"])
-        scan(0)
-        vgather(ch[1], vm)
-        empty(0, lambda: vgather(vm, vn), lambda: vgather(vn, vl))
-        if t:
-            v(lambda: V.tensor_copy(T.N[:, 2048:3072:16], T["RC%d" % (t - 1)][:, :]), ["RC%d" % (t - 1)], lanes("N", 128, 192))
-        for k in range(1, len(ch) - 1):
-            scan(k)
-            if k > 1:
-                empty(k - 1)
-        v(lambda: V.tensor_scalar(T.eb[:, 0:L], B, EPS / 2, 65536.0, A_.is_lt, A_.mult), lanes("X", 0, L), ["eb"])
-        if t == 0:
-            station(L0u, PS[3][:, 136:144], ["PS3"], ["L0u"])
-            station(L0f, PS[3][:, 136:144], ["PS3"], ["L0f"])
-            cards16(192, 576, "1")
-        empty(len(ch) - 2)
-        if not last:
-            p([mm(PS[7][:, 0:L], Ib, T.x15[:, 0:L], True, False), mm(PS[7][:, 0:L], Ib, T.R[:, 15:16 * L:16], False, True)], ["Iw", "x15"] + lanes("R", 0, L), ["PS7"])
-        if t == 0:
-            p(shift(PS[3][:, 128:512], 192, 576) + pick(PS[3][:, 0:24], T.Zb, 192, 576) + pick(PS[3][:, 24:36], T.Yb, 192, 384), ["Zb", "Yb", "Sb", "CZ", "ch1"], ["PS3"])
-        for k in range(max(VCALLS)):
-            v(lambda: V.tensor_copy(T.Br[:, L * k:L * k + L], B), lanes("X", 0, L), ["Br%d" % k])
-        BR = ["Br%d" % k for k in range(max(VCALLS))]
-        if not last:
-            v(lambda: V.tensor_scalar(T.R16[:, 0:L], PS[7][:, 0:L], 2048.0, None, A_.min), ["PS7"], ["R16"])
-        p([mm(PS[2][:, 0:L], OB, T.R[:, 0:16 * L:16], True, False), mm(PS[2][:, 0:L], Ib, T.eb[:, 0:L], False, True)]
-          + ([] if last else [mm(PS[2][:, 192:192 + L], OB, T.R16[:, 0:L], True, True)]), ["OB", "Iw", "eb", "R16"] + lanes("R", 0, L), ["PS2"])
-        if t == 0:
-            v(lambda: V.tensor_scalar(T.ic[:, :], T.ia[:, :], 15, None, A_.bitwise_and), ["ia"], ["ic"])
-            v(lambda: V.tensor_scalar(T.pmj[:, :], T.pmi[:, :], 15, None, A_.bitwise_and), ["pmi"], ["pmj"])
-            for out, src, key, k in (("In8", Ib, "Iw", -8192.0), ("In", Ib, "Iw", -1.0), ("Ma", T.Tri[:, :], "Tri", 8192.0),
-                                     ("OB16", OB, "OB", 16384.0), ("T16", T.Tri[:, :], "Tri", 16384.0)):
-                v(lambda: V.tensor_scalar(T[out][:, :], src, k, None, A_.mult), [key], [out])
-            v(lambda: V.tensor_scalar(T.OD[:, :], T.ic[:, :], 0.0, 8192.0, A_.not_equal, A_.mult), ["ic"], ["OD"])
-            v(lambda: V.tensor_scalar(T.th0[:, :], T.pmj[:, :], float(KV), 8.0, A_.is_lt, A_.mult), ["pmj"], ["th0"])
-            v(lambda: V.tensor_copy(T.occf[:, :, :], T.raw[:, :, :]), ["raw0", "raw1"], ["occf"])
-            v(lambda: V.tensor_scalar(T.O2[:, :], T.OD[:, :], 8192.0, None, A_.add), ["OD"], ["O2"])
-            v(lambda: V.tensor_scalar(T.T1[:, :], T.OD[:, :], 2.0, -32768.0, A_.mult, A_.add), ["OD"], ["T1"])
-            v(lambda: V.tensor_scalar(T.thr[:, :], T.th0[:, :], -0.5, None, A_.add), ["th0"], ["thr"])
-            select("Mn", T.Ma[:, :], "Ma", [[1, 128]], A_.not_equal, -8192.0, 0, -1)
-        v(lambda: V.tensor_scalar(T.nl[:, 0:L], PS[2][:, 0:L], 32767.5, 16384.0, A_.is_ge, A_.mult), ["PS2"], ["nl"])
-        if not last:
-            v(lambda: V.tensor_scalar(T.uf[:, 0:L], PS[2][:, 192:192 + L], 32767.5, None, A_.is_lt), ["PS2"], ["uf"])
-        if t == 0:
-            station(T.cu[:, 192:576], PS[3][:, 128:512], ["PS3"], ["cu1"])
-            station(T.L0u[:, 12:36], PS[3][:, 0:24], ["PS3"], ["L0u"])
-            station(T.L0f[:, 12:36], PS[3][:, 0:24], ["PS3"], ["L0f"])
-            station(T.L0u[:, 48:60], PS[3][:, 24:36], ["PS3"], ["L15"])
-        if not last:
-            sw = T["SW%d" % t]
+        def sgather(a, b):
+            s(lambda: S.activation(T.X[:, 16 * a:16 * b], cw.indirect(T.cu[:, c0 + a:c0 + b]), F_.Copy), CW + ["cu%d" % t], lanes("X", a, b))
+
+        def was_empty():
+            v(lambda: V.tensor_scalar(T.eb[:, 0:L], B, EPS / 2, 65536.0, A_.is_lt, A_.mult), lanes("X", 0, L), ["eb"])
+
+        def first_dumps():
+            gp(lambda: g.affine_select(T.DT[:, 16:M:17], T.L0u[:, 12 * t:12 * t + C], [[0, C]], A_.is_equal, 0.0, 0, 0), ["L0u1" if t else "L0u0"], ["DT"])
+
+        def last_stations():
+            s(lambda: S.activation(T.x15[:, 0:L], cw.indirect(T.L0u[:, 36 + 12 * t:36 + 12 * t + C]), F_.Copy), CW + ["L15"], ["x15"])
+
+        def needs_copy(k, on_vector):
+            if on_vector:
+                v(lambda: V.tensor_copy(T.Br[:, L * k:L * k + L], B), lanes("X", 0, L), [BR[k]])
+            else:
+                gp(lambda: g.affine_select(T.Br[:, L * k:L * k + L], B, [[0, L]], A_.is_equal, 0.0, 0, 0), lanes("X", 0, L), [BR[k]])
+
+        def sums():
+            p([mm(PS[2][:, 0:L], OB, T.R[:, 0:16 * L:16], True, False), mm(PS[2][:, 0:L], Ib, T.eb[:, 0:L], False, True)], ["OB", "Iw", "eb"] + lanes("R", 0, L), ["PS2"])
+            if not last:
+                p([mm(PS[5][:, 0:L], Ib, T.x15[:, 0:L], True, False), mm(PS[5][:, 0:L], Ib, T.R[:, 15:16 * L:16], False, True)], ["Iw", "x15"] + lanes("R", 0, L), ["PS5"])
+
+        def not_lost():
+            v(lambda: V.tensor_scalar(T.nl[:, 0:C, 0:16], PS[2][:, 0:L], 32767.5, 16384.0, A_.is_ge, A_.mult), ["PS2"], ["nl"])
+
+        def rest():
+            v(lambda: V.tensor_scalar(T.R16[:, 0:L], PS[5][:, 0:L], 2048.0, None, A_.min), ["PS5"], ["R16"])
+            p(mm(PS[5][:, 0:L], OB, T.R16[:, 0:L], True, True), ["OB", "R16"], ["PS5"])
+
+        def unmet():
+            v(lambda: V.tensor_scalar(T.uf[:, 0:L], PS[5][:, 0:L], 32767.5, None, A_.is_lt), ["PS5"], ["uf"])
+
+        def slots():
             v(lambda: V.tensor_tensor_scan(T.cum[:, 0:L], T.uf[:, 0:L], T.uf[:, 0:L], 0.0, A_.add, A_.max), ["uf"], ["cum"])
-            p([mm(PS[7][:, 0:L], Ib, T.O2[:, 0:L], True, False), mm(PS[7][:, 0:L], T.In8[:, :], T.uf[:, 0:L], False, False),
-               mm(PS[7][:, 0:L], Ib, T.cum[:, 0:L], False, True)], ["Iw", "In8", "O2", "uf", "cum"], ["PS7"])
-        p(mm(PS[4][:, 0:L], T.In[:, :], T.nl[:, 0:L], True, False), ["In", "nl"], ["PS4"])
-        v(lambda: V.tensor_scalar(T.mf[:, 0:L], T.cov[:, :].indirect(L0u), -2048.0, None, A_.add), ["cov", "L0u"], ["mf"])
-        if not last:
-            own_needs(t + 1)
-        v(lambda: V.transpose(T.mt[:, 0:L], T.mf[:, 0:L]), ["mf"], ["mt"])
-        p([mm(PS[3][:, c:16 * C:C], T["Iw%d" % (c % 2)][:, 16 + 16 * (c % 2 - h):144 + 16 * (c % 2 - h)], T.mt[:, 32 * (c // 2) + 16 * h:32 * (c // 2) + 16 * h + 16], h == 0, h == 1)
-           for c in range(C) for h in range(2)], ["Iw0", "Iw1", "mt"], ["PS3"])
-        if not last:
-            v(lambda: V.tensor_tensor_scan(T.uy[:, 0:L], T.DU[:, 0:L], PS[7][:, 0:L], 0.0, A_.max, A_.min), ["DU", "PS7"], ["uy"])
-            if t == 0:
-                v(lambda: V.tensor_scalar(T.N[:, 2048:3072], T.X[:, 0:1024], 0.0, 2048.0, A_.mult, A_.add), lanes("X", 0, 64), lanes("N", 128, 192))
+            p([mm(PS[5][:, 0:L], T.J[:, :], T.O2[:, 0:L], True, False), mm(PS[5][:, 0:L], T.In8[:, :], T.uf[:, 0:L], False, False),
+               mm(PS[5][:, 0:L], Ib, T.cum[:, 0:L], False, True)], ["Iw", "J", "In8", "O2", "uf", "cum"], ["PS5"])
+
+        def slot_list(mid):
+            v(lambda: V.tensor_tensor_scan(T.uy[:, 0:L], T.DU[:, 0:L], PS[5][:, 0:L], 0.0, A_.max, A_.min), ["DU", "PS5"], ["uy"])
+            mid()
             v(lambda: V.tensor_scalar(T.ul[:, 0:C], T.uy[:, 15:L:16], -1.0, None, A_.add), ["uy"], ["ul"])
-        v(lambda: V.tensor_scalar(T.mu[:, 0:L], PS[3][:, 0:L], 2048.0, None, A_.add), ["PS3"], ["mu"])
-        if not last:
+
+        def hand_on():
+            sw = T["SW%d" % t]
             v(lambda: V.tensor_copy(sw[:, :].indirect(T.ul[:, 0:C]), T.R16[:, 0:L]), ["ul", "R16"], ["SW%d" % t])
+
+        def send():
+            sw = T["SW%d" % t]
             before("G", ["SW%d" % t], [])
             rid, pid, _se = topo.addr(nxt)
             em = sum(1 << e for e in topo.engines(core, nxt)[:NE])
             g.remote_dma(T["RC%d" % t][:, :], sw[:, 0:64], T.sem["arr%d" % t], T.sem.snt, pid, rid, em)
+
+        def numbers(r):
+            n = 12 if r else 8
+            v(lambda: V.tensor_copy(T.nv[:, 0:16 * n], T.NUM[:, 0:NRD].indirect(T.LG[:, 12 * r:12 * r + n])), NUMW + ["LG"], ["nv"])
+
+        def moved(r):
+            n = 12 if r else 8
+            v(lambda: V.tensor_copy(T.NUM[:, :].indirect(T.LL[:, 24 * r:24 * r + n]), T.nv[:, 0:16 * n]), ["LLa", "nv"], NUMW)
+
+        vgather(0, ch[1])
         if t == 0:
-            count_up(T.NUM[:, 0:NRD], "NUM", [[0, NRD]], 2047, 0)
-            dma("Y", T.NUM[0:128:32, 0:NST], T.occf[:, 0, :], ["occf", "NUM"], ["NUM0"])
-            dma("Y", T.NUM[16:128:32, 0:NST], T.occf[:, 1, :], ["occf", "NUM"], ["NUM1"])
+            vm, vl = VLANES
+            sgather(ch[1], ch[2])
+            sgather(vl, L)
+            lasts(0)
+            last_stations()
+            own_needs(0)
+            scan(0)
+            vgather(ch[2], vm)
+            scan(1)
+            empty(0, None, lambda: vgather(vm, vl))
+            empty(1, lambda: firsts(0))
+            scan(2)
+            was_empty()
+            sums()
+            cards16(192, 576, "1")
+            shift(1)
+            dma("Y", T.N[:, 2048:3072], T.N[:, 0:1024], lanes("N", 0, 64), lanes("N", 128, 192))
+            empty(2, lambda: needs_copy(0, True))
+            needs_copy(1, True)
+            rest()
+            not_lost()
+            needs_copy(2, True)
+            unmet()
+            slots()
+            ends(1)
+            covers(0)
+            slot_list(lambda: turn(0))
+            hand_on()
+            cover_lists(0)
+            firsts(1)
+            lasts(1)
         else:
-            Lb = 128 if t == 1 else 192
-            if t == 1:
-                v(lambda: V.tensor_copy(T.nv[:, 64:192], T.NUM[:, 0:NRD].indirect(T.LG[:, 0:8])), NUMW + ["LG"], ["nv"])
-            v(lambda: V.tensor_copy(T.NUM[:, :].indirect(T.LL[:, 0:Lb // 16]), T.nv[:, 192 - Lb:192]), ["LLa", "nv"], NUMW)
-        if last:
-            dma("Y", T.NL[:, :], T.NUM[0:128:16, 0:NST], NUMW, ["NL"])
-            dma("Y", T.EL[:, :], T.SK[0:128:16, 0:NST], SKW, ["EL"])
-        p(mm(PS[5][:, 0:L], Ib, T.mf[:, 0:L], True, False), ["Iw", "mf"], ["PS5"])
-        p(mm(PS[6][:, 0:L], Ib, T.T1[:, 0:L], True, False), ["Iw", "T1"], ["PS6"])
-        p([mm(PS[7][:, 0:L], Ib, T.T1[:, 0:L], True, False), mm(PS[7][:, 0:L], Ib, T.nl[:, 0:L], False, False)], ["Iw", "T1", "nl"], ["PS7"])
+            sgather(ch[1], ch[2])
+            sgather(ch[2], SLANES)
+            if not last:
+                last_stations()
+            scan(0)
+            covers(t)
+            scan(1)
+            empty(0, lambda: turn(t))
+            first_dumps()
+            vgather(SLANES + 8, ch[3])
+            empty(1, None, lambda: vgather(SLANES, SLANES + 8))
+            scan(2)
+            vgather(ch[3], VG)
+            empty(2, lambda: cover_lists(t), lambda: vgather(VG, L))
+            v(lambda: V.tensor_copy(T.N[:, 2048:3072:16], T["RC%d" % (t - 1)][:, :]), ["RC%d" % (t - 1)], lanes("N", 128, 192))
+            scan(3)
+            for k in range(len(BR)):
+                needs_copy(k, False)
+            if not last:
+                count_up(T.NUM[:, 0:NRD // 2], "NUM", [[0, NRD // 2]], 2047, 0)
+            was_empty()
+            if last:
+                numbers(0)
+                sums()
+                empty(3, lambda: moved(0))
+                not_lost()
+                numbers(1)
+                moved(1)
+                dma("Y", T.NL[:, :], T.NUM[0:128:16, 0:NST], NUMW, ["NL"])
+                dma("Y", T.EL[:, :], T.SK[0:128:16, 0:NST], SKW, ["EL"])
+            else:
+                sums()
+                shift(2)
+                empty(3)
+                rest()
+                not_lost()
+                unmet()
+                slots()
+                slot_list(lambda: None)
+                hand_on()
+        DB = [0, 1, 3]
+        p([mm(PS[4][:, 0:L], T.J[:, :], T.TH[:, 0:L], True, False), mm(PS[4][:, 0:L], T.In[:, :], T.nl[:, 0:C, 0:16], False, False)], ["J", "TH", "In", "nl"], ["PS4"])
+        for k in range(3):
+            p(mm(PS[DB[k]][:, 0:2 * L], T.In[:, :], T.Br[:, 0:2 * L], True, False), ["In"] + BR, ["PS%d" % DB[k]])
+        p(mm(PS[2][:, 0:H], Ib, T.mf[:, H:L], True, False), ["Iw", "mf"], ["PS2"])
+        p([mm(PS[7][:, 0:M], T.J[:, :], T.T1[:, 0:M], True, False), mm(PS[7][:, 0:M], Ib, T.nl[:, 0:C, :], False, False)], ["Iw", "J", "T1", "nl", "pad"], ["PS7"])
+        p(mm(PS[5][:, 0:H], Ib, T.mf[:, 0:H], True, False), ["Iw", "mf"], ["PS5"])
         done = []
 
         def count(cs):
@@ -354,71 +449,87 @@ def rank_program(g, core, T, topo):
               SKW + ["mu"] + BR, ["ge%d" % i for i in range(a, b)])
             return range(a, b)
 
-        def sgather(k):
-            i, n = KV + sum(SCALLS[:k]), SCALLS[k]
-            s(lambda: S.activation(T.AG[:, 2 * L * k:2 * L * k + n * L], win.indirect(T.mu[:, C * i:C * (i + n)]), F_.Copy), SKW + ["mu"], ["AG%d" % k])
+        def scall(a, b):
+            s(lambda: S.activation(T.AG[:, L * a:L * b], win.indirect(T.mu[:, C * (KV + a):C * (KV + b)]), F_.Copy), SKW + ["mu"], ["AG%d" % j for j in range(a, b)])
 
         def sdiff(k):
-            D, n = PS[k % 2][:, 0:SCALLS[k] * L], SCALLS[k]
-            p([mm(D, T.In[:, :], T.Br[:, 0:n * L], True, False), mm(D, Ib, T.AG[:, 2 * L * k:2 * L * k + n * L], False, True)],
-              ["Iw", "In", "AG%d" % k] + BR, ["PS%d" % (k % 2)])
+            p(mm(PS[DB[k]][:, 0:2 * L], Ib, T.AG[:, 2 * L * k:2 * L * k + 2 * L], False, True), ["Iw", "AG%d" % (2 * k), "AG%d" % (2 * k + 1)], ["PS%d" % DB[k]])
 
         def ssign(k):
-            i, n = KV + sum(SCALLS[:k]), SCALLS[k]
-            s(lambda: S.activation(T.ge[:, L * i:L * (i + n)], PS[k % 2][:, 0:n * L], F_.Sign, bias=EPS / 2), ["PS%d" % (k % 2)], ["ge%d" % j for j in range(i, i + n)])
-            return range(i, i + n)
+            i = KV + 2 * k
+            s(lambda: S.activation(T.ge[:, L * i:L * i + 2 * L], PS[DB[k]][:, 0:2 * L], F_.Sign, bias=EPS / 2), ["PS%d" % DB[k]], ["ge%d" % i, "ge%d" % (i + 1)])
+            return [i, i + 1]
 
-        sgather(0)
-        va = vcall(0)
-        sdiff(0)
-        sgather(1)
-        sa = ssign(0)
-        vb = vcall(1)
-        sdiff(1)
-        count(va)
-        sgather(2)
-        count(sa)
-        sb = ssign(1)
-        vc = vcall(2)
-        sdiff(2)
-        count(vb)
-        sc = ssign(2)
-        count(sb)
-        vd = vcall(3)
-        count(vc)
-        count(sc)
-        count(vd)
-        if last:
-            s(lambda: S.activation(PS[2][:, 0:256], T.EL[:, :], F_.Relu, bias=2047.0, scale=-(2.0 ** 60)), ["EL"], ["PS2"])
-        v(lambda: V.tensor_scalar(T.Fb[:, 0:L], PS[4][:, 0:L], T.thr[:, 0:1], None, A_.is_ge), ["PS4", "thr"], ["Fb"])
-        p(mm(PS[5][:, 0:L], T.Mn[:, :], T.Fb[:, 0:L], False, True), ["Mn", "Fb"], ["PS5"])
-        v(lambda: V.tensor_scalar(T.selm[:, 0:L], PS[5][:, 0:L], 8192.0, 2048.0, A_.add, A_.min), ["PS5"], ["selm"])
-        p(mm(PS[6][:, 0:L], OB, T.selm[:, 0:L], False, True), ["OB", "selm"], ["PS6"])
-        p(mm(PS[0][:, 0:L], OB, T.selm[:, 0:L], True, True), ["OB", "selm"], ["PS0"])
-        p(mm(PS[7][:, 0:L], OB, T.selm[:, 0:L], False, False), ["OB", "selm"], ["PS7"])
-        if last:
-            v(lambda: V.tensor_tensor(T.YL[:, :], PS[2][:, 0:256], T.NL[:, :], A_.max), ["NL", "PS2"], ["YL"])
-            dma("Y", T.NF[0:128:16, 0:NST], T.YL[:, :], ["YL"], ["NF"])
-        v(lambda: V.tensor_tensor_scan(T.v1[:, 0:L], T.DT[:, 0:L], PS[6][:, 0:L], 0.0, A_.max, A_.min), ["DT", "PS6"], ["v1"])
-        s(lambda: S.activation(T.Rh[:, 0:L], PS[0][:, 0:L], F_.Copy, bias=-30720.0), ["PS0"], ["Rh"])
-        for c in range(C):
-            v(lambda: V.tensor_scalar(T.E2[:, c, 0:L - 16 * c], T.Rh[:, 16 * c:L], -2048.0, T.v1[:, 16 * c + 15:16 * c + 16], A_.add, A_.is_equal), ["Rh", "v1"], ["E%d" % c])
-            if c < C - 1:
-                p(mm(PS[7][:, 16 * c + 16:L], T.OB16[:, :], T.E2[:, c, 16:L - 16 * c], False, False), ["OB16", "E%d" % c], [])
-            if c == 1:
-                v(lambda: V.tensor_scalar(T.LG[:, 0:C], T.v1[:, 15:L:16], float(NST), None, A_.add), ["v1"], ["LG"])
-                if not last:
-                    s(lambda: S.activation(T.sv[:, 192 - L:192], win.indirect(T.LG[:, 0:C]), F_.Copy), SKW + ["LG"], ["sv"])
-                if t:
-                    s(lambda: S.activation(T.nv[:, 0:192], T.NUM[:, 0:NRD].indirect(T.LG[:, 0:C]), F_.Copy), NUMW + ["LG"], ["nv"])
-        p(mm(PS[7][:, 0:L], T.T16[:, :], T.E2[:, 0:C, 0:16], False, True), ["T16"] + ["E%d" % c for c in range(C)], ["PS7"])
-        v(lambda: V.tensor_tensor_scan(T.v2[:, 0:L], T.DT[:, 0:L], PS[7][:, 0:L], 0.0, A_.max, A_.min), ["DT", "PS7"], ["v2"])
-        v(lambda: V.tensor_tensor(T.la[:, 0:C], T.v2[:, 15:L:16], L0f, A_.max), ["v2", "L0f"], ["la"])
-        v(lambda: V.tensor_scalar(T.LL[:, C:2 * C], T.v2[:, 15:L:16], float(NST), None, A_.add), ["v2"], ["LLb"])
-        v(lambda: V.tensor_copy(T.LL[:, 0:C], T.la[:, 0:C]), ["la"], ["LLa"])
         if not last:
-            v(lambda: V.tensor_copy(T.SK[:, :].indirect(T.LL[:, 0:2 * C]), T.sv[:, 192 - L:192 + L]), ["LLa", "LLb", "sv", "svz"], SKW)
-    v(lambda: V.tensor_copy(T.NF[:, :].indirect(T.LL[:, 0:24]), T.nv[:, :]), ["LLa", "LLb", "nv", "nvz"], ["NF"])
-    dma("Y", T.y[:, :], T.NF[0:128:16, 0:NST], ["NF"], ["y"])
+            dma("Y", T.SKC[:, 0:CP[t][0]], T.SK[:, 0:CP[t][0]], SKW, ["SCa"])
+            a, b = CP[t][0], CP[t][1]
+            if t == 0:
+                first_dumps()
+            gp(lambda: g.affine_select(T.SKC[:, a:b], T.SK[:, a:b], [[0, b - a]], A_.is_equal, 0.0, 0, 0), SKW, ["SCd"])
+            send()
+        if t == 0:
+            for h in range(2):
+                gp(lambda: g.affine_select(T.occf[:, h, :], T.r16[:, :, 16 * h:16 * h + 16], [[0, 128]], A_.is_equal, 0.0, 0, 0), ["r16%d" % h], ["occf"])
+        if t == 1:
+            count_up(T.nv[:, 192:384], "nvz", [[0, 192]], 2047, 0)
+            count_up(T.NUM[:, NRD // 2:NRD], "NUM", [[0, NRD // 2]], 2047, 0)
+            dma("Y", T.NUM[0:128:32, 0:NST], T.occf[:, 0, :], ["occf", "NUM"], ["NUM0"])
+            dma("Y", T.NUM[16:128:32, 0:NST], T.occf[:, 1, :], ["occf", "NUM"], ["NUM1"])
+        scall(0, 4)
+        scall(4, 6)
+        vc = [vcall(k) for k in range(4)]
+        if last:
+            v(lambda: V.tensor_scalar(PS[6][:, 128:384], T.EL[:, :], EPS / 2, 2047.0, A_.is_lt, A_.mult), ["EL"], ["PS6"])
+            v(lambda: V.tensor_tensor(T.YL[:, :], PS[6][:, 128:384], T.NL[:, :], A_.max), ["NL", "PS6"], ["YL"])
+            dma("Y", T.SKC[0:128:16, 0:NST], T.YL[:, :], ["YL"], SCW)
+        else:
+            shifted(t + 1)
+            own_needs(t + 1)
+        sdiff(0)
+        sdiff(1)
+        count(vc[0])
+        sdiff(2)
+        sc = [ssign(k) for k in range(3)]
+        for cs in (vc[1], sc[0], sc[1], vc[2], sc[2], vc[3]):
+            count(cs)
+        if not last:
+            s(lambda: S.activation(T.SKC[:, CP[t][1]:CP[t][2]], T.SK[:, CP[t][1]:CP[t][2]], F_.Copy), SKW, ["SCb"])
+        for k in (6, 3):
+            p(mm(PS[k][:, 0:M // 2], T.J[:, :], T.T1[:, 0:M // 2], True, False), ["J", "T1"], ["PS%d" % k])
+        halves = ((0, 5, 6, 0), (H, 2, 3, 1))
+        for a, z, _k, _r in halves:
+            v(lambda: V.tensor_scalar(T.Fb[:, a:a + H], PS[4][:, a:a + H], 0.5, None, A_.is_ge), ["PS4"], ["Fb%d" % a])
+            p(mm(PS[z][:, 0:H], T.Mn[:, :], T.Fb[:, a:a + H], False, True), ["Mn", "Fb%d" % a], ["PS%d" % z])
+        for a, z, k, r in halves:
+            c, m = a // 16, 17 * a // 16
+            v(lambda: V.tensor_scalar(T.selm[:, c:c + D, 0:16], PS[z][:, 0:H], 16384.0, 2048.0, A_.add, A_.min), ["PS%d" % z], ["selm%d" % a])
+            p(mm(PS[r][:, 0:M // 2], OB, T.selm[:, c:c + D, :], True, True), ["OB", "pad", "selm%d" % a], ["PS%d" % r])
+            p(mm(PS[k][:, 0:M // 2], OB, T.selm[:, c:c + D, :], False, True), ["OB", "selm%d" % a], ["PS%d" % k])
+            s(lambda: S.activation(T.Rh[:, m:m + M // 2], PS[r][:, 0:M // 2], F_.Copy, bias=-30720.0), ["PS%d" % r], ["Rh%d" % a])
+        p(mm(PS[7][:, 0:M], OB, T.selm[:, 0:C, :], False, False), ["OB", "selm0", "selm%d" % H], ["PS7"])
+        for a, z, k, r in halves:
+            m = 17 * a // 16
+            v(lambda: V.tensor_tensor_scan(T.v1[:, m:m + M // 2], T.DT[:, m:m + M // 2], PS[k][:, 0:M // 2], 0.0, A_.max, A_.min), ["DT", "PS%d" % k], ["v1%d" % a])
+        if not last:
+            s(lambda: S.activation(T.SKC[:, CP[t][2]:NRD], T.SK[:, CP[t][2]:NRD], F_.Copy), SKW, ["SCc"])
+        for c in range(C):
+            v(lambda: V.tensor_scalar(T.E2[:, c, 0:M - 17 * c], T.Rh[:, 17 * c:M], -2048.0, T.v1[:, 17 * c + 15:17 * c + 16], A_.add, A_.is_equal),
+              ["Rh0", "Rh%d" % H, "v10" if c < D else "v1%d" % H], ["E%d" % c])
+            p(([mm(PS[7][:, 17 * c + 17:M], T.OB16[:, :], T.E2[:, c, 17:M - 17 * c], False, False)] if c < C - 1 else [])
+              + [mm(PS[7][:, 17 * c:17 * c + 16], T.T16[:, :], T.E2[:, c, 0:16], False, c == C - 1)], ["OB16", "T16", "E%d" % c], ["PS7"] if c == C - 1 else [])
+        v(lambda: V.tensor_scalar(LG, T.v1[:, 15:M:17], float(NST), None, A_.add), ["v10", "v1%d" % H], ["LG"])
+        if not last:
+            s(lambda: S.activation(T.sv[:, 0:L], win.indirect(LG), F_.Copy), SKW + ["LG"], ["sv"])
+        else:
+            s(lambda: S.activation(T.nv[:, 0:192], T.NUM[:, 0:NRD].indirect(LG), F_.Copy), NUMW + ["LG"], ["nv"])
+        v(lambda: V.tensor_tensor_scan(T.v2[:, 0:M], T.DT[:, 0:M], PS[7][:, 0:M], 0.0, A_.max, A_.min), ["DT", "PS7"], ["v2"])
+        v(lambda: V.tensor_scalar(LB, T.v2[:, 15:M:17], float(NST), None, A_.add), ["v2"], ["LLb"])
+        v(lambda: V.tensor_copy(LA, T.v2[:, 16:M:17]), ["v2"], ["LLa"])
+        if not last:
+            for zw, zk, vw, vk in ((T.SKC, SCW, T.SK, SKW), (T.SK, SKW, T.SKC, SCW)):
+                s(lambda: S.activation(zw[:, :].indirect(LB), T.ZS[:, 0:L], F_.Sigmoid), ["LLb", "ZS"], zk)
+                v(lambda: V.tensor_copy(vw[:, :].indirect(LA), T.sv[:, 0:L]), ["LLa", "sv"], vk)
+    v(lambda: V.tensor_copy(T.SKC[:, :].indirect(T.LL[:, 48:72]), T.nv[:, :]), ["LLa", "LLb", "nv", "nvz"], SCW)
+    dma("Y", T.y[:, :], T.SKC[0:128:16, 0:NST], SCW, ["y"])
     g.wait_ge(T.sem.snt, 2 * NE)
     finish()

from concourse.mybir import dt, AluOpType as A_, ActivationFunctionType as F_

EPS = 2.0 ** -40
NST = 4096
NBG = NST + 16
NRD = NST + 32
NKP = 4608
SC = 8192.0
VCALLS = [3, 3, 3, 1]
KV = sum(VCALLS)
CHUNKS = {128: [0, 24, 64, 128], 192: [0, 24, 64, 128, 192]}
VLANES = (76, 88)
SLANES = 104
VG = 156
CP = ((1408, 2304, 3200), (1664, 2304, 3200))
KS = 136

TYPES = {"b": "bfloat16", "f": "float32", "i": "int32", "u": "uint16", "h": "float16"}
BUFS = """b skw 2064  h tr 256  u bof 256  f SK 8704  f NUM 4448  f SKC 8544  i cov 4096  i cd32 576  u cu 576  h ch 576
b X 3072  h N 3072  h R 3072  b x15 192  h R16 192  b nd 384  f ZS 1024  f z16 16  f yl 64  u lst 192  h mf 192  h mt 192
u mu 192  b Br 768  b AG 1152  b ge 3072  b eb 192  b Fb 192  f v1 204  f v2 204  f dtf 204  f DT 204  b T1 204  h Rh 204  u LG 36
u LL 72  f sv 192  f nv 384  b uf 192  b cum 192  f uy 192  u ul 12  f SW0 512  f SW1 512  f RC0 64  f RC1 64
u L0u 60  f duf 192  f DU 192  b O2 192  b CTa 64  b CTb 64  b CZ 192  b ones 192  b J 128  b TH 192
b OBa 160  b OB 160  b OB16 128  b Sb 128  b Wb 160  b Zb 160  b Yb 160  b Iw 160  b Iw0 160  b Iw1 160  b In 128
b In8 128  b Tri 128  b T16 128  b Mn 128  f EL 256  f NL 256  f YL 256""".split()
SCRATCH = {BUFS[k + 1]: ("sbuf", [128, int(BUFS[k + 2])], TYPES[BUFS[k]]) for k in range(0, len(BUFS), 3)}
SCRATCH["raw"] = ("sbuf", [128, 2, 128], "int32")
SCRATCH["occf"] = ("sbuf", [128, 2, 128], "float32")
SCRATCH["r16"] = ("sbuf", [128, 8, 32], "float16")
SCRATCH["E2"] = ("sbuf", [128, 12, 204], "bfloat16")
for _n, _t in (("selm", "float16"), ("nl", "bfloat16"), ("c16", "bfloat16")):
    SCRATCH[_n] = ("sbuf", [128, 12, 17], _t)
for _b in range(8):
    SCRATCH["PS%d" % _b] = ("psum", [128, 512], "float32")
SEMAPHORES = ["qV", "qS", "qP", "qG", "arr0", "arr1", "snt"] + ["d%d" % i for i in range(18)]


def tracker(g, T):
    eng = {"V": g.vector, "S": g.scalar, "P": g.tensor, "G": g, "Y": g.sync}
    num = {"V": 0, "S": 0, "P": 0, "G": 0, "D": 0}
    know = {q: {} for q in eng}
    snaps, lastw, readers = {}, {}, {}

    def semof(p):
        return T.sem["q" + p] if p in "VSPG" else T.sem[p]

    def waits(q, deps):
        best = {}
        for p, n in deps:
            if know[q].get(p, 0) < n:
                best[p] = max(n, best.get(p, 0))
        items = list(best.items())
        for p, n in items:
            if any(p2 != p and snaps[(p2, n2)].get(p, 0) >= n for p2, n2 in items):
                continue
            eng[q].wait_ge(semof(p), n)
        k = know[q]
        for p, n in items:
            for a, b in snaps[(p, n)].items():
                k[a] = max(k.get(a, 0), b)
            k[p] = max(k.get(p, 0), n)

    def before(q, R, W):
        d = [lastw[r] for r in R if r in lastw]
        for r in R:
            if r[:2] == "PS":
                d += [x for x in readers.get(r, []) if x[0] != q]
        for w in W:
            if w in lastw and not (q == "P" and lastw[w][0] == "P"):
                d.append(lastw[w])
            d += readers.get(w, [])
        waits(q, d)

    def note(tok, R, W):
        for r in R:
            readers.setdefault(r, []).append(tok)
        for w in W:
            lastw[w] = tok
            readers[w] = []

    def op(q, fns, R, W):
        before(q, R, W)
        fns = fns if isinstance(fns, list) else [fns]
        for f in fns[:-1]:
            f()
        num[q] += 1
        fns[-1]().then_inc(semof(q), 1)
        tok = (q, num[q])
        snaps[tok] = dict(know[q])
        note(tok, R, W)

    def dma(q, out, in_, R, W):
        before(q, R, W)
        p = "d%d" % num["D"]
        num["D"] += 1
        eng[q].dma_start(out, in_).then_inc(T.sem[p], 16)
        tok = (p, 16)
        snaps[tok] = dict(know[q])
        note(tok, R, W)

    def arrive(p, n, W):
        snaps[(p, n)] = {}
        note((p, n), [], W)

    def finish():
        for p, n in [(q, num[q]) for q in "VSPG" if num[q]] + [("d%d" % i, 16) for i in range(num["D"])]:
            if know["G"].get(p, 0) < n:
                g.wait_ge(semof(p), n)

    return op, dma, arrive, before, finish


def rank_program(g, core, T, topo):
    rank = T.rank_of(core)
    if rank is None:
        return
    cores = list(T.cores)
    nxt = cores[(rank + 1) % len(cores)]
    NE = 4
    V, S, P = g.vector, g.scalar, g.tensor
    op, dma, arrive, before, finish = tracker(g, T)
    arrive("arr0", NE, ["RC0"])
    arrive("arr1", NE, ["RC1"])
    SKW = ["SKa", "SKb", "SKz", "SKy"]
    SCW = ["SCa", "SCb", "SCc", "SCd"]
    NUMW = ["NUM0", "NUM1"]
    BR = ["Br%d" % k for k in range(max(VCALLS))]
    PS = [T["PS%d" % b] for b in range(8)]
    Ib, OB = T.Iw[:, 16:144], T.OB[:, 16:144]
    win = T.SK[:, 0:NRD]

    def v(fn, R, W):
        op("V", fn, R, W)

    def s(fn, R, W):
        op("S", fn, R, W)

    def p(fns, R, W):
        op("P", fns, R, W)

    def gp(fn, R, W):
        op("G", fn, R, W)

    def mm(out, l, r, a, b):
        return lambda: P.matmul(out, l, r, a, b)

    def lanes(key, a, b):
        return ["%s%d" % (key, k) for k in range(a // 8, (b + 7) // 8)]

    def select(out, src, key, pattern, cmp, fill, base, mult):
        gp(lambda: g.affine_select(T[out][:, :], src, pattern, cmp, fill, base, mult), [key], [out])

    def count_up(out, key, pattern, base, mult):
        gp(lambda: g.iota(out, pattern, base, mult, allow_small_or_imprecise_dtypes=True), [], [key])

    def pick(out, lhs, a, b):
        return [mm(out, lhs[:, 16 - i:144 - i], T.ch[:, a + i:b:16], i == 0, i == 15) for i in range(16)]

    def station(out, src, R, W):
        v(lambda: V.tensor_scalar(out, src, SC, 2048.0, A_.mult, A_.add), R, W)

    def cards16(a, b, key):
        v(lambda: V.tensor_scalar(T.ch[:, a:b], T.cd32[:, a:b], -2048.0, 1.0 / SC, A_.add, A_.mult), ["cd" + key], ["ch" + key])

    def shift(t):
        a, n = 192 * t, 192 if t else 128
        p([mm(PS[6][:, 128:128 + n], T.Zb[:, 16:144], T.CZ[:, 0:n], True, False), mm(PS[6][:, 128:128 + n], T.Sb[:, :], T.ch[:, a:a + n], False, True)],
          ["Zb", "Sb", "CZ", "ch1" if t else "ch0"], ["PS6"])

    def ends(t):
        a, b, c = (192, 384, 576) if t else (0, 128, 128)
        p(pick(PS[4][:, 216:216 + (b - a) // 16], T.Yb, a, b) + pick(PS[4][:, 192:192 + (c - a) // 16], T.Zb, a, c), ["Zb", "Yb", "ch%d" % t], ["PS4"])

    def shifted(t):
        n = 192 if t else 128
        station(T.cu[:, 192 * t:192 * t + n], PS[6][:, 128:128 + n], ["PS6"], ["cu%d" % t])

    def firsts(t):
        n = 24 if t else 8
        station(T.L0u[:, 12 * t:12 * t + n], PS[4][:, 192:192 + n], ["PS4"], ["L0u%d" % t])

    def lasts(t):
        C = 12 if t else 8
        station(T.L0u[:, 36 + 12 * t:36 + 12 * t + C], PS[4][:, 216:216 + C], ["PS4"], ["L15"])

    def own_needs(t):
        v(lambda: V.tensor_scalar(T.N[:, 0:2048:16], T.nd[:, 128 * t:128 * t + 128], -1.0, 2048.0, A_.mult, A_.add), ["nd1" if t else "nd0"], lanes("N", 0, 128))

    def covers(t):
        C = 12 if t else 8
        v(lambda: V.tensor_scalar(T.mf[:, 0:16 * C], T.cov[:, :].indirect(T.L0u[:, 12 * t:12 * t + C]), -2048.0, None, A_.add), ["cov", "L0u1" if t else "L0u0"], ["mf"])

    def turn(t):
        C = 12 if t else 8
        v(lambda: V.transpose(T.mt[:, 0:16 * C], T.mf[:, 0:16 * C]), ["mf"], ["mt"])
        p([mm(PS[3][:, c:16 * C:C], T["Iw%d" % (c % 2)][:, 16 + 16 * (c % 2 - h):144 + 16 * (c % 2 - h)], T.mt[:, 32 * (c // 2) + 16 * h:32 * (c // 2) + 16 * h + 16], h == 0, h == 1)
           for c in range(C) for h in range(2)], ["Iw0", "Iw1", "mt"], ["PS3"])

    def cover_lists(t):
        L = 192 if t else 128
        v(lambda: V.tensor_scalar(T.mu[:, 0:L], PS[3][:, 0:L], 2048.0, None, A_.add), ["PS3"], ["mu"])

    dma("Y", T.raw[:, 0, :], T.occ[0:8:2, :], [], ["raw0"])
    dma("S", T.raw[:, 1, :], T.occ[1:8:2, :], [], ["raw1"])
    dma("Y", T.skw[:, 0:2048], T.skill[:, :], [], ["skw"])
    dma("S", T.cd32[:, 0:128], T.cards[:, 0:128], [], ["cd0"])
    dma("S", T.nd[:, 0:128], T.need[:, 0:128], [], ["nd0"])
    dma("Y", T.cd32[:, 192:576], T.cards[:, 192:576], [], ["cd1"])
    dma("Y", T.cov[:, :], T.cover[:, :], [], ["cov"])
    dma("Y", T.nd[:, 128:384], T.need[:, 128:384], [], ["nd1"])

    v(lambda: V.memset(T.ones[:, :], 1.0), [], ["ones"])
    v(lambda: V.memset(T.z16[:, :], -200.0), [], ["z16"])
    v(lambda: V.memset(T.c16[:, :, :], 16384.0), [], ["c16"])
    s(lambda: S.activation(T.SK[:, NST:NBG], T.z16[:, :], F_.Sigmoid), ["z16"], ["SKz"])
    select("OBa", T.ones[:, 0:160], "ones", [[-16, 10], [0, 16]], A_.is_ge, 0.0, 16, 1)
    select("OB", T.OBa[:, :], "OBa", [[16, 10], [0, 16]], A_.is_ge, 0.0, -1, -1)
    select("Iw", T.ones[:, 0:160], "ones", [[1, 160]], A_.is_equal, 0.0, -16, -1)
    select("Tri", OB, "OB", [[1, 128]], A_.is_gt, 0.0, 0, -1)
    for out, src, key, k in (("OB16", OB, "OB", 16384.0), ("In8", Ib, "Iw", -8192.0), ("In", Ib, "Iw", -1.0), ("T16", T.Tri[:, :], "Tri", 16384.0)):
        s(lambda: S.activation(T[out][:, :], src, F_.Copy, scale=k), [key], [out])
    for buf in ("SW0", "SW1"):
        s(lambda: S.activation(T[buf][:, 0:64], T.ones[:, 0:64], F_.Copy, scale=2048.0), ["ones"], [buf])
    select("Sb", OB, "OB", [[1, 128]], A_.is_equal, 0.0, -1, -1)
    select("Wb", T.OB[:, :], "OB", [[0, 10], [1, 16]], A_.is_equal, 0.0, 0, 0)
    select("Zb", T.Wb[:, :], "Wb", [[1, 160]], A_.is_equal, 0.0, -16, -1)
    select("Yb", T.Wb[:, :], "Wb", [[1, 160]], A_.is_equal, 0.0, -1, -1)
    count_up(T.ZS[:, :], "ZS", [[0, 1024]], -200, 0)
    select("J", T.ones[:, 0:128], "ones", [[0, 8], [1, 16]], A_.is_equal, 0.0, 0, -1)
    select("O2", T.c16[:, :, 0:16], "c16", [[0, 12], [1, 16]], A_.not_equal, 8192.0, 0, -1)
    for h in range(2):
        select("Iw%d" % h, T.Iw[:, :], "Iw", [[0, 5], [1, 2], [0, 16]], A_.is_equal, 0.0, h - 1, 0)
    count_up(T.duf[:, :], "duf", [[16, 12], [0, 16]], 193, 1)
    select("DU", T.duf[:, :], "duf", [[0, 12], [1, 16]], A_.is_equal, 0.0, 0, 0)
    select("TH", T.ones[:, :], "ones", [[0, 192]], A_.is_ge, -7.0, -KV, 1)
    select("T1", T.c16[:, :, :], "c16", [[0, 12], [1, 17]], A_.not_equal, -32768.0, 0, -1)
    count_up(T.dtf[:, :], "dtf", [[16, 12], [0, 17]], NRD + 1, 1)
    select("DT", T.dtf[:, :], "dtf", [[0, 12], [1, 17]], A_.is_equal, -8192.0, 0, 0)
    for buf in (T.selm, T.nl):
        gp(lambda: g.affine_select(buf[:, :, 16], T.ones[:, 0:12], [[0, 12]], A_.is_gt, 0.0, 0, 0), ["ones"], ["pad"])
    select("Mn", T.T16[:, :], "T16", [[1, 128]], A_.not_equal, -16384.0, 0, -1)
    v(lambda: V.memset(T.X[:, 0:1024], 2048.0), [], lanes("X", 0, 64))
    v(lambda: V.memset(T.SK[:, NBG:NRD], 8192.0), [], ["SKy"])
    v(lambda: V.memset(T.skw[:, 2048:2064], -1.0), [], ["skz"])
    v(lambda: V.tensor_copy(T.N[:, 0:1024], T.X[:, 0:1024]), lanes("X", 0, 64), lanes("N", 0, 64))
    for h in range(2):
        v(lambda: V.tensor_copy(T.r16[:, :, 16 * h:16 * h + 16], T.raw[:, h, :]), ["raw%d" % h], ["r16%d" % h])
    for b in range(8):
        v(lambda: V.transpose(T.tr[:, b:256:8], T.r16[:, b, :]), ["r160", "r161"], ["tr%d" % b])
    v(lambda: V.tensor_scalar(T.bof[:, :], T.tr[:, :], 1.0 + 0.5 / 2046.5, None, A_.mult), ["tr%d" % b for b in range(8)], ["bof"])
    s(lambda: S.activation(T.SK[:, 0:16 * KS], T.skw[:, :].indirect(T.bof[:, 0:KS]), F_.Relu, bias=EPS), ["skw", "skz", "bof"], ["SKa"])
    v(lambda: V.memset(T.CZ[:, :], (NBG - 2048) / SC), [], ["CZ"])
    cards16(0, 128, "0")
    shift(0)
    ends(0)
    v(lambda: V.tensor_copy(T.N[:, 1024:2048], T.X[:, 0:1024]), lanes("X", 0, 64), lanes("N", 64, 128))
    v(lambda: V.memset(T.CTa[:, :], -32768.0), [], ["CTa"])
    v(lambda: V.memset(T.CTb[:, :], NKP / SC), [], ["CTb"])
    v(lambda: V.tensor_scalar(T.SK[:, 16 * KS:NST], T.skw[:, :].indirect(T.bof[:, KS:256]), EPS, 0.0, A_.add, A_.max), ["skw", "skz", "bof"], ["SKb"])
    shifted(0)

    for t in range(3):
        last = t == 2
        L = 128 if t == 0 else 192
        C = L // 16
        H, D, M = L // 2, C // 2, 17 * C
        c0, kc = 192 * t, "ch1" if t else "ch0"
        LG, LA, LB = T.LG[:, 12 * t:12 * t + C], T.LL[:, 24 * t:24 * t + C], T.LL[:, 24 * t + C:24 * t + 2 * C]
        ch = CHUNKS[L]
        cw, CW = (win, SKW) if t == 0 else (T.SKC[:, 0:NRD], SCW)
        B = T.X[:, 1:16 * L:16]

        def scan(k):
            a, b = ch[k], ch[k + 1]
            Y = PS[k % 2][:, 0:b - a]
            v(lambda: V.tensor_tensor_scan(T.R[:, 16 * a:16 * b], T.X[:, 16 * a:16 * b], T.N[:, 16 * a:16 * b], 0.0, A_.add, A_.min),
              lanes("X", a, b) + lanes("N", a, b), lanes("R", a, b))
            p([mm(Y, Ib, T.CTa[:, 0:b - a], True, False), mm(Y, Ib, T.CTb[:, 0:b - a], False, False)], ["Iw", "CTa", "CTb"], ["PS%d" % (k % 2)])
            p([mm(Y, T.Wb[:, 16 - i:144 - i], T.R[:, 16 * a + i:16 * b:16], False, False) for i in range(16)]
              + [mm(Y, Ib, T.ch[:, c0 + a:c0 + b], False, True)], ["Wb", kc] + lanes("R", a, b), ["PS%d" % (k % 2)])

        def empty(k, mid=None, end=None):
            a, b = ch[k], ch[k + 1]
            v(lambda: V.tensor_tensor(T.yl[:, 0:b - a], PS[k % 2][:, 0:b - a], T.ch[:, c0 + a:c0 + b], A_.max), ["PS%d" % (k % 2), kc], ["yl"])
            if mid:
                mid()
            station(T.lst[:, a:b], T.yl[:, 0:b - a], ["yl"], ["lst%d" % k])
            if end:
                end()
            s(lambda: S.activation(T.SK[:, :].indirect(T.lst[:, a:b]), T.ZS[:, 0:16 * (b - a)], F_.Sigmoid), ["lst%d" % k, "ZS"], SKW)

        def vgather(a, b):
            v(lambda: V.tensor_copy(T.X[:, 16 * a:16 * b], cw.indirect(T.cu[:, c0 + a:c0 + b])), CW + ["cu%d" % t], lanes("X", a, b))

        def sgather(a, b):
            s(lambda: S.activation(T.X[:, 16 * a:16 * b], cw.indirect(T.cu[:, c0 + a:c0 + b]), F_.Copy), CW + ["cu%d" % t], lanes("X", a, b))

        def was_empty():
            v(lambda: V.tensor_scalar(T.eb[:, 0:L], B, EPS / 2, 65536.0, A_.is_lt, A_.mult), lanes("X", 0, L), ["eb"])

        def first_dumps():
            gp(lambda: g.affine_select(T.DT[:, 16:M:17], T.L0u[:, 12 * t:12 * t + C], [[0, C]], A_.is_equal, 0.0, 0, 0), ["L0u1" if t else "L0u0"], ["DT"])

        def last_stations():
            s(lambda: S.activation(T.x15[:, 0:L], cw.indirect(T.L0u[:, 36 + 12 * t:36 + 12 * t + C]), F_.Copy), CW + ["L15"], ["x15"])

        def needs_copy(k, on_vector):
            if on_vector:
                v(lambda: V.tensor_copy(T.Br[:, L * k:L * k + L], B), lanes("X", 0, L), [BR[k]])
            else:
                gp(lambda: g.affine_select(T.Br[:, L * k:L * k + L], B, [[0, L]], A_.is_equal, 0.0, 0, 0), lanes("X", 0, L), [BR[k]])

        def sums():
            p([mm(PS[2][:, 0:L], OB, T.R[:, 0:16 * L:16], True, False), mm(PS[2][:, 0:L], Ib, T.eb[:, 0:L], False, True)], ["OB", "Iw", "eb"] + lanes("R", 0, L), ["PS2"])
            if not last:
                p([mm(PS[5][:, 0:L], Ib, T.x15[:, 0:L], True, False), mm(PS[5][:, 0:L], Ib, T.R[:, 15:16 * L:16], False, True)], ["Iw", "x15"] + lanes("R", 0, L), ["PS5"])

        def not_lost():
            v(lambda: V.tensor_scalar(T.nl[:, 0:C, 0:16], PS[2][:, 0:L], 32767.5, 16384.0, A_.is_ge, A_.mult), ["PS2"], ["nl"])

        def rest():
            v(lambda: V.tensor_scalar(T.R16[:, 0:L], PS[5][:, 0:L], 2048.0, None, A_.min), ["PS5"], ["R16"])
            p(mm(PS[5][:, 0:L], OB, T.R16[:, 0:L], True, True), ["OB", "R16"], ["PS5"])

        def unmet():
            v(lambda: V.tensor_scalar(T.uf[:, 0:L], PS[5][:, 0:L], 32767.5, None, A_.is_lt), ["PS5"], ["uf"])

        def slots():
            v(lambda: V.tensor_tensor_scan(T.cum[:, 0:L], T.uf[:, 0:L], T.uf[:, 0:L], 0.0, A_.add, A_.max), ["uf"], ["cum"])
            p([mm(PS[5][:, 0:L], T.J[:, :], T.O2[:, 0:L], True, False), mm(PS[5][:, 0:L], T.In8[:, :], T.uf[:, 0:L], False, False),
               mm(PS[5][:, 0:L], Ib, T.cum[:, 0:L], False, True)], ["Iw", "J", "In8", "O2", "uf", "cum"], ["PS5"])

        def slot_list(mid):
            v(lambda: V.tensor_tensor_scan(T.uy[:, 0:L], T.DU[:, 0:L], PS[5][:, 0:L], 0.0, A_.max, A_.min), ["DU", "PS5"], ["uy"])
            mid()
            v(lambda: V.tensor_scalar(T.ul[:, 0:C], T.uy[:, 15:L:16], -1.0, None, A_.add), ["uy"], ["ul"])

        def hand_on():
            sw = T["SW%d" % t]
            v(lambda: V.tensor_copy(sw[:, :].indirect(T.ul[:, 0:C]), T.R16[:, 0:L]), ["ul", "R16"], ["SW%d" % t])

        def send():
            sw = T["SW%d" % t]
            before("G", ["SW%d" % t], [])
            rid, pid, _se = topo.addr(nxt)
            em = sum(1 << e for e in topo.engines(core, nxt)[:NE])
            g.remote_dma(T["RC%d" % t][:, :], sw[:, 0:64], T.sem["arr%d" % t], T.sem.snt, pid, rid, em)

        def numbers(r):
            n = 12 if r else 8
            v(lambda: V.tensor_copy(T.nv[:, 0:16 * n], T.NUM[:, 0:NRD].indirect(T.LG[:, 12 * r:12 * r + n])), NUMW + ["LG"], ["nv"])

        def moved(r):
            n = 12 if r else 8
            v(lambda: V.tensor_copy(T.NUM[:, :].indirect(T.LL[:, 24 * r:24 * r + n]), T.nv[:, 0:16 * n]), ["LLa", "nv"], NUMW)

        vgather(0, ch[1])
        if t == 0:
            vm, vl = VLANES
            sgather(ch[1], ch[2])
            sgather(vl, L)
            lasts(0)
            last_stations()
            own_needs(0)
            scan(0)
            vgather(ch[2], vm)
            scan(1)
            empty(0, None, lambda: vgather(vm, vl))
            empty(1, lambda: firsts(0))
            scan(2)
            was_empty()
            sums()
            cards16(192, 576, "1")
            shift(1)
            dma("Y", T.N[:, 2048:3072], T.N[:, 0:1024], lanes("N", 0, 64), lanes("N", 128, 192))
            empty(2, lambda: needs_copy(0, True))
            needs_copy(1, True)
            rest()
            not_lost()
            needs_copy(2, True)
            unmet()
            slots()
            ends(1)
            covers(0)
            slot_list(lambda: turn(0))
            hand_on()
            cover_lists(0)
            firsts(1)
            lasts(1)
        else:
            sgather(ch[1], ch[2])
            sgather(ch[2], SLANES)
            if not last:
                last_stations()
            scan(0)
            covers(t)
            scan(1)
            empty(0, lambda: turn(t))
            first_dumps()
            vgather(SLANES + 8, ch[3])
            empty(1, None, lambda: vgather(SLANES, SLANES + 8))
            scan(2)
            vgather(ch[3], VG)
            empty(2, lambda: cover_lists(t), lambda: vgather(VG, L))
            v(lambda: V.tensor_copy(T.N[:, 2048:3072:16], T["RC%d" % (t - 1)][:, :]), ["RC%d" % (t - 1)], lanes("N", 128, 192))
            scan(3)
            for k in range(len(BR)):
                needs_copy(k, False)
            if not last:
                count_up(T.NUM[:, 0:NRD // 2], "NUM", [[0, NRD // 2]], 2047, 0)
            was_empty()
            if last:
                numbers(0)
                sums()
                empty(3, lambda: moved(0))
                not_lost()
                numbers(1)
                moved(1)
                dma("Y", T.NL[:, :], T.NUM[0:128:16, 0:NST], NUMW, ["NL"])
                dma("Y", T.EL[:, :], T.SK[0:128:16, 0:NST], SKW, ["EL"])
            else:
                sums()
                shift(2)
                empty(3)
                rest()
                not_lost()
                unmet()
                slots()
                slot_list(lambda: None)
                hand_on()
        DB = [0, 1, 3]
        p([mm(PS[4][:, 0:L], T.J[:, :], T.TH[:, 0:L], True, False), mm(PS[4][:, 0:L], T.In[:, :], T.nl[:, 0:C, 0:16], False, False)], ["J", "TH", "In", "nl"], ["PS4"])
        for k in range(3):
            p(mm(PS[DB[k]][:, 0:2 * L], T.In[:, :], T.Br[:, 0:2 * L], True, False), ["In"] + BR, ["PS%d" % DB[k]])
        p(mm(PS[2][:, 0:H], Ib, T.mf[:, H:L], True, False), ["Iw", "mf"], ["PS2"])
        p([mm(PS[7][:, 0:M], T.J[:, :], T.T1[:, 0:M], True, False), mm(PS[7][:, 0:M], Ib, T.nl[:, 0:C, :], False, False)], ["Iw", "J", "T1", "nl", "pad"], ["PS7"])
        p(mm(PS[5][:, 0:H], Ib, T.mf[:, 0:H], True, False), ["Iw", "mf"], ["PS5"])
        done = []

        def count(cs):
            for i in cs:
                done.append(i)
                p(mm(PS[4][:, 0:L], T.Wb[:, 16 - i:144 - i], T.ge[:, L * i:L * i + L], False, len(done) == 16), ["Wb", "ge%d" % i], ["PS4"] if len(done) == 16 else [])

        def vcall(k):
            a = sum(VCALLS[:k])
            b = a + VCALLS[k]
            v(lambda: V.tensor_tensor(T.ge[:, L * a:L * b], win.indirect(T.mu[:, C * a:C * b]), T.Br[:, 0:L * (b - a)], A_.is_ge),
              SKW + ["mu"] + BR, ["ge%d" % i for i in range(a, b)])
            return range(a, b)

        def scall(a, b):
            s(lambda: S.activation(T.AG[:, L * a:L * b], win.indirect(T.mu[:, C * (KV + a):C * (KV + b)]), F_.Copy), SKW + ["mu"], ["AG%d" % j for j in range(a, b)])

        def sdiff(k):
            p(mm(PS[DB[k]][:, 0:2 * L], Ib, T.AG[:, 2 * L * k:2 * L * k + 2 * L], False, True), ["Iw", "AG%d" % (2 * k), "AG%d" % (2 * k + 1)], ["PS%d" % DB[k]])

        def ssign(k):
            i = KV + 2 * k
            s(lambda: S.activation(T.ge[:, L * i:L * i + 2 * L], PS[DB[k]][:, 0:2 * L], F_.Sign, bias=EPS / 2), ["PS%d" % DB[k]], ["ge%d" % i, "ge%d" % (i + 1)])
            return [i, i + 1]

        if not last:
            dma("Y", T.SKC[:, 0:CP[t][0]], T.SK[:, 0:CP[t][0]], SKW, ["SCa"])
            a, b = CP[t][0], CP[t][1]
            if t == 0:
                first_dumps()
            gp(lambda: g.affine_select(T.SKC[:, a:b], T.SK[:, a:b], [[0, b - a]], A_.is_equal, 0.0, 0, 0), SKW, ["SCd"])
            send()
        if t == 0:
            for h in range(2):
                gp(lambda: g.affine_select(T.occf[:, h, :], T.r16[:, :, 16 * h:16 * h + 16], [[0, 128]], A_.is_equal, 0.0, 0, 0), ["r16%d" % h], ["occf"])
        if t == 1:
            count_up(T.nv[:, 192:384], "nvz", [[0, 192]], 2047, 0)
            count_up(T.NUM[:, NRD // 2:NRD], "NUM", [[0, NRD // 2]], 2047, 0)
            dma("Y", T.NUM[0:128:32, 0:NST], T.occf[:, 0, :], ["occf", "NUM"], ["NUM0"])
            dma("Y", T.NUM[16:128:32, 0:NST], T.occf[:, 1, :], ["occf", "NUM"], ["NUM1"])
        scall(0, 4)
        scall(4, 6)
        vc = [vcall(k) for k in range(4)]
        if last:
            v(lambda: V.tensor_scalar(PS[6][:, 128:384], T.EL[:, :], EPS / 2, 2047.0, A_.is_lt, A_.mult), ["EL"], ["PS6"])
            v(lambda: V.tensor_tensor(T.YL[:, :], PS[6][:, 128:384], T.NL[:, :], A_.max), ["NL", "PS6"], ["YL"])
            dma("Y", T.SKC[0:128:16, 0:NST], T.YL[:, :], ["YL"], SCW)
        else:
            shifted(t + 1)
            own_needs(t + 1)
        sdiff(0)
        sdiff(1)
        count(vc[0])
        sdiff(2)
        sc = [ssign(k) for k in range(3)]
        for cs in (vc[1], sc[0], sc[1], vc[2], sc[2], vc[3]):
            count(cs)
        if not last:
            s(lambda: S.activation(T.SKC[:, CP[t][1]:CP[t][2]], T.SK[:, CP[t][1]:CP[t][2]], F_.Copy), SKW, ["SCb"])
        for k in (6, 3):
            p(mm(PS[k][:, 0:M // 2], T.J[:, :], T.T1[:, 0:M // 2], True, False), ["J", "T1"], ["PS%d" % k])
        halves = ((0, 5, 6, 0), (H, 2, 3, 1))
        for a, z, _k, _r in halves:
            v(lambda: V.tensor_scalar(T.Fb[:, a:a + H], PS[4][:, a:a + H], 0.5, None, A_.is_ge), ["PS4"], ["Fb%d" % a])
            p(mm(PS[z][:, 0:H], T.Mn[:, :], T.Fb[:, a:a + H], False, True), ["Mn", "Fb%d" % a], ["PS%d" % z])
        for a, z, k, r in halves:
            c, m = a // 16, 17 * a // 16
            v(lambda: V.tensor_scalar(T.selm[:, c:c + D, 0:16], PS[z][:, 0:H], 16384.0, 2048.0, A_.add, A_.min), ["PS%d" % z], ["selm%d" % a])
            p(mm(PS[r][:, 0:M // 2], OB, T.selm[:, c:c + D, :], True, True), ["OB", "pad", "selm%d" % a], ["PS%d" % r])
            p(mm(PS[k][:, 0:M // 2], OB, T.selm[:, c:c + D, :], False, True), ["OB", "selm%d" % a], ["PS%d" % k])
            s(lambda: S.activation(T.Rh[:, m:m + M // 2], PS[r][:, 0:M // 2], F_.Copy, bias=-30720.0), ["PS%d" % r], ["Rh%d" % a])
        p(mm(PS[7][:, 0:M], OB, T.selm[:, 0:C, :], False, False), ["OB", "selm0", "selm%d" % H], ["PS7"])
        for a, z, k, r in halves:
            m = 17 * a // 16
            v(lambda: V.tensor_tensor_scan(T.v1[:, m:m + M // 2], T.DT[:, m:m + M // 2], PS[k][:, 0:M // 2], 0.0, A_.max, A_.min), ["DT", "PS%d" % k], ["v1%d" % a])
        if not last:
            s(lambda: S.activation(T.SKC[:, CP[t][2]:NRD], T.SK[:, CP[t][2]:NRD], F_.Copy), SKW, ["SCc"])
        for c in range(C):
            v(lambda: V.tensor_scalar(T.E2[:, c, 0:M - 17 * c], T.Rh[:, 17 * c:M], -2048.0, T.v1[:, 17 * c + 15:17 * c + 16], A_.add, A_.is_equal),
              ["Rh0", "Rh%d" % H, "v10" if c < D else "v1%d" % H], ["E%d" % c])
            p(([mm(PS[7][:, 17 * c + 17:M], T.OB16[:, :], T.E2[:, c, 17:M - 17 * c], False, False)] if c < C - 1 else [])
              + [mm(PS[7][:, 17 * c:17 * c + 16], T.T16[:, :], T.E2[:, c, 0:16], False, c == C - 1)], ["OB16", "T16", "E%d" % c], ["PS7"] if c == C - 1 else [])
        v(lambda: V.tensor_scalar(LG, T.v1[:, 15:M:17], float(NST), None, A_.add), ["v10", "v1%d" % H], ["LG"])
        if not last:
            s(lambda: S.activation(T.sv[:, 0:L], win.indirect(LG), F_.Copy), SKW + ["LG"], ["sv"])
        else:
            s(lambda: S.activation(T.nv[:, 0:192], T.NUM[:, 0:NRD].indirect(LG), F_.Copy), NUMW + ["LG"], ["nv"])
        v(lambda: V.tensor_tensor_scan(T.v2[:, 0:M], T.DT[:, 0:M], PS[7][:, 0:M], 0.0, A_.max, A_.min), ["DT", "PS7"], ["v2"])
        v(lambda: V.tensor_scalar(LB, T.v2[:, 15:M:17], float(NST), None, A_.add), ["v2"], ["LLb"])
        v(lambda: V.tensor_copy(LA, T.v2[:, 16:M:17]), ["v2"], ["LLa"])
        if not last:
            for zw, zk, vw, vk in ((T.SKC, SCW, T.SK, SKW), (T.SK, SKW, T.SKC, SCW)):
                s(lambda: S.activation(zw[:, :].indirect(LB), T.ZS[:, 0:L], F_.Sigmoid), ["LLb", "ZS"], zk)
                v(lambda: V.tensor_copy(vw[:, :].indirect(LA), T.sv[:, 0:L]), ["LLa", "sv"], vk)
    v(lambda: V.tensor_copy(T.SKC[:, :].indirect(T.LL[:, 48:72]), T.nv[:, :]), ["LLa", "LLb", "nv", "nvz"], SCW)
    dma("Y", T.y[:, :], T.SKC[0:128:16, 0:NST], SCW, ["y"])
    g.wait_ge(T.sem.snt, 2 * NE)
    finish()
